import numpy as np
import ml_dtypes


def mxq(x, axis, fmt="e4m3"):
    dtype, down = {"e4m3": (ml_dtypes.float8_e4m3fn, 7), "e5m2": (ml_dtypes.float8_e5m2, 14)}[fmt]
    v = np.moveaxis(np.asarray(x, np.float32).astype(ml_dtypes.bfloat16).astype(np.float64), axis, -1)
    blocks = v.reshape(v.shape[:-1] + (-1, 32))
    amax = np.abs(blocks).max(-1, keepdims=True)
    byte = np.maximum(np.where(amax > 0, np.frexp(amax)[1] - 1 + 127, 0) - down, 1)
    scale = np.exp2(byte - 127.0)
    codes = (blocks / scale).astype(np.float32).astype(dtype).astype(np.float64)
    return np.moveaxis((codes * scale).reshape(v.shape), -1, axis)


WIDE = False


def mx_kscale(k):
    if not WIDE:
        return np.ones(k)
    levels = np.array([18, -18])
    if k % 512:
        return np.exp2(np.random.permutation(np.resize(levels, k // 32))).repeat(32)
    a = np.empty((k // 512, 16))
    for p in range(k // 512):
        a[p, :8] = np.random.permutation(np.resize(levels, 8))
        for g in range(8):
            far = levels[np.abs(levels - a[p, g]) >= 10]
            a[p, g + 8] = far[np.random.randint(len(far))]
    return np.exp2(a.ravel()).repeat(32)


def f64(x):
    return np.asarray(x).astype(np.float64)


def striped(idx):
    return np.tile(np.asarray(idx).reshape(-1, 16).T, (8, 1)).astype(np.uint16)


def unstriped(offs):
    return offs[:16].T.reshape(-1).astype(np.int64)


B, N, T, D, DV, R = 1, 512, 2048, 512, 512, 1024


def setup_inputs():
    n = np.random.standard_normal
    idx = np.random.permutation(T)[:B * N]
    s = mx_kscale(D)[:, None]
    z = mx_kscale(R)[:, None]
    q = n((B, D, R))
    do = n((B, DV, R))
    return {
        "qT": (q * s).astype(np.float32),
        "kT": (n((D, T)) * (1.00 / np.sqrt(D)) / s).astype(np.float32),
        "rw": (np.random.uniform(0.5, 1.5, (B, R, 1)) * 1.0 / np.sqrt(R) * z).astype(np.float32),
        "dom": (do.transpose(0, 2, 1) / z).astype(np.float32),
        "offs": striped(idx),
    }


def reference(qT, kT, rw, dom, offs):
    idx = unstriped(offs)
    pick = lambda x: x[:, idx].reshape(x.shape[0], B, N).transpose(1, 0, 2)
    a = mxq(f64(qT), 1, "e4m3").transpose(0, 2, 1) @ mxq(pick(f64(kT)), 1, "e4m3")
    p = np.square(np.maximum(a, 0.0))
    dv = mxq(f64(dom), 1, "e5m2").transpose(0, 2, 1) @ mxq(f64(rw) * p, 1, "e4m3")
    gv = np.zeros((DV, T))
    gv[:, idx] = dv.transpose(1, 0, 2).reshape(DV, B * N)
    return gv

@@ -1,0 +1,226 @@
+from contextlib import ExitStack
+
+import concourse.mybir as mybir
+
+N, T, D, DV, R = 512, 2048, 512, 512, 1024
+FLOPS = 2 * R * N * D + 2 * R * N * DV
+
+F32 = mybir.dt.float32
+BF16 = mybir.dt.bfloat16
+U32 = mybir.dt.uint32
+U16 = mybir.dt.uint16
+U8 = mybir.dt.uint8
+E4 = mybir.dt.float8_e4m3fn_x4
+E5 = mybir.dt.float8_e5m2_x4
+COPY = mybir.ActivationFunctionType.Copy
+MULT = mybir.AluOpType.mult
+ADD = mybir.AluOpType.add
+MAX = mybir.AluOpType.max
+
+P = 128
+PACK = 4
+PASS = P * PACK
+G = R // PASS
+E_TILES = DV // P
+CH = 128
+Q_PIECE = 256
+WINDOWS = 3
+
+
+def tile_attend_gat_v_kernel(tc, qT, kT, rw, dom, offs, out):
+    nc = tc.nc
+
+    def cast(engine, dst, src):
+        if engine == "S":
+            nc.scalar.activation(out=dst, in_=src, func=COPY)
+        elif engine == "V":
+            nc.vector.tensor_copy(out=dst, in_=src)
+        else:
+            nc.gpsimd.tensor_scalar(out=dst, in0=src, scalar1=1.0, scalar2=0.0, op0=MULT, op1=ADD)
+
+    with ExitStack() as ctx:
+        keep = ctx.enter_context(tc.tile_pool(name="keep", bufs=1))
+        ring = ctx.enter_context(tc.tile_pool(name="ring", bufs=4))
+        spsum = ctx.enter_context(tc.psum_pool(name="spsum", bufs=6))
+        opsum = ctx.enter_context(tc.psum_pool(name="opsum", bufs=2))
+
+        offsets = keep.tile([P, N // 16], U16, name="offsets")
+        k_planes = [keep.tile([P, T], F32, name="k_plane%d" % j) for j in range(PACK)]
+        k_rows = kT.rearrange("(p j) c -> p j c", j=PACK)
+        q_rows = qT[0].rearrange("(p j) r -> p j r", j=PACK)
+        q_raw = [keep.tile([P, PACK, Q_PIECE], F32, name="q_raw%d" % i) for i in range(R // Q_PIECE)]
+        gate = keep.tile([P, G, PACK], F32, name="gate")
+        d_rows = dom[0].rearrange("(g p j) e -> g p j e", p=P, j=PACK)
+        d_first = [keep.tile([P, PACK, P], F32, name="d_first%d" % g) for g in range(G)]
+        d_rest = [keep.tile([P, PACK, DV - P], F32, name="d_rest%d" % g) for g in range(G)]
+        windows = [keep.tile([P, T], F32, name="window%d" % e) for e in range(WINDOWS)]
+
+        def load_q(i):
+            nc.sync.dma_start(out=q_raw[i][:], in_=q_rows[:, :, i * Q_PIECE : (i + 1) * Q_PIECE])
+
+        nc.sync.dma_start(out=k_planes[0][:], in_=k_rows[:, 0, :])
+        nc.sync.dma_start(offsets[:], offs)
+        for j in range(1, PACK):
+            nc.sync.dma_start(out=k_planes[j][:], in_=k_rows[:, j, :])
+        load_q(0)
+        load_q(1)
+        nc.sync.dma_start(out=gate[:], in_=rw[0].rearrange("(g p t) o -> p g (t o)", p=P, t=PACK))
+        load_q(2)
+        load_q(3)
+        for g in range(G):
+            nc.sync.dma_start(out=d_first[g][:], in_=d_rows[g, :, :, 0:P])
+        for g in range(G):
+            nc.sync.dma_start(out=d_rest[g][:], in_=d_rows[g, :, :, P:DV])
+
+        for window in windows:
+            nc.vector.memset(window[:], 0.0)
+
+        k_bf = keep.tile([P, N, PACK], BF16, name="k_bf", align_bytes=64)
+        k_codes = keep.tile([P, N], U32, name="k_codes", align_bytes=64)
+        k_scales = keep.tile([P, N], U8, name="k_scales", align_bytes=64)
+        q_bf = [keep.tile([P, PACK, P, PACK], BF16, name="q_bf%d" % g, align_bytes=64) for g in range(G)]
+        q_codes = [keep.tile([P, PASS], U32, name="q_codes%d" % g, align_bytes=64) for g in range(G)]
+        q_scales = [keep.tile([P, PASS], U8, name="q_scales%d" % g, align_bytes=64) for g in range(G)]
+        w_bf = [keep.tile([P, N, PACK], BF16, name="w_bf%d" % g, align_bytes=64) for g in range(G)]
+        w_codes = [keep.tile([P, N], U32, name="w_codes%d" % g, align_bytes=64) for g in range(G)]
+        w_scales = [keep.tile([P, N], U8, name="w_scales%d" % g, align_bytes=64) for g in range(G)]
+        d_bf = [keep.tile([P, G, P, PACK], BF16, name="d_bf%d" % e, align_bytes=64) for e in range(E_TILES)]
+        d_codes = [keep.tile([P, G, P], U32, name="d_codes%d" % e, align_bytes=64) for e in range(E_TILES)]
+        d_scales = [keep.tile([P, G, P], U8, name="d_scales%d" % e, align_bytes=64) for e in range(E_TILES)]
+
+        def gather(j, lo, hi):
+            nc.vector.tensor_copy(
+                out=k_bf[:, lo:hi, j], in_=k_planes[j][:].indirect(offsets[:, lo // 16 : hi // 16])
+            )
+
+        def quant_k(lo, hi):
+            nc.vector.quantize_mx(
+                out=k_codes[:, lo:hi].bitcast(E4),
+                scales=k_scales[:, lo:hi],
+                in_=k_bf[:, lo:hi, :].rearrange("p n j -> p (n j)"),
+            )
+
+        def cast_q(i, engine, parts):
+            g, h = divmod(i, PASS // Q_PIECE)
+            width = Q_PIECE // PACK // parts
+            for s in range(parts):
+                m0 = h * (Q_PIECE // PACK) + s * width
+                src = q_raw[i][:].rearrange("p j (m t) -> p m t j", t=PACK)[:, s * width : (s + 1) * width]
+                dst = q_bf[g][:].rearrange("p t m j -> p m t j")[:, m0 : m0 + width]
+                cast(engine, dst, src)
+
+        def quant_q(g):
+            nc.vector.quantize_mx(
+                out=q_codes[g][:].bitcast(E4),
+                scales=q_scales[g][:],
+                in_=q_bf[g][:].rearrange("p t m j -> p (t m j)"),
+            )
+
+        def cast_d(e, g, engine):
+            if e == 0:
+                src = d_first[g][:]
+            else:
+                src = d_rest[g][:, :, (e - 1) * P : e * P]
+            cast(engine, d_bf[e][:, g], src.rearrange("p j e -> p e j"))
+
+        def quant_d(e):
+            nc.vector.quantize_mx(
+                out=d_codes[e][:].rearrange("p g e -> p (g e)").bitcast(E5),
+                scales=d_scales[e][:].rearrange("p g e -> p (g e)"),
+                in_=d_bf[e][:].rearrange("p g e j -> p (g e j)"),
+            )
+
+        def weights(g, c):
+            cols = slice(c * CH, (c + 1) * CH)
+            bank = spsum.tile([P, PACK, CH], F32, name="scores")
+            for t in range(PACK):
+                nc.tensor.matmul_mx(
+                    out=bank[:, t, :],
+                    lhsT=q_codes[g][:, t * P : (t + 1) * P].bitcast(E4),
+                    lhsT_scale=q_scales[g][:, t * P : (t + 1) * P],
+                    rhs=k_codes[:, cols].bitcast(E4),
+                    rhs_scale=k_scales[:, cols],
+                    start=True,
+                    stop=True,
+                )
+            gated = ring.tile([P, PACK, CH], F32, name="gated")
+            for t in range(PACK):
+                nc.scalar.activation(out=gated[:, t, :], in_=bank[:, t, :], func=COPY, scale=gate[:, g, t : t + 1])
+            nc.vector.scalar_tensor_tensor(
+                out=w_bf[g][:, cols, :],
+                in0=bank[:].rearrange("p t n -> p n t"),
+                scalar=0.0,
+                in1=gated[:].rearrange("p t n -> p n t"),
+                op0=MAX,
+                op1=MULT,
+            )
+
+        def quant_w(g, lo, hi):
+            nc.vector.quantize_mx(
+                out=w_codes[g][:, lo:hi].bitcast(E4),
+                scales=w_scales[g][:, lo:hi],
+                in_=w_bf[g][:, lo:hi, :].rearrange("p n t -> p (n t)"),
+            )
+
+        def product(e, parts):
+            acc = opsum.tile([P, N], F32, name="acc")
+            for g in range(G):
+                nc.tensor.matmul_mx(
+                    out=acc[:],
+                    lhsT=d_codes[e][:, g, :].bitcast(E5),
+                    lhsT_scale=d_scales[e][:, g, :],
+                    rhs=w_codes[g][:].bitcast(E4),
+                    rhs_scale=w_scales[g][:],
+                    start=(g == 0),
+                    stop=(g == G - 1),
+                )
+            dense = ring.tile([P, N], F32, name="dense")
+            width = N // parts
+            for s in range(parts):
+                cols = slice(s * width, (s + 1) * width)
+                nc.scalar.activation(out=dense[:, cols], in_=acc[:, cols], func=COPY)
+            return dense
+
+        def place(e, dense, parts):
+            window = windows[e % WINDOWS]
+            width = N // parts
+            for s in range(parts):
+                lo, hi = s * width, (s + 1) * width
+                nc.vector.tensor_copy(out=window[:].indirect(offsets[:, lo // 16 : hi // 16]), in_=dense[:, lo:hi])
+            nc.sync.dma_start(out=out[e * P : (e + 1) * P, :], in_=window[:])
+
+        for j in range(PACK - 1):
+            gather(j, 0, N)
+        gather(PACK - 1, 0, N // 2)
+        gather(PACK - 1, N // 2, N)
+        quant_k(0, N // 2)
+        quant_k(N // 2, N)
+        cast_q(0, "S", 1)
+        cast_q(1, "V", 1)
+        quant_q(0)
+        cast_q(2, "G", 2)
+        cast_q(3, "G", 2)
+        weights(0, 0)
+        weights(0, 1)
+        quant_q(1)
+        weights(0, 2)
+        weights(0, 3)
+        for e in range(E_TILES):
+            for g in range(G):
+                cast_d(e, g, "G")
+        weights(1, 0)
+        quant_w(0, 0, N)
+        weights(1, 1)
+        quant_d(0)
+        weights(1, 2)
+        quant_w(1, 0, N // 2)
+        weights(1, 3)
+        quant_w(1, N // 2, 3 * N // 4)
+        quant_w(1, 3 * N // 4, N)
+        dense = product(0, 2)
+        for e in range(1, E_TILES):
+            quant_d(e)
+        place(0, dense, 2)
+        for e in range(1, E_TILES):
+            dense = product(e, 1)
+            place(e, dense, 1)

@@ -41,6 +41,7 @@ def tile_attend_gat_v_kernel(tc, qT, kT, rw, dom, offs, out):
     with ExitStack() as ctx:
         keep = ctx.enter_context(tc.tile_pool(name="keep", bufs=1))
         ring = ctx.enter_context(tc.tile_pool(name="ring", bufs=4))
+        stage = ctx.enter_context(tc.tile_pool(name="stage", bufs=3))
         spsum = ctx.enter_context(tc.psum_pool(name="spsum", bufs=6))
         opsum = ctx.enter_context(tc.psum_pool(name="opsum", bufs=2))
 
@@ -72,8 +73,9 @@ def tile_attend_gat_v_kernel(tc, qT, kT, rw, dom, offs, out):
         for g in range(G):
             nc.sync.dma_start(out=d_rest[g][:], in_=d_rows[g, :, :, P:DV])
 
-        for window in windows:
+        for window in windows[:-1]:
             nc.vector.memset(window[:], 0.0)
+        nc.gpsimd.memset(windows[-1][:], 0.0)
 
         k_bf = keep.tile([P, N, PACK], BF16, name="k_bf", align_bytes=64)
         k_codes = keep.tile([P, N], U32, name="k_codes", align_bytes=64)
@@ -84,7 +86,7 @@ def tile_attend_gat_v_kernel(tc, qT, kT, rw, dom, offs, out):
         w_bf = [keep.tile([P, N, PACK], BF16, name="w_bf%d" % g, align_bytes=64) for g in range(G)]
         w_codes = [keep.tile([P, N], U32, name="w_codes%d" % g, align_bytes=64) for g in range(G)]
         w_scales = [keep.tile([P, N], U8, name="w_scales%d" % g, align_bytes=64) for g in range(G)]
-        d_bf = [keep.tile([P, G, P, PACK], BF16, name="d_bf%d" % e, align_bytes=64) for e in range(E_TILES)]
+        d_bf = {0: keep.tile([P, G, P, PACK], BF16, name="d_bf0", align_bytes=64)}
         d_codes = [keep.tile([P, G, P], U32, name="d_codes%d" % e, align_bytes=64) for e in range(E_TILES)]
         d_scales = [keep.tile([P, G, P], U8, name="d_scales%d" % e, align_bytes=64) for e in range(E_TILES)]
 
@@ -100,13 +102,14 @@ def tile_attend_gat_v_kernel(tc, qT, kT, rw, dom, offs, out):
                 in_=k_bf[:, lo:hi, :].rearrange("p n j -> p (n j)"),
             )
 
-        def cast_q(i, engine, parts):
+        def cast_q(i, engines):
             g, h = divmod(i, PASS // Q_PIECE)
-            width = Q_PIECE // PACK // parts
-            for s in range(parts):
-                m0 = h * (Q_PIECE // PACK) + s * width
-                src = q_raw[i][:].rearrange("p j (m t) -> p m t j", t=PACK)[:, s * width : (s + 1) * width]
-                dst = q_bf[g][:].rearrange("p t m j -> p m t j")[:, m0 : m0 + width]
+            width = PACK // len(engines)
+            ms = slice(h * (Q_PIECE // PACK), (h + 1) * (Q_PIECE // PACK))
+            for s, engine in enumerate(engines):
+                ts = slice(s * width, (s + 1) * width)
+                src = q_raw[i][:].rearrange("p j (m t) -> p m t j", t=PACK)[:, :, ts]
+                dst = q_bf[g][:].rearrange("p t m j -> p m t j")[:, ms, ts]
                 cast(engine, dst, src)
 
         def quant_q(g):
@@ -117,6 +120,8 @@ def tile_attend_gat_v_kernel(tc, qT, kT, rw, dom, offs, out):
             )
 
         def cast_d(e, g, engine):
+            if e not in d_bf:
+                d_bf.setdefault(e, stage.tile([P, G, P, PACK], BF16, name="d_late", tag="stage", align_bytes=64))
             if e == 0:
                 src = d_first[g][:]
             else:
@@ -143,7 +148,7 @@ def tile_attend_gat_v_kernel(tc, qT, kT, rw, dom, offs, out):
                     start=True,
                     stop=True,
                 )
-            gated = ring.tile([P, PACK, CH], F32, name="gated")
+            gated = stage.tile([P, PACK, CH], F32, name="gated", tag="stage", align_bytes=64)
             for t in range(PACK):
                 nc.scalar.activation(out=gated[:, t, :], in_=bank[:, t, :], func=COPY, scale=gate[:, g, t : t + 1])
             nc.vector.scalar_tensor_tensor(
@@ -195,20 +200,19 @@ def tile_attend_gat_v_kernel(tc, qT, kT, rw, dom, offs, out):
         gather(PACK - 1, N // 2, N)
         quant_k(0, N // 2)
         quant_k(N // 2, N)
-        cast_q(0, "S", 1)
-        cast_q(1, "V", 1)
+        cast_q(0, "S")
+        cast_q(1, "V")
         quant_q(0)
-        cast_q(2, "G", 2)
-        cast_q(3, "G", 2)
+        cast_q(2, "V")
         weights(0, 0)
         weights(0, 1)
+        cast_q(3, "VS")
         quant_q(1)
         weights(0, 2)
         weights(0, 3)
-        for e in range(E_TILES):
-            for g in range(G):
-                cast_d(e, g, "G")
         weights(1, 0)
+        cast_d(0, 0, "V")
+        cast_d(0, 1, "S")
         quant_w(0, 0, N)
         weights(1, 1)
         quant_d(0)
@@ -218,9 +222,14 @@ def tile_attend_gat_v_kernel(tc, qT, kT, rw, dom, offs, out):
         quant_w(1, N // 2, 3 * N // 4)
         quant_w(1, 3 * N // 4, N)
         dense = product(0, 2)
-        for e in range(1, E_TILES):
-            quant_d(e)
+        for g in range(G):
+            cast_d(1, g, "S")
+        quant_d(1)
         place(0, dense, 2)
         for e in range(1, E_TILES):
             dense = product(e, 1)
+            if e + 1 < E_TILES:
+                for g in range(G):
+                    cast_d(e + 1, g, "S")
+                quant_d(e + 1)
             place(e, dense, 1)

@@ -23,8 +23,9 @@ PASS = P * PACK
 G = R // PASS
 E_TILES = DV // P
 CH = 128
-Q_PIECE = 256
-WINDOWS = 3
+HALF = N // 2
+Q_CUT = 768
+WINDOWS = 4
 
 
 def tile_attend_gat_v_kernel(tc, qT, kT, rw, dom, offs, out):
@@ -40,8 +41,9 @@ def tile_attend_gat_v_kernel(tc, qT, kT, rw, dom, offs, out):
 
     with ExitStack() as ctx:
         keep = ctx.enter_context(tc.tile_pool(name="keep", bufs=1))
-        ring = ctx.enter_context(tc.tile_pool(name="ring", bufs=4))
+        late = ctx.enter_context(tc.tile_pool(name="late", bufs=1))
         stage = ctx.enter_context(tc.tile_pool(name="stage", bufs=3))
+        final = ctx.enter_context(tc.tile_pool(name="final", bufs=1))
         spsum = ctx.enter_context(tc.psum_pool(name="spsum", bufs=6))
         opsum = ctx.enter_context(tc.psum_pool(name="opsum", bufs=2))
 
@@ -49,33 +51,30 @@ def tile_attend_gat_v_kernel(tc, qT, kT, rw, dom, offs, out):
         k_planes = [keep.tile([P, T], F32, name="k_plane%d" % j) for j in range(PACK)]
         k_rows = kT.rearrange("(p j) c -> p j c", j=PACK)
         q_rows = qT[0].rearrange("(p j) r -> p j r", j=PACK)
-        q_raw = [keep.tile([P, PACK, Q_PIECE], F32, name="q_raw%d" % i) for i in range(R // Q_PIECE)]
+        q_head = keep.tile([P, PACK, Q_CUT], F32, name="q_head")
+        q_tail = keep.tile([P, PACK, R - Q_CUT], F32, name="q_tail")
+
         gate = keep.tile([P, G, PACK], F32, name="gate")
         d_rows = dom[0].rearrange("(g p j) e -> g p j e", p=P, j=PACK)
         d_first = [keep.tile([P, PACK, P], F32, name="d_first%d" % g) for g in range(G)]
         d_rest = [keep.tile([P, PACK, DV - P], F32, name="d_rest%d" % g) for g in range(G)]
         windows = [keep.tile([P, T], F32, name="window%d" % e) for e in range(WINDOWS)]
 
-        def load_q(i):
-            nc.sync.dma_start(out=q_raw[i][:], in_=q_rows[:, :, i * Q_PIECE : (i + 1) * Q_PIECE])
-
-        nc.sync.dma_start(out=k_planes[0][:], in_=k_rows[:, 0, :])
+        nc.sync.dma_start(out=q_head[:], in_=q_rows[:, :, :Q_CUT])
         nc.sync.dma_start(offsets[:], offs)
-        for j in range(1, PACK):
-            nc.sync.dma_start(out=k_planes[j][:], in_=k_rows[:, j, :])
-        load_q(0)
-        load_q(1)
         nc.sync.dma_start(out=gate[:], in_=rw[0].rearrange("(g p t) o -> p g (t o)", p=P, t=PACK))
-        load_q(2)
-        load_q(3)
+        for j in range(PACK):
+            nc.sync.dma_start(out=k_planes[j][:], in_=k_rows[:, j, :])
+        nc.sync.dma_start(out=q_tail[:], in_=q_rows[:, :, Q_CUT:])
         for g in range(G):
             nc.sync.dma_start(out=d_first[g][:], in_=d_rows[g, :, :, 0:P])
         for g in range(G):
             nc.sync.dma_start(out=d_rest[g][:], in_=d_rows[g, :, :, P:DV])
 
-        for window in windows[:-1]:
+        for window in windows[:2]:
             nc.vector.memset(window[:], 0.0)
-        nc.gpsimd.memset(windows[-1][:], 0.0)
+        for window in windows[2:]:
+            nc.gpsimd.memset(window[:], 0.0)
 
         k_bf = keep.tile([P, N, PACK], BF16, name="k_bf", align_bytes=64)
         k_codes = keep.tile([P, N], U32, name="k_codes", align_bytes=64)
@@ -84,11 +83,15 @@ def tile_attend_gat_v_kernel(tc, qT, kT, rw, dom, offs, out):
         q_codes = [keep.tile([P, PASS], U32, name="q_codes%d" % g, align_bytes=64) for g in range(G)]
         q_scales = [keep.tile([P, PASS], U8, name="q_scales%d" % g, align_bytes=64) for g in range(G)]
         w_bf = [keep.tile([P, N, PACK], BF16, name="w_bf%d" % g, align_bytes=64) for g in range(G)]
-        w_codes = [keep.tile([P, N], U32, name="w_codes%d" % g, align_bytes=64) for g in range(G)]
-        w_scales = [keep.tile([P, N], U8, name="w_scales%d" % g, align_bytes=64) for g in range(G)]
+        w_codes = [keep.tile([P, HALF + N], U32, name="w_codes%d" % g, align_bytes=64) for g in range(G)]
+        w_scales = [keep.tile([P, HALF + N], U8, name="w_scales%d" % g, align_bytes=64) for g in range(G)]
         d_bf = {0: keep.tile([P, G, P, PACK], BF16, name="d_bf0", align_bytes=64)}
         d_codes = [keep.tile([P, G, P], U32, name="d_codes%d" % e, align_bytes=64) for e in range(E_TILES)]
         d_scales = [keep.tile([P, G, P], U8, name="d_scales%d" % e, align_bytes=64) for e in range(E_TILES)]
+
+        for g in range(G):
+            nc.gpsimd.memset(w_codes[g][:, :HALF], 0)
+            nc.gpsimd.memset(w_scales[g][:, :HALF], 0)
 
         def gather(j, lo, hi):
             nc.vector.tensor_copy(
@@ -102,15 +105,11 @@ def tile_attend_gat_v_kernel(tc, qT, kT, rw, dom, offs, out):
                 in_=k_bf[:, lo:hi, :].rearrange("p n j -> p (n j)"),
             )
 
-        def cast_q(i, engines):
-            g, h = divmod(i, PASS // Q_PIECE)
-            width = PACK // len(engines)
-            ms = slice(h * (Q_PIECE // PACK), (h + 1) * (Q_PIECE // PACK))
-            for s, engine in enumerate(engines):
-                ts = slice(s * width, (s + 1) * width)
-                src = q_raw[i][:].rearrange("p j (m t) -> p m t j", t=PACK)[:, :, ts]
-                dst = q_bf[g][:].rearrange("p t m j -> p m t j")[:, ms, ts]
-                cast(engine, dst, src)
+        def cast_q(raw, first, lo, hi, ts, engine):
+            g = lo // PASS
+            ms = slice((lo - g * PASS) // PACK, (hi - g * PASS) // PACK)
+            src = raw[:, :, lo - first : hi - first].rearrange("p j (m t) -> p m t j", t=PACK)
+            cast(engine, q_bf[g][:].rearrange("p t m j -> p m t j")[:, ms, ts], src[:, :, ts])
 
         def quant_q(g):
             nc.vector.quantize_mx(
@@ -121,11 +120,8 @@ def tile_attend_gat_v_kernel(tc, qT, kT, rw, dom, offs, out):
 
         def cast_d(e, g, engine):
             if e not in d_bf:
-                d_bf.setdefault(e, stage.tile([P, G, P, PACK], BF16, name="d_late", tag="stage", align_bytes=64))
-            if e == 0:
-                src = d_first[g][:]
-            else:
-                src = d_rest[g][:, :, (e - 1) * P : e * P]
+                d_bf.setdefault(e, late.tile([P, G, P, PACK], BF16, name="d_late", tag="stage", align_bytes=64))
+            src = d_first[g][:] if e == 0 else d_rest[g][:, :, (e - 1) * P : e * P]
             cast(engine, d_bf[e][:, g], src.rearrange("p j e -> p e j"))
 
         def quant_d(e):
@@ -135,7 +131,7 @@ def tile_attend_gat_v_kernel(tc, qT, kT, rw, dom, offs, out):
                 in_=d_bf[e][:].rearrange("p g e j -> p (g e j)"),
             )
 
-        def weights(g, c):
+        def weights(g, c, pool):
             cols = slice(c * CH, (c + 1) * CH)
             bank = spsum.tile([P, PACK, CH], F32, name="scores")
             for t in range(PACK):
@@ -148,7 +144,7 @@ def tile_attend_gat_v_kernel(tc, qT, kT, rw, dom, offs, out):
                     start=True,
                     stop=True,
                 )
-            gated = stage.tile([P, PACK, CH], F32, name="gated", tag="stage", align_bytes=64)
+            gated = pool.tile([P, PACK, CH], F32, name="gated", tag="stage", align_bytes=64)
             for t in range(PACK):
                 nc.scalar.activation(out=gated[:, t, :], in_=bank[:, t, :], func=COPY, scale=gate[:, g, t : t + 1])
             nc.vector.scalar_tensor_tensor(
@@ -162,74 +158,80 @@ def tile_attend_gat_v_kernel(tc, qT, kT, rw, dom, offs, out):
 
         def quant_w(g, lo, hi):
             nc.vector.quantize_mx(
-                out=w_codes[g][:, lo:hi].bitcast(E4),
-                scales=w_scales[g][:, lo:hi],
+                out=w_codes[g][:, HALF + lo : HALF + hi].bitcast(E4),
+                scales=w_scales[g][:, HALF + lo : HALF + hi],
                 in_=w_bf[g][:, lo:hi, :].rearrange("p n t -> p (n t)"),
             )
 
-        def product(e, parts):
+        def product(e, first):
             acc = opsum.tile([P, N], F32, name="acc")
             for g in range(G):
                 nc.tensor.matmul_mx(
                     out=acc[:],
                     lhsT=d_codes[e][:, g, :].bitcast(E5),
                     lhsT_scale=d_scales[e][:, g, :],
-                    rhs=w_codes[g][:].bitcast(E4),
-                    rhs_scale=w_scales[g][:],
+                    rhs=w_codes[g][:, first : first + N].bitcast(E4),
+                    rhs_scale=w_scales[g][:, first : first + N],
                     start=(g == 0),
                     stop=(g == G - 1),
                 )
-            dense = ring.tile([P, N], F32, name="dense")
-            width = N // parts
-            for s in range(parts):
-                cols = slice(s * width, (s + 1) * width)
-                nc.scalar.activation(out=dense[:, cols], in_=acc[:, cols], func=COPY)
-            return dense
+            return acc
 
-        def place(e, dense, parts):
-            window = windows[e % WINDOWS]
-            width = N // parts
-            for s in range(parts):
-                lo, hi = s * width, (s + 1) * width
-                nc.vector.tensor_copy(out=window[:].indirect(offsets[:, lo // 16 : hi // 16]), in_=dense[:, lo:hi])
-            nc.sync.dma_start(out=out[e * P : (e + 1) * P, :], in_=window[:])
+        def new_dense(pool):
+            return pool.tile([P, N], F32, name="dense", tag="stage", align_bytes=64)
 
+        def place(e, src, lo, hi):
+            nc.vector.tensor_copy(out=windows[e][:].indirect(offsets[:, lo // 16 : hi // 16]), in_=src)
+
+        def store(e):
+            nc.sync.dma_start(out=out[e * P : (e + 1) * P, :], in_=windows[e][:])
+
+        cast_q(q_head, 0, 0, PASS, slice(0, PACK), "S")
+        cast_q(q_head, 0, PASS, Q_CUT, slice(0, PACK), "S")
         for j in range(PACK - 1):
             gather(j, 0, N)
-        gather(PACK - 1, 0, N // 2)
-        gather(PACK - 1, N // 2, N)
-        quant_k(0, N // 2)
-        quant_k(N // 2, N)
-        cast_q(0, "S")
-        cast_q(1, "V")
         quant_q(0)
-        cast_q(2, "V")
-        weights(0, 0)
-        weights(0, 1)
-        cast_q(3, "VS")
+        gather(PACK - 1, 0, HALF)
+        quant_k(0, HALF)
+        gather(PACK - 1, HALF, N)
+        quant_k(HALF, N)
+        cast_q(q_tail, Q_CUT, Q_CUT, R, slice(0, 2), "S")
+        cast_q(q_tail, Q_CUT, Q_CUT, R, slice(2, PACK), "V")
         quant_q(1)
-        weights(0, 2)
-        weights(0, 3)
-        weights(1, 0)
-        cast_d(0, 0, "V")
+        weights(0, 0, stage)
+        weights(0, 1, stage)
+        weights(1, 0, stage)
+        cast_d(0, 0, "S")
+        quant_w(0, 0, HALF)
+        weights(1, 1, stage)
         cast_d(0, 1, "S")
-        quant_w(0, 0, N)
-        weights(1, 1)
+        weights(0, 2, stage)
+        quant_w(1, 0, HALF)
         quant_d(0)
-        weights(1, 2)
-        quant_w(1, 0, N // 2)
-        weights(1, 3)
-        quant_w(1, N // 2, 3 * N // 4)
-        quant_w(1, 3 * N // 4, N)
-        dense = product(0, 2)
+        weights(0, 3, late)
+        weights(1, 2, stage)
+        quant_w(0, HALF, N)
+        weights(1, 3, final)
+        acc_a = product(0, 0)
+        dense_b = new_dense(stage)
+        dense_a = new_dense(final)
+        quant_w(1, HALF, N)
+        nc.scalar.activation(out=dense_a[:, :HALF], in_=acc_a[:, HALF:], func=COPY)
+        acc = product(0, HALF)
+        nc.scalar.activation(out=dense_b[:, :HALF], in_=acc[:, HALF:], func=COPY)
         for g in range(G):
             cast_d(1, g, "S")
         quant_d(1)
-        place(0, dense, 2)
+        place(0, dense_a[:, :HALF], 0, HALF)
+        place(0, dense_b[:, :HALF], HALF, N)
+        store(0)
         for e in range(1, E_TILES):
-            dense = product(e, 1)
+            acc = product(e, HALF)
+            dense = new_dense(stage)
+            nc.scalar.activation(out=dense[:], in_=acc[:], func=COPY)
             if e + 1 < E_TILES:
                 for g in range(G):
                     cast_d(e + 1, g, "S")
                 quant_d(e + 1)
-            place(e, dense, 1)
+            place(e, dense[:], 0, N)
+            store(e)

@@ -54,7 +54,7 @@ def tile_attend_gat_v_kernel(tc, qT, kT, rw, dom, offs, out):
         q_head = keep.tile([P, PACK, Q_CUT], F32, name="q_head")
         q_tail = keep.tile([P, PACK, R - Q_CUT], F32, name="q_tail")
 
-        gate = keep.tile([P, G, PACK], F32, name="gate")
+        gate = keep.tile([P, G, 2 * PACK], F32, name="gate")
         d_rows = dom[0].rearrange("(g p j) e -> g p j e", p=P, j=PACK)
         d_first = [keep.tile([P, PACK, P], F32, name="d_first%d" % g) for g in range(G)]
         d_rest = [keep.tile([P, PACK, DV - P], F32, name="d_rest%d" % g) for g in range(G)]
@@ -62,10 +62,10 @@ def tile_attend_gat_v_kernel(tc, qT, kT, rw, dom, offs, out):
 
         nc.sync.dma_start(out=q_head[:], in_=q_rows[:, :, :Q_CUT])
         nc.sync.dma_start(offsets[:], offs)
-        nc.sync.dma_start(out=gate[:], in_=rw[0].rearrange("(g p t) o -> p g (t o)", p=P, t=PACK))
         for j in range(PACK):
             nc.sync.dma_start(out=k_planes[j][:], in_=k_rows[:, j, :])
         nc.sync.dma_start(out=q_tail[:], in_=q_rows[:, :, Q_CUT:])
+        nc.sync.dma_start(out=gate[:, :, :PACK], in_=rw[0].rearrange("(g p t) o -> p g (t o)", p=P, t=PACK))
         for g in range(G):
             nc.sync.dma_start(out=d_first[g][:], in_=d_rows[g, :, :, 0:P])
         for g in range(G):
@@ -77,6 +77,7 @@ def tile_attend_gat_v_kernel(tc, qT, kT, rw, dom, offs, out):
             nc.gpsimd.memset(window[:], 0.0)
 
         k_bf = keep.tile([P, N, PACK], BF16, name="k_bf", align_bytes=64)
+        k_dense = keep.tile([P, PACK, N], F32, name="k_dense")
         k_codes = keep.tile([P, N], U32, name="k_codes", align_bytes=64)
         k_scales = keep.tile([P, N], U8, name="k_scales", align_bytes=64)
         q_bf = [keep.tile([P, PACK, P, PACK], BF16, name="q_bf%d" % g, align_bytes=64) for g in range(G)]
@@ -95,8 +96,11 @@ def tile_attend_gat_v_kernel(tc, qT, kT, rw, dom, offs, out):
 
         def gather(j, lo, hi):
             nc.vector.tensor_copy(
-                out=k_bf[:, lo:hi, j], in_=k_planes[j][:].indirect(offsets[:, lo // 16 : hi // 16])
+                out=k_dense[:, j, lo:hi], in_=k_planes[j][:].indirect(offsets[:, lo // 16 : hi // 16])
             )
+
+        def cast_k(j, lo, hi, engine):
+            cast(engine, k_bf[:, lo:hi, j : j + 2], k_dense[:, j : j + 2, lo:hi].rearrange("p j n -> p n j"))
 
         def quant_k(lo, hi):
             nc.vector.quantize_mx(
@@ -191,9 +195,12 @@ def tile_attend_gat_v_kernel(tc, qT, kT, rw, dom, offs, out):
         for j in range(PACK - 1):
             gather(j, 0, N)
         quant_q(0)
+        cast_k(0, 0, N, "S")
         gather(PACK - 1, 0, HALF)
-        quant_k(0, HALF)
         gather(PACK - 1, HALF, N)
+        cast_k(2, 0, HALF, "V")
+        cast_k(2, HALF, N, "V")
+        quant_k(0, HALF)
         quant_k(HALF, N)
         cast_q(q_tail, Q_CUT, Q_CUT, R, slice(0, 2), "S")
         cast_q(q_tail, Q_CUT, Q_CUT, R, slice(2, PACK), "V")

@@ -24,7 +24,7 @@ G = R // PASS
 E_TILES = DV // P
 CH = 128
 HALF = N // 2
-Q_CUT = 768
+Q_PIECE = 256
 WINDOWS = 4
 
 
@@ -41,7 +41,10 @@ def tile_attend_gat_v_kernel(tc, qT, kT, rw, dom, offs, out):
 
     with ExitStack() as ctx:
         keep = ctx.enter_context(tc.tile_pool(name="keep", bufs=1))
-        late = ctx.enter_context(tc.tile_pool(name="late", bufs=1))
+        late1 = ctx.enter_context(tc.tile_pool(name="late1", bufs=1))
+        late2 = ctx.enter_context(tc.tile_pool(name="late2", bufs=1))
+        mid_pool = ctx.enter_context(tc.tile_pool(name="mid_pool", bufs=1))
+        last_pool = ctx.enter_context(tc.tile_pool(name="last_pool", bufs=1))
         stage = ctx.enter_context(tc.tile_pool(name="stage", bufs=3))
         final = ctx.enter_context(tc.tile_pool(name="final", bufs=1))
         spsum = ctx.enter_context(tc.psum_pool(name="spsum", bufs=6))
@@ -51,25 +54,36 @@ def tile_attend_gat_v_kernel(tc, qT, kT, rw, dom, offs, out):
         k_planes = [keep.tile([P, T], F32, name="k_plane%d" % j) for j in range(PACK)]
         k_rows = kT.rearrange("(p j) c -> p j c", j=PACK)
         q_rows = qT[0].rearrange("(p j) r -> p j r", j=PACK)
-        q_head = keep.tile([P, PACK, Q_CUT], F32, name="q_head")
-        q_tail = keep.tile([P, PACK, R - Q_CUT], F32, name="q_tail")
+        q_head = keep.tile([P, PACK, PASS], F32, name="q_head")
+        q_mid = keep.tile([P, PACK, Q_PIECE], F32, name="q_mid")
+        q_tail = keep.tile([P, PACK, Q_PIECE], F32, name="q_tail")
 
         gate = keep.tile([P, G, 2 * PACK], F32, name="gate")
         d_rows = dom[0].rearrange("(g p j) e -> g p j e", p=P, j=PACK)
         d_first = [keep.tile([P, PACK, P], F32, name="d_first%d" % g) for g in range(G)]
-        d_rest = [keep.tile([P, PACK, DV - P], F32, name="d_rest%d" % g) for g in range(G)]
+        d_mid = [
+            keep.tile([P, PACK, 2 * P], F32, name="d_mid0"),
+            mid_pool.tile([P, PACK, 2 * P], F32, name="d_mid1", tag="stage", align_bytes=64),
+        ]
+        d_last = [
+            keep.tile([P, PACK, P], F32, name="d_last0"),
+            last_pool.tile([P, PACK, P], F32, name="d_last1", tag="stage", align_bytes=64),
+        ]
         windows = [keep.tile([P, T], F32, name="window%d" % e) for e in range(WINDOWS)]
 
-        nc.sync.dma_start(out=q_head[:], in_=q_rows[:, :, :Q_CUT])
+        nc.sync.dma_start(out=q_head[:], in_=q_rows[:, :, :PASS])
         nc.sync.dma_start(offsets[:], offs)
         for j in range(PACK):
             nc.sync.dma_start(out=k_planes[j][:], in_=k_rows[:, j, :])
-        nc.sync.dma_start(out=q_tail[:], in_=q_rows[:, :, Q_CUT:])
+        nc.sync.dma_start(out=q_mid[:], in_=q_rows[:, :, PASS : PASS + Q_PIECE])
+        nc.sync.dma_start(out=q_tail[:], in_=q_rows[:, :, PASS + Q_PIECE :])
         nc.sync.dma_start(out=gate[:, :, :PACK], in_=rw[0].rearrange("(g p t) o -> p g (t o)", p=P, t=PACK))
         for g in range(G):
             nc.sync.dma_start(out=d_first[g][:], in_=d_rows[g, :, :, 0:P])
         for g in range(G):
-            nc.sync.dma_start(out=d_rest[g][:], in_=d_rows[g, :, :, P:DV])
+            nc.sync.dma_start(out=d_mid[g][:], in_=d_rows[g, :, :, P : 3 * P])
+        for g in range(G):
+            nc.sync.dma_start(out=d_last[g][:], in_=d_rows[g, :, :, 3 * P : DV])
 
         for window in windows[:2]:
             nc.vector.memset(window[:], 0.0)
@@ -124,9 +138,13 @@ def tile_attend_gat_v_kernel(tc, qT, kT, rw, dom, offs, out):
 
         def cast_d(e, g, engine):
             if e not in d_bf:
-                d_bf.setdefault(e, late.tile([P, G, P, PACK], BF16, name="d_late", tag="stage", align_bytes=64))
-            src = d_first[g][:] if e == 0 else d_rest[g][:, :, (e - 1) * P : e * P]
-            cast(engine, d_bf[e][:, g], src.rearrange("p j e -> p e j"))
+                d_bf.setdefault(e, (late2 if e == 2 else late1).tile([P, G, P, PACK], BF16, name="d_late", tag="stage", align_bytes=64))
+            src = {0: d_first[g][:], 1: d_mid[g][:, :, :P], 2: d_mid[g][:, :, P:], 3: d_last[g][:]}[e]
+            cast(
+                engine,
+                d_bf[e][:, g].rearrange("p (c i) j -> p c j i", i=PACK),
+                src.rearrange("p j (c i) -> p c j i", i=PACK),
+            )
 
         def quant_d(e):
             nc.vector.quantize_mx(
@@ -191,54 +209,58 @@ def tile_attend_gat_v_kernel(tc, qT, kT, rw, dom, offs, out):
             nc.sync.dma_start(out=out[e * P : (e + 1) * P, :], in_=windows[e][:])
 
         cast_q(q_head, 0, 0, PASS, slice(0, PACK), "S")
-        cast_q(q_head, 0, PASS, Q_CUT, slice(0, PACK), "S")
         for j in range(PACK - 1):
             gather(j, 0, N)
         quant_q(0)
         cast_k(0, 0, N, "S")
-        gather(PACK - 1, 0, HALF)
         gather(PACK - 1, HALF, N)
+        gather(PACK - 1, 0, HALF)
+        cast_k(2, HALF, HALF + CH, "S")
+        cast_k(2, HALF + CH, N, "S")
         cast_k(2, 0, HALF, "V")
-        cast_k(2, HALF, N, "V")
+        quant_k(HALF, HALF + CH)
         quant_k(0, HALF)
-        quant_k(HALF, N)
-        cast_q(q_tail, Q_CUT, Q_CUT, R, slice(0, 2), "S")
-        cast_q(q_tail, Q_CUT, Q_CUT, R, slice(2, PACK), "V")
+        quant_k(HALF + CH, N)
+        cast_q(q_mid, PASS, PASS, PASS + Q_PIECE, slice(0, 2), "S")
+        cast_q(q_mid, PASS, PASS, PASS + Q_PIECE, slice(2, PACK), "S")
+        cast_q(q_tail, PASS + Q_PIECE, PASS + Q_PIECE, R, slice(0, PACK), "V")
         quant_q(1)
+        weights(0, 2, stage)
         weights(0, 0, stage)
         weights(0, 1, stage)
-        weights(1, 0, stage)
         cast_d(0, 0, "S")
+        weights(1, 0, stage)
         quant_w(0, 0, HALF)
-        weights(1, 1, stage)
         cast_d(0, 1, "S")
-        weights(0, 2, stage)
-        quant_w(1, 0, HALF)
+        weights(1, 1, stage)
         quant_d(0)
-        weights(0, 3, late)
-        weights(1, 2, stage)
+        weights(0, 3, late1)
+        quant_w(1, 0, HALF)
+        weights(1, 2, late2)
         quant_w(0, HALF, N)
         weights(1, 3, final)
         acc_a = product(0, 0)
-        dense_b = new_dense(stage)
-        dense_a = new_dense(final)
-        quant_w(1, HALF, N)
-        nc.scalar.activation(out=dense_a[:, :HALF], in_=acc_a[:, HALF:], func=COPY)
-        acc = product(0, HALF)
-        nc.scalar.activation(out=dense_b[:, :HALF], in_=acc[:, HALF:], func=COPY)
         for g in range(G):
             cast_d(1, g, "S")
+        quant_w(1, HALF, N)
         quant_d(1)
+        dense_a = new_dense(final)
+        nc.scalar.activation(out=dense_a[:, :HALF], in_=acc_a[:, HALF:], func=COPY)
+        acc = product(0, HALF)
+        for g in range(G):
+            cast_d(2, g, "S")
+        dense_b = new_dense(mid_pool)
+        nc.scalar.activation(out=dense_b[:, :HALF], in_=acc[:, HALF:], func=COPY)
         place(0, dense_a[:, :HALF], 0, HALF)
+        quant_d(2)
         place(0, dense_b[:, :HALF], HALF, N)
         store(0)
+        for g in range(G):
+            cast_d(3, g, "S")
+        quant_d(3)
         for e in range(1, E_TILES):
             acc = product(e, HALF)
-            dense = new_dense(stage)
+            dense = new_dense(last_pool if e == 1 else stage)
             nc.scalar.activation(out=dense[:], in_=acc[:], func=COPY)
-            if e + 1 < E_TILES:
-                for g in range(G):
-                    cast_d(e + 1, g, "S")
-                quant_d(e + 1)
             place(e, dense[:], 0, N)
             store(e)

@@ -1,6 +1,7 @@
 from contextlib import ExitStack
 
 import concourse.mybir as mybir
+from concourse.masks import make_identity
 
 N, T, D, DV, R = 512, 2048, 512, 512, 1024
 FLOPS = 2 * R * N * D + 2 * R * N * DV
@@ -42,7 +43,6 @@ def tile_attend_gat_v_kernel(tc, qT, kT, rw, dom, offs, out):
     with ExitStack() as ctx:
         keep = ctx.enter_context(tc.tile_pool(name="keep", bufs=1))
         late1 = ctx.enter_context(tc.tile_pool(name="late1", bufs=1))
-        late2 = ctx.enter_context(tc.tile_pool(name="late2", bufs=1))
         mid_pool = ctx.enter_context(tc.tile_pool(name="mid_pool", bufs=1))
         last_pool = ctx.enter_context(tc.tile_pool(name="last_pool", bufs=1))
         stage = ctx.enter_context(tc.tile_pool(name="stage", bufs=3))
@@ -58,7 +58,9 @@ def tile_attend_gat_v_kernel(tc, qT, kT, rw, dom, offs, out):
         q_mid = keep.tile([P, PACK, Q_PIECE], F32, name="q_mid")
         q_tail = keep.tile([P, PACK, Q_PIECE], F32, name="q_tail")
 
-        gate = keep.tile([P, G, 2 * PACK], F32, name="gate")
+        gate_rows = keep.tile([P, PASS], F32, name="gate_rows")
+        identity = keep.tile([P, P], F32, name="identity")
+        gate = keep.tile([P, PACK, G], F32, name="gate")
         d_rows = dom[0].rearrange("(g p j) e -> g p j e", p=P, j=PACK)
         d_first = [keep.tile([P, PACK, P], F32, name="d_first%d" % g) for g in range(G)]
         d_mid = [
@@ -71,13 +73,14 @@ def tile_attend_gat_v_kernel(tc, qT, kT, rw, dom, offs, out):
         ]
         windows = [keep.tile([P, T], F32, name="window%d" % e) for e in range(WINDOWS)]
 
+        nc.vector.memset(gate_rows[:], 0.0)
         nc.sync.dma_start(out=q_head[:], in_=q_rows[:, :, :PASS])
         nc.sync.dma_start(offsets[:], offs)
+        nc.sync.dma_start(out=gate_rows[:G, :], in_=rw[0].rearrange("(g r) o -> g (r o)", g=G))
         for j in range(PACK):
             nc.sync.dma_start(out=k_planes[j][:], in_=k_rows[:, j, :])
         nc.sync.dma_start(out=q_mid[:], in_=q_rows[:, :, PASS : PASS + Q_PIECE])
         nc.sync.dma_start(out=q_tail[:], in_=q_rows[:, :, PASS + Q_PIECE :])
-        nc.sync.dma_start(out=gate[:, :, :PACK], in_=rw[0].rearrange("(g p t) o -> p g (t o)", p=P, t=PACK))
         for g in range(G):
             nc.sync.dma_start(out=d_first[g][:], in_=d_rows[g, :, :, 0:P])
         for g in range(G):
@@ -89,6 +92,12 @@ def tile_attend_gat_v_kernel(tc, qT, kT, rw, dom, offs, out):
             nc.vector.memset(window[:], 0.0)
         for window in windows[2:]:
             nc.gpsimd.memset(window[:], 0.0)
+
+        make_identity(nc, identity[:])
+        turned = spsum.tile([P, PACK, CH], F32, name="scores")
+        for t in range(PACK):
+            nc.tensor.transpose(turned[:, t, :], gate_rows[:, t::PACK], identity[:])
+        nc.scalar.activation(out=gate[:], in_=turned[:, :, :G], func=COPY)
 
         k_bf = keep.tile([P, N, PACK], BF16, name="k_bf", align_bytes=64)
         k_dense = keep.tile([P, PACK, N], F32, name="k_dense")
@@ -105,8 +114,8 @@ def tile_attend_gat_v_kernel(tc, qT, kT, rw, dom, offs, out):
         d_scales = [keep.tile([P, G, P], U8, name="d_scales%d" % e, align_bytes=64) for e in range(E_TILES)]
 
         for g in range(G):
-            nc.gpsimd.memset(w_codes[g][:, :HALF], 0)
-            nc.gpsimd.memset(w_scales[g][:, :HALF], 0)
+            nc.gpsimd.memset(w_codes[g][:, N:], 0)
+            nc.gpsimd.memset(w_scales[g][:, N:], 0)
 
         def gather(j, lo, hi):
             nc.vector.tensor_copy(
@@ -123,11 +132,11 @@ def tile_attend_gat_v_kernel(tc, qT, kT, rw, dom, offs, out):
                 in_=k_bf[:, lo:hi, :].rearrange("p n j -> p (n j)"),
             )
 
-        def cast_q(raw, first, lo, hi, ts, engine):
+        def cast_q(raw, first, lo, hi, engine):
             g = lo // PASS
             ms = slice((lo - g * PASS) // PACK, (hi - g * PASS) // PACK)
-            src = raw[:, :, lo - first : hi - first].rearrange("p j (m t) -> p m t j", t=PACK)
-            cast(engine, q_bf[g][:].rearrange("p t m j -> p m t j")[:, ms, ts], src[:, :, ts])
+            src = raw[:, :, lo - first : hi - first].rearrange("p j (m t) -> p m j t", t=PACK)
+            cast(engine, q_bf[g][:].rearrange("p t m j -> p m j t")[:, ms], src)
 
         def quant_q(g):
             nc.vector.quantize_mx(
@@ -137,8 +146,10 @@ def tile_attend_gat_v_kernel(tc, qT, kT, rw, dom, offs, out):
             )
 
         def cast_d(e, g, engine):
+            if e == 2 and e not in d_bf:
+                d_bf.setdefault(e, final.tile([P, G, P, PACK], BF16, name="d_bf2", align_bytes=64, offset=4 * HALF))
             if e not in d_bf:
-                d_bf.setdefault(e, (late2 if e == 2 else late1).tile([P, G, P, PACK], BF16, name="d_late", tag="stage", align_bytes=64))
+                d_bf.setdefault(e, late1.tile([P, G, P, PACK], BF16, name="d_late", tag="stage", align_bytes=64))
             src = {0: d_first[g][:], 1: d_mid[g][:, :, :P], 2: d_mid[g][:, :, P:], 3: d_last[g][:]}[e]
             cast(
                 engine,
@@ -166,9 +177,12 @@ def tile_attend_gat_v_kernel(tc, qT, kT, rw, dom, offs, out):
                     start=True,
                     stop=True,
                 )
-            gated = pool.tile([P, PACK, CH], F32, name="gated", tag="stage", align_bytes=64)
+            if pool is final:
+                gated = pool.tile([P, PACK, CH], F32, name="gated_last", align_bytes=64, offset=0)
+            else:
+                gated = pool.tile([P, PACK, CH], F32, name="gated", tag="stage", align_bytes=64)
             for t in range(PACK):
-                nc.scalar.activation(out=gated[:, t, :], in_=bank[:, t, :], func=COPY, scale=gate[:, g, t : t + 1])
+                nc.scalar.activation(out=gated[:, t, :], in_=bank[:, t, :], func=COPY, scale=gate[:, t, g : g + 1])
             nc.vector.scalar_tensor_tensor(
                 out=w_bf[g][:, cols, :],
                 in0=bank[:].rearrange("p t n -> p n t"),
@@ -180,8 +194,8 @@ def tile_attend_gat_v_kernel(tc, qT, kT, rw, dom, offs, out):
 
         def quant_w(g, lo, hi):
             nc.vector.quantize_mx(
-                out=w_codes[g][:, HALF + lo : HALF + hi].bitcast(E4),
-                scales=w_scales[g][:, HALF + lo : HALF + hi],
+                out=w_codes[g][:, lo:hi].bitcast(E4),
+                scales=w_scales[g][:, lo:hi],
                 in_=w_bf[g][:, lo:hi, :].rearrange("p n t -> p (n t)"),
             )
 
@@ -208,58 +222,58 @@ def tile_attend_gat_v_kernel(tc, qT, kT, rw, dom, offs, out):
         def store(e):
             nc.sync.dma_start(out=out[e * P : (e + 1) * P, :], in_=windows[e][:])
 
-        cast_q(q_head, 0, 0, PASS, slice(0, PACK), "S")
+        cast_q(q_head, 0, 0, PASS, "S")
         for j in range(PACK - 1):
             gather(j, 0, N)
         quant_q(0)
         cast_k(0, 0, N, "S")
         gather(PACK - 1, HALF, N)
         gather(PACK - 1, 0, HALF)
-        cast_k(2, HALF, HALF + CH, "S")
+        cast_k(2, HALF, HALF + CH, "V")
         cast_k(2, HALF + CH, N, "S")
         cast_k(2, 0, HALF, "V")
         quant_k(HALF, HALF + CH)
-        quant_k(0, HALF)
         quant_k(HALF + CH, N)
-        cast_q(q_mid, PASS, PASS, PASS + Q_PIECE, slice(0, 2), "S")
-        cast_q(q_mid, PASS, PASS, PASS + Q_PIECE, slice(2, PACK), "S")
-        cast_q(q_tail, PASS + Q_PIECE, PASS + Q_PIECE, R, slice(0, PACK), "V")
+        quant_k(0, HALF)
+        cast_q(q_mid, PASS, PASS, PASS + Q_PIECE // 2, "S")
+        cast_q(q_mid, PASS, PASS + Q_PIECE // 2, PASS + Q_PIECE, "S")
+        cast_q(q_tail, PASS + Q_PIECE, PASS + Q_PIECE, R, "V")
         quant_q(1)
         weights(0, 2, stage)
+        weights(0, 3, stage)
         weights(0, 0, stage)
-        weights(0, 1, stage)
         cast_d(0, 0, "S")
+        weights(1, 2, stage)
+        quant_w(0, HALF, N)
+        cast_d(0, 1, "S")
+        weights(1, 3, stage)
+        quant_d(0)
+        weights(0, 1, late1)
+        quant_w(1, HALF, N)
         weights(1, 0, stage)
         quant_w(0, 0, HALF)
-        cast_d(0, 1, "S")
-        weights(1, 1, stage)
-        quant_d(0)
-        weights(0, 3, late1)
-        quant_w(1, 0, HALF)
-        weights(1, 2, late2)
-        quant_w(0, HALF, N)
-        weights(1, 3, final)
-        acc_a = product(0, 0)
+        weights(1, 1, final)
+        acc_a = product(0, HALF)
         for g in range(G):
             cast_d(1, g, "S")
-        quant_w(1, HALF, N)
+        quant_w(1, 0, HALF)
         quant_d(1)
-        dense_a = new_dense(final)
-        nc.scalar.activation(out=dense_a[:, :HALF], in_=acc_a[:, HALF:], func=COPY)
-        acc = product(0, HALF)
+        dense_a = final.tile([P, HALF], F32, name="dense_a", align_bytes=64, offset=0)
+        nc.scalar.activation(out=dense_a[:], in_=acc_a[:, :HALF], func=COPY)
+        acc = product(0, 0)
         for g in range(G):
             cast_d(2, g, "S")
         dense_b = new_dense(mid_pool)
-        nc.scalar.activation(out=dense_b[:, :HALF], in_=acc[:, HALF:], func=COPY)
-        place(0, dense_a[:, :HALF], 0, HALF)
+        nc.scalar.activation(out=dense_b[:, :HALF], in_=acc[:, :HALF], func=COPY)
+        place(0, dense_a[:], HALF, N)
         quant_d(2)
-        place(0, dense_b[:, :HALF], HALF, N)
+        place(0, dense_b[:, :HALF], 0, HALF)
         store(0)
         for g in range(G):
             cast_d(3, g, "S")
         quant_d(3)
         for e in range(1, E_TILES):
-            acc = product(e, HALF)
+            acc = product(e, 0)
             dense = new_dense(last_pool if e == 1 else stage)
             nc.scalar.activation(out=dense[:], in_=acc[:], func=COPY)
             place(e, dense[:], 0, N)

@@ -73,10 +73,10 @@ def tile_attend_gat_v_kernel(tc, qT, kT, rw, dom, offs, out):
         ]
         windows = [keep.tile([P, T], F32, name="window%d" % e) for e in range(WINDOWS)]
 
-        nc.vector.memset(gate_rows[:], 0.0)
+        nc.gpsimd.memset(gate_rows[:], 0.0)
         nc.sync.dma_start(out=q_head[:], in_=q_rows[:, :, :PASS])
         nc.sync.dma_start(offsets[:], offs)
-        nc.sync.dma_start(out=gate_rows[:G, :], in_=rw[0].rearrange("(g r) o -> g (r o)", g=G))
+        nc.scalar.dma_start(out=gate_rows[:G, :], in_=rw[0].rearrange("(g r) o -> g (r o)", g=G))
         for j in range(PACK):
             nc.sync.dma_start(out=k_planes[j][:], in_=k_rows[:, j, :])
         nc.sync.dma_start(out=q_mid[:], in_=q_rows[:, :, PASS : PASS + Q_PIECE])

@@ -26,7 +26,7 @@ E_TILES = DV // P
 CH = 128
 HALF = N // 2
 Q_PIECE = 256
-WINDOWS = 4
+WINDOWS = 3
 
 
 def tile_attend_gat_v_kernel(tc, qT, kT, rw, dom, offs, out):
@@ -73,7 +73,7 @@ def tile_attend_gat_v_kernel(tc, qT, kT, rw, dom, offs, out):
         ]
         windows = [keep.tile([P, T], F32, name="window%d" % e) for e in range(WINDOWS)]
 
-        nc.gpsimd.memset(gate_rows[:], 0.0)
+        nc.vector.memset(gate_rows[:], 0.0)
         nc.sync.dma_start(out=q_head[:], in_=q_rows[:, :, :PASS])
         nc.sync.dma_start(offsets[:], offs)
         nc.scalar.dma_start(out=gate_rows[:G, :], in_=rw[0].rearrange("(g r) o -> g (r o)", g=G))
@@ -88,10 +88,8 @@ def tile_attend_gat_v_kernel(tc, qT, kT, rw, dom, offs, out):
         for g in range(G):
             nc.sync.dma_start(out=d_last[g][:], in_=d_rows[g, :, :, 3 * P : DV])
 
-        for window in windows[:2]:
+        for window in windows:
             nc.vector.memset(window[:], 0.0)
-        for window in windows[2:]:
-            nc.gpsimd.memset(window[:], 0.0)
 
         make_identity(nc, identity[:])
         turned = spsum.tile([P, PACK, CH], F32, name="scores")
@@ -114,8 +112,8 @@ def tile_attend_gat_v_kernel(tc, qT, kT, rw, dom, offs, out):
         d_scales = [keep.tile([P, G, P], U8, name="d_scales%d" % e, align_bytes=64) for e in range(E_TILES)]
 
         for g in range(G):
-            nc.gpsimd.memset(w_codes[g][:, N:], 0)
-            nc.gpsimd.memset(w_scales[g][:, N:], 0)
+            nc.vector.memset(w_codes[g][:, N:], 0)
+            nc.vector.memset(w_scales[g][:, N:].bitcast(U32), 0)
 
         def gather(j, lo, hi):
             nc.vector.tensor_copy(
@@ -217,10 +215,10 @@ def tile_attend_gat_v_kernel(tc, qT, kT, rw, dom, offs, out):
             return pool.tile([P, N], F32, name="dense", tag="stage", align_bytes=64)
 
         def place(e, src, lo, hi):
-            nc.vector.tensor_copy(out=windows[e][:].indirect(offsets[:, lo // 16 : hi // 16]), in_=src)
+            nc.vector.tensor_copy(out=windows[e % WINDOWS][:].indirect(offsets[:, lo // 16 : hi // 16]), in_=src)
 
         def store(e):
-            nc.sync.dma_start(out=out[e * P : (e + 1) * P, :], in_=windows[e][:])
+            nc.sync.dma_start(out=out[e * P : (e + 1) * P, :], in_=windows[e % WINDOWS][:])
 
         cast_q(q_head, 0, 0, PASS, "S")
         for j in range(PACK - 1):

@@ -1,7 +1,6 @@
 from contextlib import ExitStack
 
 import concourse.mybir as mybir
-from concourse.masks import make_identity
 
 N, T, D, DV, R = 512, 2048, 512, 512, 1024
 FLOPS = 2 * R * N * D + 2 * R * N * DV
@@ -58,9 +57,7 @@ def tile_attend_gat_v_kernel(tc, qT, kT, rw, dom, offs, out):
         q_mid = keep.tile([P, PACK, Q_PIECE], F32, name="q_mid")
         q_tail = keep.tile([P, PACK, Q_PIECE], F32, name="q_tail")
 
-        gate_rows = keep.tile([P, PASS], F32, name="gate_rows")
-        identity = keep.tile([P, P], F32, name="identity")
-        gate = keep.tile([P, PACK, G], F32, name="gate")
+        gate = keep.tile([P, G, 2 * PACK], F32, name="gate")
         d_rows = dom[0].rearrange("(g p j) e -> g p j e", p=P, j=PACK)
         d_first = [keep.tile([P, PACK, P], F32, name="d_first%d" % g) for g in range(G)]
         d_mid = [
@@ -73,14 +70,13 @@ def tile_attend_gat_v_kernel(tc, qT, kT, rw, dom, offs, out):
         ]
         windows = [keep.tile([P, T], F32, name="window%d" % e) for e in range(WINDOWS)]
 
-        nc.vector.memset(gate_rows[:], 0.0)
         nc.sync.dma_start(out=q_head[:], in_=q_rows[:, :, :PASS])
         nc.sync.dma_start(offsets[:], offs)
-        nc.scalar.dma_start(out=gate_rows[:G, :], in_=rw[0].rearrange("(g r) o -> g (r o)", g=G))
         for j in range(PACK):
             nc.sync.dma_start(out=k_planes[j][:], in_=k_rows[:, j, :])
         nc.sync.dma_start(out=q_mid[:], in_=q_rows[:, :, PASS : PASS + Q_PIECE])
         nc.sync.dma_start(out=q_tail[:], in_=q_rows[:, :, PASS + Q_PIECE :])
+        nc.sync.dma_start(out=gate[:, :, :PACK], in_=rw[0].rearrange("(g p t) o -> p g (t o)", p=P, t=PACK))
         for g in range(G):
             nc.sync.dma_start(out=d_first[g][:], in_=d_rows[g, :, :, 0:P])
         for g in range(G):
@@ -90,12 +86,6 @@ def tile_attend_gat_v_kernel(tc, qT, kT, rw, dom, offs, out):
 
         for window in windows:
             nc.vector.memset(window[:], 0.0)
-
-        make_identity(nc, identity[:])
-        turned = spsum.tile([P, PACK, CH], F32, name="scores")
-        for t in range(PACK):
-            nc.tensor.transpose(turned[:, t, :], gate_rows[:, t::PACK], identity[:])
-        nc.scalar.activation(out=gate[:], in_=turned[:, :, :G], func=COPY)
 
         k_bf = keep.tile([P, N, PACK], BF16, name="k_bf", align_bytes=64)
         k_dense = keep.tile([P, PACK, N], F32, name="k_dense")
@@ -180,7 +170,7 @@ def tile_attend_gat_v_kernel(tc, qT, kT, rw, dom, offs, out):
             else:
                 gated = pool.tile([P, PACK, CH], F32, name="gated", tag="stage", align_bytes=64)
             for t in range(PACK):
-                nc.scalar.activation(out=gated[:, t, :], in_=bank[:, t, :], func=COPY, scale=gate[:, t, g : g + 1])
+                nc.scalar.activation(out=gated[:, t, :], in_=bank[:, t, :], func=COPY, scale=gate[:, g, t : t + 1])
             nc.vector.scalar_tensor_tensor(
                 out=w_bf[g][:, cols, :],
                 in0=bank[:].rearrange("p t n -> p n t"),

@@ -70,7 +70,7 @@ def tile_attend_gat_v_kernel(tc, qT, kT, rw, dom, offs, out):
         ]
         windows = [keep.tile([P, T], F32, name="window%d" % e) for e in range(WINDOWS)]
 
-        nc.sync.dma_start(out=q_head[:], in_=q_rows[:, :, :PASS])
+        nc.scalar.dma_start(out=q_head[:], in_=q_rows[:, :, :PASS])
         nc.sync.dma_start(offsets[:], offs)
         for j in range(PACK):
             nc.sync.dma_start(out=k_planes[j][:], in_=k_rows[:, j, :])
@@ -208,7 +208,12 @@ def tile_attend_gat_v_kernel(tc, qT, kT, rw, dom, offs, out):
             nc.vector.tensor_copy(out=windows[e % WINDOWS][:].indirect(offsets[:, lo // 16 : hi // 16]), in_=src)
 
         def store(e):
-            nc.sync.dma_start(out=out[e * P : (e + 1) * P, :], in_=windows[e % WINDOWS][:])
+            rows = out[e * P : (e + 1) * P, :]
+            if e + 1 < E_TILES:
+                nc.sync.dma_start(out=rows, in_=windows[e % WINDOWS][:])
+            else:
+                nc.sync.dma_start(out=rows[:, : T // 2], in_=windows[e % WINDOWS][:, : T // 2])
+                nc.scalar.dma_start(out=rows[:, T // 2 :], in_=windows[e % WINDOWS][:, T // 2 :])
 
         cast_q(q_head, 0, 0, PASS, "S")
         for j in range(PACK - 1):

@@ -166,16 +166,16 @@ def tile_attend_gat_v_kernel(tc, qT, kT, rw, dom, offs, out):
                     stop=True,
                 )
             if pool is final:
-                gated = pool.tile([P, PACK, CH], F32, name="gated_last", align_bytes=64, offset=0)
+                gated = pool.tile([P, PACK, CH + 1], F32, name="gated_last", align_bytes=64, offset=0)
             else:
-                gated = pool.tile([P, PACK, CH], F32, name="gated", tag="stage", align_bytes=64)
+                gated = pool.tile([P, PACK, CH + 1], F32, name="gated", tag="stage", align_bytes=64)
             for t in range(PACK):
-                nc.scalar.activation(out=gated[:, t, :], in_=bank[:, t, :], func=COPY, scale=gate[:, g, t : t + 1])
+                nc.scalar.activation(out=gated[:, t, :CH], in_=bank[:, t, :], func=COPY, scale=gate[:, g, t : t + 1])
             nc.vector.scalar_tensor_tensor(
                 out=w_bf[g][:, cols, :],
                 in0=bank[:].rearrange("p t n -> p n t"),
                 scalar=0.0,
-                in1=gated[:].rearrange("p t n -> p n t"),
+                in1=gated[:, :, :CH].rearrange("p t n -> p n t"),
                 op0=MAX,
                 op1=MULT,
             )
@@ -235,7 +235,7 @@ def tile_attend_gat_v_kernel(tc, qT, kT, rw, dom, offs, out):
         weights(0, 2, stage)
         weights(0, 3, stage)
         weights(0, 0, stage)
-        cast_d(0, 0, "S")
+        cast_d(0, 0, "V")
         weights(1, 2, stage)
         quant_w(0, HALF, N)
         cast_d(0, 1, "S")

@@ -25,6 +25,7 @@ E_TILES = DV // P
 CH = 128
 HALF = N // 2
 Q_PIECE = 256
+Q_SHARE = 96
 WINDOWS = 3
 
 
@@ -41,6 +42,7 @@ def tile_attend_gat_v_kernel(tc, qT, kT, rw, dom, offs, out):
 
     with ExitStack() as ctx:
         keep = ctx.enter_context(tc.tile_pool(name="keep", bufs=1))
+        after_q = ctx.enter_context(tc.tile_pool(name="after_q", bufs=1))
         late1 = ctx.enter_context(tc.tile_pool(name="late1", bufs=1))
         mid_pool = ctx.enter_context(tc.tile_pool(name="mid_pool", bufs=1))
         last_pool = ctx.enter_context(tc.tile_pool(name="last_pool", bufs=1))
@@ -91,13 +93,16 @@ def tile_attend_gat_v_kernel(tc, qT, kT, rw, dom, offs, out):
         k_dense = keep.tile([P, PACK, N], F32, name="k_dense")
         k_codes = keep.tile([P, N], U32, name="k_codes", align_bytes=64)
         k_scales = keep.tile([P, N], U8, name="k_scales", align_bytes=64)
-        q_bf = [keep.tile([P, PACK, P, PACK], BF16, name="q_bf%d" % g, align_bytes=64) for g in range(G)]
+        q_bf = [
+            keep.tile([P, PACK, P, PACK], BF16, name="q_bf0", align_bytes=64),
+            after_q.tile([P, PACK, P, PACK], BF16, name="q_bf1", tag="stage", align_bytes=64),
+        ]
         q_codes = [keep.tile([P, PASS], U32, name="q_codes%d" % g, align_bytes=64) for g in range(G)]
         q_scales = [keep.tile([P, PASS], U8, name="q_scales%d" % g, align_bytes=64) for g in range(G)]
         w_bf = [keep.tile([P, N, PACK], BF16, name="w_bf%d" % g, align_bytes=64) for g in range(G)]
         w_codes = [keep.tile([P, HALF + N], U32, name="w_codes%d" % g, align_bytes=64) for g in range(G)]
         w_scales = [keep.tile([P, HALF + N], U8, name="w_scales%d" % g, align_bytes=64) for g in range(G)]
-        d_bf = {0: keep.tile([P, G, P, PACK], BF16, name="d_bf0", align_bytes=64)}
+        d_bf = {}
         d_codes = [keep.tile([P, G, P], U32, name="d_codes%d" % e, align_bytes=64) for e in range(E_TILES)]
         d_scales = [keep.tile([P, G, P], U8, name="d_scales%d" % e, align_bytes=64) for e in range(E_TILES)]
 
@@ -134,16 +139,21 @@ def tile_attend_gat_v_kernel(tc, qT, kT, rw, dom, offs, out):
             )
 
         def cast_d(e, g, engine):
+            if e == 0 and e not in d_bf:
+                d_bf.setdefault(e, after_q.tile([P, G, P, PACK], BF16, name="d_bf0", tag="stage", align_bytes=64))
             if e == 2 and e not in d_bf:
                 d_bf.setdefault(e, final.tile([P, G, P, PACK], BF16, name="d_bf2", align_bytes=64, offset=4 * HALF))
             if e not in d_bf:
                 d_bf.setdefault(e, late1.tile([P, G, P, PACK], BF16, name="d_late", tag="stage", align_bytes=64))
             src = {0: d_first[g][:], 1: d_mid[g][:, :, :P], 2: d_mid[g][:, :, P:], 3: d_last[g][:]}[e]
-            cast(
-                engine,
-                d_bf[e][:, g].rearrange("p (c i) j -> p c j i", i=PACK),
-                src.rearrange("p j (c i) -> p c j i", i=PACK),
-            )
+            if engine == "G":
+                cast(engine, d_bf[e][:, g], src.rearrange("p j e -> p e j"))
+            else:
+                cast(
+                    engine,
+                    d_bf[e][:, g].rearrange("p (c i) j -> p c j i", i=PACK),
+                    src.rearrange("p j (c i) -> p c j i", i=PACK),
+                )
 
         def quant_d(e):
             nc.vector.quantize_mx(
@@ -230,12 +240,13 @@ def tile_attend_gat_v_kernel(tc, qT, kT, rw, dom, offs, out):
         quant_k(0, HALF)
         cast_q(q_mid, PASS, PASS, PASS + Q_PIECE // 2, "S")
         cast_q(q_mid, PASS, PASS + Q_PIECE // 2, PASS + Q_PIECE, "S")
-        cast_q(q_tail, PASS + Q_PIECE, PASS + Q_PIECE, R, "V")
+        cast_q(q_tail, PASS + Q_PIECE, PASS + Q_PIECE, R - Q_SHARE, "V")
+        cast_q(q_tail, PASS + Q_PIECE, R - Q_SHARE, R, "S")
         quant_q(1)
         weights(0, 2, stage)
         weights(0, 3, stage)
         weights(0, 0, stage)
-        cast_d(0, 0, "V")
+        cast_d(0, 0, "G")
         weights(1, 2, stage)
         quant_w(0, HALF, N)
         cast_d(0, 1, "S")

@@ -25,7 +25,7 @@ E_TILES = DV // P
 CH = 128
 HALF = N // 2
 Q_PIECE = 256
-Q_SHARE = 96
+Q_SHARE = 48
 WINDOWS = 3
 
 

@@ -24,8 +24,8 @@ G = R // PASS
 E_TILES = DV // P
 CH = 128
 HALF = N // 2
-Q_PIECE = 256
-Q_SHARE = 48
+Q_PIECES = ((0, 256), (256, 512), (512, 768), (768, 896), (896, 1024))
+Q_SHARE = 96
 WINDOWS = 3
 
 
@@ -42,12 +42,10 @@ def tile_attend_gat_v_kernel(tc, qT, kT, rw, dom, offs, out):
 
     with ExitStack() as ctx:
         keep = ctx.enter_context(tc.tile_pool(name="keep", bufs=1))
-        after_q = ctx.enter_context(tc.tile_pool(name="after_q", bufs=1))
-        late1 = ctx.enter_context(tc.tile_pool(name="late1", bufs=1))
-        mid_pool = ctx.enter_context(tc.tile_pool(name="mid_pool", bufs=1))
-        last_pool = ctx.enter_context(tc.tile_pool(name="last_pool", bufs=1))
         stage = ctx.enter_context(tc.tile_pool(name="stage", bufs=3))
-        final = ctx.enter_context(tc.tile_pool(name="final", bufs=1))
+        after_quant = ctx.enter_context(tc.tile_pool(name="after_quant", bufs=1))
+        after_q = ctx.enter_context(tc.tile_pool(name="after_q", bufs=1))
+        dense_pool = ctx.enter_context(tc.tile_pool(name="dense_pool", bufs=2))
         spsum = ctx.enter_context(tc.psum_pool(name="spsum", bufs=6))
         opsum = ctx.enter_context(tc.psum_pool(name="opsum", bufs=2))
 
@@ -55,36 +53,29 @@ def tile_attend_gat_v_kernel(tc, qT, kT, rw, dom, offs, out):
         k_planes = [keep.tile([P, T], F32, name="k_plane%d" % j) for j in range(PACK)]
         k_rows = kT.rearrange("(p j) c -> p j c", j=PACK)
         q_rows = qT[0].rearrange("(p j) r -> p j r", j=PACK)
-        q_head = keep.tile([P, PACK, PASS], F32, name="q_head")
-        q_mid = keep.tile([P, PACK, Q_PIECE], F32, name="q_mid")
-        q_tail = keep.tile([P, PACK, Q_PIECE], F32, name="q_tail")
+        q_raw = [keep.tile([P, PACK, hi - lo], F32, name="q_raw%d" % lo) for lo, hi in Q_PIECES[:-1]]
+        q_raw.append(after_q.tile([P, PACK, R - Q_PIECES[-1][0]], F32, name="q_last", tag="shared", align_bytes=64))
 
         gate = keep.tile([P, G, 2 * PACK], F32, name="gate")
         d_rows = dom[0].rearrange("(g p j) e -> g p j e", p=P, j=PACK)
-        d_first = [keep.tile([P, PACK, P], F32, name="d_first%d" % g) for g in range(G)]
-        d_mid = [
-            keep.tile([P, PACK, 2 * P], F32, name="d_mid0"),
-            mid_pool.tile([P, PACK, 2 * P], F32, name="d_mid1", tag="stage", align_bytes=64),
-        ]
-        d_last = [
-            keep.tile([P, PACK, P], F32, name="d_last0"),
-            last_pool.tile([P, PACK, P], F32, name="d_last1", tag="stage", align_bytes=64),
-        ]
+        d_first = keep.tile([P, G, PACK, P], F32, name="d_first")
+        d_second = [keep.tile([P, PACK, P], F32, name="d_second%d" % g) for g in range(G)]
+        d_rest = [keep.tile([P, PACK, 2 * P], F32, name="d_rest%d" % g) for g in range(G)]
         windows = [keep.tile([P, T], F32, name="window%d" % e) for e in range(WINDOWS)]
 
-        nc.scalar.dma_start(out=q_head[:], in_=q_rows[:, :, :PASS])
+        nc.sync.dma_start(out=k_planes[0][:], in_=k_rows[:, 0, :])
         nc.sync.dma_start(offsets[:], offs)
-        for j in range(PACK):
+        for j in range(1, PACK):
             nc.sync.dma_start(out=k_planes[j][:], in_=k_rows[:, j, :])
-        nc.sync.dma_start(out=q_mid[:], in_=q_rows[:, :, PASS : PASS + Q_PIECE])
-        nc.sync.dma_start(out=q_tail[:], in_=q_rows[:, :, PASS + Q_PIECE :])
-        nc.sync.dma_start(out=gate[:, :, :PACK], in_=rw[0].rearrange("(g p t) o -> p g (t o)", p=P, t=PACK))
+        nc.scalar.dma_start(out=gate[:, :, :PACK], in_=rw[0].rearrange("(g p t) o -> p g (t o)", p=P, t=PACK))
+        for raw, (lo, hi) in zip(q_raw, Q_PIECES):
+            nc.sync.dma_start(out=raw[:], in_=q_rows[:, :, lo:hi])
         for g in range(G):
-            nc.sync.dma_start(out=d_first[g][:], in_=d_rows[g, :, :, 0:P])
+            nc.sync.dma_start(out=d_first[:, g], in_=d_rows[g, :, :, 0:P])
         for g in range(G):
-            nc.sync.dma_start(out=d_mid[g][:], in_=d_rows[g, :, :, P : 3 * P])
+            nc.sync.dma_start(out=d_second[g][:], in_=d_rows[g, :, :, P : 2 * P])
         for g in range(G):
-            nc.sync.dma_start(out=d_last[g][:], in_=d_rows[g, :, :, 3 * P : DV])
+            nc.sync.dma_start(out=d_rest[g][:], in_=d_rows[g, :, :, 2 * P : DV])
 
         for window in windows:
             nc.vector.memset(window[:], 0.0)
@@ -95,11 +86,11 @@ def tile_attend_gat_v_kernel(tc, qT, kT, rw, dom, offs, out):
         k_scales = keep.tile([P, N], U8, name="k_scales", align_bytes=64)
         q_bf = [
             keep.tile([P, PACK, P, PACK], BF16, name="q_bf0", align_bytes=64),
-            after_q.tile([P, PACK, P, PACK], BF16, name="q_bf1", tag="stage", align_bytes=64),
+            after_quant.tile([P, PACK, P, PACK], BF16, name="q_bf1", tag="stage", align_bytes=64),
         ]
         q_codes = [keep.tile([P, PASS], U32, name="q_codes%d" % g, align_bytes=64) for g in range(G)]
         q_scales = [keep.tile([P, PASS], U8, name="q_scales%d" % g, align_bytes=64) for g in range(G)]
-        w_bf = [keep.tile([P, N, PACK], BF16, name="w_bf%d" % g, align_bytes=64) for g in range(G)]
+        w_bf = {}
         w_codes = [keep.tile([P, HALF + N], U32, name="w_codes%d" % g, align_bytes=64) for g in range(G)]
         w_scales = [keep.tile([P, HALF + N], U8, name="w_scales%d" % g, align_bytes=64) for g in range(G)]
         d_bf = {}
@@ -125,27 +116,25 @@ def tile_attend_gat_v_kernel(tc, qT, kT, rw, dom, offs, out):
                 in_=k_bf[:, lo:hi, :].rearrange("p n j -> p (n j)"),
             )
 
-        def cast_q(raw, first, lo, hi, engine):
+        def cast_q(lo, hi, engine, ts=slice(0, PACK)):
             g = lo // PASS
+            raw, first = [(raw, a) for raw, (a, b) in zip(q_raw, Q_PIECES) if a <= lo < b][0]
             ms = slice((lo - g * PASS) // PACK, (hi - g * PASS) // PACK)
             src = raw[:, :, lo - first : hi - first].rearrange("p j (m t) -> p m j t", t=PACK)
-            cast(engine, q_bf[g][:].rearrange("p t m j -> p m j t")[:, ms], src)
+            cast(engine, q_bf[g][:].rearrange("p t m j -> p m j t")[:, ms, :, ts], src[:, :, :, ts])
 
-        def quant_q(g):
-            nc.vector.quantize_mx(
-                out=q_codes[g][:].bitcast(E4),
-                scales=q_scales[g][:],
-                in_=q_bf[g][:].rearrange("p t m j -> p (t m j)"),
-            )
+        def quant_q(g, lo, hi):
+            for t in range(PACK):
+                nc.vector.quantize_mx(
+                    out=q_codes[g][:, t * P + lo : t * P + hi].bitcast(E4),
+                    scales=q_scales[g][:, t * P + lo : t * P + hi],
+                    in_=q_bf[g][:, t, lo:hi, :].rearrange("p m j -> p (m j)"),
+                )
 
         def cast_d(e, g, engine):
-            if e == 0 and e not in d_bf:
-                d_bf.setdefault(e, after_q.tile([P, G, P, PACK], BF16, name="d_bf0", tag="stage", align_bytes=64))
-            if e == 2 and e not in d_bf:
-                d_bf.setdefault(e, final.tile([P, G, P, PACK], BF16, name="d_bf2", align_bytes=64, offset=4 * HALF))
             if e not in d_bf:
-                d_bf.setdefault(e, late1.tile([P, G, P, PACK], BF16, name="d_late", tag="stage", align_bytes=64))
-            src = {0: d_first[g][:], 1: d_mid[g][:, :, :P], 2: d_mid[g][:, :, P:], 3: d_last[g][:]}[e]
+                d_bf.setdefault(e, keep.tile([P, G, P, PACK], BF16, name="d_bf%d" % e, align_bytes=64))
+            src = {0: d_first[:, g], 1: d_second[g][:], 2: d_rest[g][:, :, :P], 3: d_rest[g][:, :, P:]}[e]
             if engine == "G":
                 cast(engine, d_bf[e][:, g], src.rearrange("p j e -> p e j"))
             else:
@@ -155,6 +144,10 @@ def tile_attend_gat_v_kernel(tc, qT, kT, rw, dom, offs, out):
                     src.rearrange("p j (c i) -> p c j i", i=PACK),
                 )
 
+        def cast_d_first():
+            d_bf.setdefault(0, after_quant.tile([P, G, P, PACK], BF16, name="d_bf0", tag="stage", align_bytes=64))
+            cast("G", d_bf[0][:], d_first[:].rearrange("p g j e -> p g e j"))
+
         def quant_d(e):
             nc.vector.quantize_mx(
                 out=d_codes[e][:].rearrange("p g e -> p (g e)").bitcast(E5),
@@ -162,10 +155,10 @@ def tile_attend_gat_v_kernel(tc, qT, kT, rw, dom, offs, out):
                 in_=d_bf[e][:].rearrange("p g e j -> p (g e j)"),
             )
 
-        def weights(g, c, pool):
+        def weights(g, c, pool, first_t=0):
             cols = slice(c * CH, (c + 1) * CH)
             bank = spsum.tile([P, PACK, CH], F32, name="scores")
-            for t in range(PACK):
+            for t in [(first_t + i) % PACK for i in range(PACK)]:
                 nc.tensor.matmul_mx(
                     out=bank[:, t, :],
                     lhsT=q_codes[g][:, t * P : (t + 1) * P].bitcast(E4),
@@ -175,12 +168,14 @@ def tile_attend_gat_v_kernel(tc, qT, kT, rw, dom, offs, out):
                     start=True,
                     stop=True,
                 )
-            if pool is final:
-                gated = pool.tile([P, PACK, CH + 1], F32, name="gated_last", align_bytes=64, offset=0)
-            else:
-                gated = pool.tile([P, PACK, CH + 1], F32, name="gated", tag="stage", align_bytes=64)
+            gated = pool.tile([P, PACK, CH + 1], F32, name="gated", tag="stage", align_bytes=64)
             for t in range(PACK):
                 nc.scalar.activation(out=gated[:, t, :CH], in_=bank[:, t, :], func=COPY, scale=gate[:, g, t : t + 1])
+            if g not in w_bf:
+                if g == 0:
+                    w_bf.setdefault(g, after_q.tile([P, N, PACK], BF16, name="w_bf0", tag="shared", align_bytes=64))
+                else:
+                    w_bf.setdefault(g, keep.tile([P, N, PACK], BF16, name="w_bf1", align_bytes=64))
             nc.vector.scalar_tensor_tensor(
                 out=w_bf[g][:, cols, :],
                 in0=bank[:].rearrange("p t n -> p n t"),
@@ -211,8 +206,10 @@ def tile_attend_gat_v_kernel(tc, qT, kT, rw, dom, offs, out):
                 )
             return acc
 
-        def new_dense(pool):
-            return pool.tile([P, N], F32, name="dense", tag="stage", align_bytes=64)
+        def leave(acc, width):
+            dense = dense_pool.tile([P, N], F32, name="dense", align_bytes=64)
+            nc.scalar.activation(out=dense[:, :width], in_=acc[:, :width], func=COPY)
+            return dense[:, :width]
 
         def place(e, src, lo, hi):
             nc.vector.tensor_copy(out=windows[e % WINDOWS][:].indirect(offsets[:, lo // 16 : hi // 16]), in_=src)
@@ -225,60 +222,49 @@ def tile_attend_gat_v_kernel(tc, qT, kT, rw, dom, offs, out):
                 nc.sync.dma_start(out=rows[:, : T // 2], in_=windows[e % WINDOWS][:, : T // 2])
                 nc.scalar.dma_start(out=rows[:, T // 2 :], in_=windows[e % WINDOWS][:, T // 2 :])
 
-        cast_q(q_head, 0, 0, PASS, "S")
         for j in range(PACK - 1):
             gather(j, 0, N)
-        quant_q(0)
         cast_k(0, 0, N, "S")
         gather(PACK - 1, HALF, N)
         gather(PACK - 1, 0, HALF)
-        cast_k(2, HALF, HALF + CH, "V")
-        cast_k(2, HALF + CH, N, "S")
+        cast_k(2, HALF, N, "V")
         cast_k(2, 0, HALF, "V")
-        quant_k(HALF, HALF + CH)
-        quant_k(HALF + CH, N)
+        quant_k(HALF, N)
         quant_k(0, HALF)
-        cast_q(q_mid, PASS, PASS, PASS + Q_PIECE // 2, "S")
-        cast_q(q_mid, PASS, PASS + Q_PIECE // 2, PASS + Q_PIECE, "S")
-        cast_q(q_tail, PASS + Q_PIECE, PASS + Q_PIECE, R - Q_SHARE, "V")
-        cast_q(q_tail, PASS + Q_PIECE, R - Q_SHARE, R, "S")
-        quant_q(1)
+        cast_q(0, 256, "S")
+        cast_q(256, PASS - Q_SHARE, "V")
+        cast_q(PASS - Q_SHARE, PASS, "S")
+        quant_q(0, 0, P)
+        cast_q(512, 768, "S")
+        cast_q(768, 896, "V")
+        cast_q(896, R, "V", slice(0, 2))
+        cast_q(896, R, "V", slice(2, PACK))
+        quant_q(1, 0, P)
         weights(0, 2, stage)
-        weights(0, 3, stage)
-        weights(0, 0, stage)
-        cast_d(0, 0, "G")
-        weights(1, 2, stage)
+        cast_d_first()
+        weights(0, 3, stage, PACK - 1)
+        weights(0, 0, stage, PACK - 1)
         quant_w(0, HALF, N)
-        cast_d(0, 1, "S")
-        weights(1, 3, stage)
-        quant_d(0)
-        weights(0, 1, late1)
+        weights(1, 2, stage)
+        weights(1, 3, stage, PACK - 1)
+        weights(0, 1, stage, PACK - 1)
         quant_w(1, HALF, N)
-        weights(1, 0, stage)
+        quant_d(0)
+        weights(1, 0, stage, PACK - 1)
+        weights(1, 1, stage, PACK - 1)
         quant_w(0, 0, HALF)
-        weights(1, 1, final)
-        acc_a = product(0, HALF)
-        for g in range(G):
-            cast_d(1, g, "S")
         quant_w(1, 0, HALF)
-        quant_d(1)
-        dense_a = final.tile([P, HALF], F32, name="dense_a", align_bytes=64, offset=0)
-        nc.scalar.activation(out=dense_a[:], in_=acc_a[:, :HALF], func=COPY)
+        place(0, leave(product(0, HALF), HALF), HALF, N)
         acc = product(0, 0)
         for g in range(G):
-            cast_d(2, g, "S")
-        dense_b = new_dense(mid_pool)
-        nc.scalar.activation(out=dense_b[:, :HALF], in_=acc[:, :HALF], func=COPY)
-        place(0, dense_a[:], HALF, N)
-        quant_d(2)
-        place(0, dense_b[:, :HALF], 0, HALF)
+            cast_d(1, g, "S")
+        quant_d(1)
+        place(0, leave(acc, HALF), 0, HALF)
         store(0)
-        for g in range(G):
-            cast_d(3, g, "S")
-        quant_d(3)
+        for e in (2, 3):
+            for g in range(G):
+                cast_d(e, g, "S")
+            quant_d(e)
         for e in range(1, E_TILES):
-            acc = product(e, 0)
-            dense = new_dense(last_pool if e == 1 else stage)
-            nc.scalar.activation(out=dense[:], in_=acc[:], func=COPY)
-            place(e, dense[:], 0, N)
+            place(e, leave(product(e, 0), N), 0, N)
             store(e)

@@ -24,7 +24,7 @@ G = R // PASS
 E_TILES = DV // P
 CH = 128
 HALF = N // 2
-Q_PIECES = ((0, 256), (256, 512), (512, 768), (768, 896), (896, 1024))
+Q_PIECES = ((0, 512), (512, 768), (768, 1024))
 Q_SHARE = 96
 WINDOWS = 3
 
@@ -58,9 +58,8 @@ def tile_attend_gat_v_kernel(tc, qT, kT, rw, dom, offs, out):
 
         gate = keep.tile([P, G, 2 * PACK], F32, name="gate")
         d_rows = dom[0].rearrange("(g p j) e -> g p j e", p=P, j=PACK)
-        d_first = keep.tile([P, G, PACK, P], F32, name="d_first")
-        d_second = [keep.tile([P, PACK, P], F32, name="d_second%d" % g) for g in range(G)]
-        d_rest = [keep.tile([P, PACK, 2 * P], F32, name="d_rest%d" % g) for g in range(G)]
+        d_first = [keep.tile([P, PACK, P], F32, name="d_first%d" % g) for g in range(G)]
+        d_rest = [keep.tile([P, PACK, DV - P], F32, name="d_rest%d" % g) for g in range(G)]
         windows = [keep.tile([P, T], F32, name="window%d" % e) for e in range(WINDOWS)]
 
         nc.sync.dma_start(out=k_planes[0][:], in_=k_rows[:, 0, :])
@@ -71,11 +70,9 @@ def tile_attend_gat_v_kernel(tc, qT, kT, rw, dom, offs, out):
         for raw, (lo, hi) in zip(q_raw, Q_PIECES):
             nc.sync.dma_start(out=raw[:], in_=q_rows[:, :, lo:hi])
         for g in range(G):
-            nc.sync.dma_start(out=d_first[:, g], in_=d_rows[g, :, :, 0:P])
+            nc.sync.dma_start(out=d_first[g][:], in_=d_rows[g, :, :, 0:P])
         for g in range(G):
-            nc.sync.dma_start(out=d_second[g][:], in_=d_rows[g, :, :, P : 2 * P])
-        for g in range(G):
-            nc.sync.dma_start(out=d_rest[g][:], in_=d_rows[g, :, :, 2 * P : DV])
+            nc.sync.dma_start(out=d_rest[g][:], in_=d_rows[g, :, :, P:DV])
 
         for window in windows:
             nc.vector.memset(window[:], 0.0)
@@ -133,8 +130,10 @@ def tile_attend_gat_v_kernel(tc, qT, kT, rw, dom, offs, out):
 
         def cast_d(e, g, engine):
             if e not in d_bf:
-                d_bf.setdefault(e, keep.tile([P, G, P, PACK], BF16, name="d_bf%d" % e, align_bytes=64))
-            src = {0: d_first[:, g], 1: d_second[g][:], 2: d_rest[g][:, :, :P], 3: d_rest[g][:, :, P:]}[e]
+                pool = after_quant if e == 0 else keep
+                tag = "stage" if e == 0 else "d_bf%d" % e
+                d_bf.setdefault(e, pool.tile([P, G, P, PACK], BF16, name="d_bf%d" % e, tag=tag, align_bytes=64))
+            src = d_first[g][:] if e == 0 else d_rest[g][:, :, (e - 1) * P : e * P]
             if engine == "G":
                 cast(engine, d_bf[e][:, g], src.rearrange("p j e -> p e j"))
             else:
@@ -143,10 +142,6 @@ def tile_attend_gat_v_kernel(tc, qT, kT, rw, dom, offs, out):
                     d_bf[e][:, g].rearrange("p (c i) j -> p c j i", i=PACK),
                     src.rearrange("p j (c i) -> p c j i", i=PACK),
                 )
-
-        def cast_d_first():
-            d_bf.setdefault(0, after_quant.tile([P, G, P, PACK], BF16, name="d_bf0", tag="stage", align_bytes=64))
-            cast("G", d_bf[0][:], d_first[:].rearrange("p g j e -> p g e j"))
 
         def quant_d(e):
             nc.vector.quantize_mx(
@@ -231,20 +226,22 @@ def tile_attend_gat_v_kernel(tc, qT, kT, rw, dom, offs, out):
         cast_k(2, 0, HALF, "V")
         quant_k(HALF, N)
         quant_k(0, HALF)
-        cast_q(0, 256, "S")
-        cast_q(256, PASS - Q_SHARE, "V")
-        cast_q(PASS - Q_SHARE, PASS, "S")
+        cast_q(0, PASS, "V", slice(0, 2))
+        cast_q(0, 352, "S", slice(2, PACK))
+        cast_q(352, PASS, "V", slice(2, PACK))
         quant_q(0, 0, P)
-        cast_q(512, 768, "S")
-        cast_q(768, 896, "V")
-        cast_q(896, R, "V", slice(0, 2))
-        cast_q(896, R, "V", slice(2, PACK))
-        quant_q(1, 0, P)
+        cast_q(512, 512 + 160, "S")
+        cast_q(512 + 160, 768, "V")
+        quant_q(1, 0, P // 2)
+        cast_q(768, R, "V", slice(0, 2))
+        cast_q(768, R, "V", slice(2, PACK))
+        quant_q(1, P // 2, P)
         weights(0, 2, stage)
-        cast_d_first()
+        cast_d(0, 0, "G")
         weights(0, 3, stage, PACK - 1)
         weights(0, 0, stage, PACK - 1)
         quant_w(0, HALF, N)
+        cast_d(0, 1, "S")
         weights(1, 2, stage)
         weights(1, 3, stage, PACK - 1)
         weights(0, 1, stage, PACK - 1)

@@ -128,18 +128,19 @@ def tile_attend_gat_v_kernel(tc, qT, kT, rw, dom, offs, out):
                     in_=q_bf[g][:, t, lo:hi, :].rearrange("p m j -> p (m j)"),
                 )
 
-        def cast_d(e, g, engine):
+        def cast_d(e, g, engine, lo=0, hi=P):
             if e not in d_bf:
                 pool = after_quant if e == 0 else keep
                 tag = "stage" if e == 0 else "d_bf%d" % e
                 d_bf.setdefault(e, pool.tile([P, G, P, PACK], BF16, name="d_bf%d" % e, tag=tag, align_bytes=64))
             src = d_first[g][:] if e == 0 else d_rest[g][:, :, (e - 1) * P : e * P]
+            src = src[:, :, lo:hi]
             if engine == "G":
-                cast(engine, d_bf[e][:, g], src.rearrange("p j e -> p e j"))
+                cast(engine, d_bf[e][:, g, lo:hi], src.rearrange("p j e -> p e j"))
             else:
                 cast(
                     engine,
-                    d_bf[e][:, g].rearrange("p (c i) j -> p c j i", i=PACK),
+                    d_bf[e][:, g, lo:hi].rearrange("p (c i) j -> p c j i", i=PACK),
                     src.rearrange("p j (c i) -> p c j i", i=PACK),
                 )
 
@@ -222,7 +223,8 @@ def tile_attend_gat_v_kernel(tc, qT, kT, rw, dom, offs, out):
         cast_k(0, 0, N, "S")
         gather(PACK - 1, HALF, N)
         gather(PACK - 1, 0, HALF)
-        cast_k(2, HALF, N, "V")
+        cast_k(2, HALF, HALF + CH, "S")
+        cast_k(2, HALF + CH, N, "V")
         cast_k(2, 0, HALF, "V")
         quant_k(HALF, N)
         quant_k(0, HALF)
@@ -230,23 +232,25 @@ def tile_attend_gat_v_kernel(tc, qT, kT, rw, dom, offs, out):
         cast_q(0, 352, "S", slice(2, PACK))
         cast_q(352, PASS, "V", slice(2, PACK))
         quant_q(0, 0, P)
-        cast_q(512, 512 + 160, "S")
-        cast_q(512 + 160, 768, "V")
+        cast_q(512, 512 + 128, "S")
+        cast_q(512 + 128, 768, "V", slice(0, 2))
+        cast_q(512 + 128, 768, "V", slice(2, PACK))
         quant_q(1, 0, P // 2)
         cast_q(768, R, "V", slice(0, 2))
-        cast_q(768, R, "V", slice(2, PACK))
+        cast_q(768, R - 0, "V", slice(2, PACK))
         quant_q(1, P // 2, P)
         weights(0, 2, stage)
         cast_d(0, 0, "G")
+        cast_d(0, 1, "G", 0, 64)
         weights(0, 3, stage, PACK - 1)
         weights(0, 0, stage, PACK - 1)
-        quant_w(0, HALF, N)
-        cast_d(0, 1, "S")
+        cast_d(0, 1, "S", 64, P)
         weights(1, 2, stage)
+        quant_w(0, HALF, N)
         weights(1, 3, stage, PACK - 1)
+        quant_d(0)
         weights(0, 1, stage, PACK - 1)
         quant_w(1, HALF, N)
-        quant_d(0)
         weights(1, 0, stage, PACK - 1)
         weights(1, 1, stage, PACK - 1)
         quant_w(0, 0, HALF)

@@ -44,6 +44,7 @@ def tile_attend_gat_v_kernel(tc, qT, kT, rw, dom, offs, out):
         keep = ctx.enter_context(tc.tile_pool(name="keep", bufs=1))
         stage = ctx.enter_context(tc.tile_pool(name="stage", bufs=3))
         after_quant = ctx.enter_context(tc.tile_pool(name="after_quant", bufs=1))
+        after_upper = ctx.enter_context(tc.tile_pool(name="after_upper", bufs=1))
         after_q = ctx.enter_context(tc.tile_pool(name="after_q", bufs=1))
         dense_pool = ctx.enter_context(tc.tile_pool(name="dense_pool", bufs=2))
         spsum = ctx.enter_context(tc.psum_pool(name="spsum", bufs=6))
@@ -130,8 +131,8 @@ def tile_attend_gat_v_kernel(tc, qT, kT, rw, dom, offs, out):
 
         def cast_d(e, g, engine, lo=0, hi=P):
             if e not in d_bf:
-                pool = after_quant if e == 0 else keep
-                tag = "stage" if e == 0 else "d_bf%d" % e
+                pool = {0: after_quant, 3: after_upper}.get(e, keep)
+                tag = "stage" if e in (0, 3) else "d_bf%d" % e
                 d_bf.setdefault(e, pool.tile([P, G, P, PACK], BF16, name="d_bf%d" % e, tag=tag, align_bytes=64))
             src = d_first[g][:] if e == 0 else d_rest[g][:, :, (e - 1) * P : e * P]
             src = src[:, :, lo:hi]
@@ -144,11 +145,11 @@ def tile_attend_gat_v_kernel(tc, qT, kT, rw, dom, offs, out):
                     src.rearrange("p j (c i) -> p c j i", i=PACK),
                 )
 
-        def quant_d(e):
+        def quant_d(e, groups=slice(0, G)):
             nc.vector.quantize_mx(
-                out=d_codes[e][:].rearrange("p g e -> p (g e)").bitcast(E5),
-                scales=d_scales[e][:].rearrange("p g e -> p (g e)"),
-                in_=d_bf[e][:].rearrange("p g e j -> p (g e j)"),
+                out=d_codes[e][:, groups].rearrange("p g e -> p (g e)").bitcast(E5),
+                scales=d_scales[e][:, groups].rearrange("p g e -> p (g e)"),
+                in_=d_bf[e][:, groups].rearrange("p g e j -> p (g e j)"),
             )
 
         def weights(g, c, pool, first_t=0):
@@ -202,8 +203,8 @@ def tile_attend_gat_v_kernel(tc, qT, kT, rw, dom, offs, out):
                 )
             return acc
 
-        def leave(acc, width):
-            dense = dense_pool.tile([P, N], F32, name="dense", align_bytes=64)
+        def leave(acc, width, pool=dense_pool):
+            dense = pool.tile([P, N], F32, name="dense", tag="stage", align_bytes=64)
             nc.scalar.activation(out=dense[:, :width], in_=acc[:, :width], func=COPY)
             return dense[:, :width]
 
@@ -249,18 +250,20 @@ def tile_attend_gat_v_kernel(tc, qT, kT, rw, dom, offs, out):
         quant_w(0, HALF, N)
         weights(1, 3, stage, PACK - 1)
         quant_d(0)
-        weights(0, 1, stage, PACK - 1)
         quant_w(1, HALF, N)
+        weights(0, 1, stage, PACK - 1)
         weights(1, 0, stage, PACK - 1)
         weights(1, 1, stage, PACK - 1)
         quant_w(0, 0, HALF)
         quant_w(1, 0, HALF)
-        place(0, leave(product(0, HALF), HALF), HALF, N)
-        acc = product(0, 0)
-        for g in range(G):
-            cast_d(1, g, "S")
-        quant_d(1)
-        place(0, leave(acc, HALF), 0, HALF)
+        upper = product(0, HALF)
+        lower = product(0, 0)
+        cast_d(1, 0, "S")
+        quant_d(1, slice(0, 1))
+        place(0, leave(upper, HALF, after_upper), HALF, N)
+        cast_d(1, 1, "S")
+        quant_d(1, slice(1, 2))
+        place(0, leave(lower, HALF), 0, HALF)
         store(0)
         for e in (2, 3):
             for g in range(G):

@@ -13,6 +13,7 @@ U8 = mybir.dt.uint8
 E4 = mybir.dt.float8_e4m3fn_x4
 E5 = mybir.dt.float8_e5m2_x4
 COPY = mybir.ActivationFunctionType.Copy
+RELU = mybir.ActivationFunctionType.Relu
 MULT = mybir.AluOpType.mult
 ADD = mybir.AluOpType.add
 MAX = mybir.AluOpType.max
@@ -43,8 +44,8 @@ def tile_attend_gat_v_kernel(tc, qT, kT, rw, dom, offs, out):
     with ExitStack() as ctx:
         keep = ctx.enter_context(tc.tile_pool(name="keep", bufs=1))
         stage = ctx.enter_context(tc.tile_pool(name="stage", bufs=3))
-        after_quant = ctx.enter_context(tc.tile_pool(name="after_quant", bufs=1))
-        after_upper = ctx.enter_context(tc.tile_pool(name="after_upper", bufs=1))
+        after_pool = ctx.enter_context(tc.tile_pool(name="after_pool", bufs=1))
+        after_cast = ctx.enter_context(tc.tile_pool(name="after_cast", bufs=1))
         after_q = ctx.enter_context(tc.tile_pool(name="after_q", bufs=1))
         dense_pool = ctx.enter_context(tc.tile_pool(name="dense_pool", bufs=2))
         spsum = ctx.enter_context(tc.psum_pool(name="spsum", bufs=6))
@@ -59,8 +60,9 @@ def tile_attend_gat_v_kernel(tc, qT, kT, rw, dom, offs, out):
 
         gate = keep.tile([P, G, 2 * PACK], F32, name="gate")
         d_rows = dom[0].rearrange("(g p j) e -> g p j e", p=P, j=PACK)
-        d_first = [keep.tile([P, PACK, P], F32, name="d_first%d" % g) for g in range(G)]
-        d_rest = [keep.tile([P, PACK, DV - P], F32, name="d_rest%d" % g) for g in range(G)]
+        d_first = after_cast.tile([P, G, PACK, P], F32, name="d_first", tag="shared", align_bytes=64)
+        d_second = [keep.tile([P, PACK, P], F32, name="d_second%d" % g) for g in range(G)]
+        d_rest = [keep.tile([P, PACK, DV - 2 * P], F32, name="d_rest%d" % g) for g in range(G)]
         windows = [keep.tile([P, T], F32, name="window%d" % e) for e in range(WINDOWS)]
 
         nc.sync.dma_start(out=k_planes[0][:], in_=k_rows[:, 0, :])
@@ -70,10 +72,12 @@ def tile_attend_gat_v_kernel(tc, qT, kT, rw, dom, offs, out):
         nc.scalar.dma_start(out=gate[:, :, :PACK], in_=rw[0].rearrange("(g p t) o -> p g (t o)", p=P, t=PACK))
         for raw, (lo, hi) in zip(q_raw, Q_PIECES):
             nc.sync.dma_start(out=raw[:], in_=q_rows[:, :, lo:hi])
+        nc.sync.dma_start(out=d_second[0][:], in_=d_rows[0, :, :, P : 2 * P])
         for g in range(G):
-            nc.sync.dma_start(out=d_first[g][:], in_=d_rows[g, :, :, 0:P])
+            nc.sync.dma_start(out=d_first[:, g], in_=d_rows[g, :, :, 0:P])
+        nc.sync.dma_start(out=d_second[1][:], in_=d_rows[1, :, :, P : 2 * P])
         for g in range(G):
-            nc.sync.dma_start(out=d_rest[g][:], in_=d_rows[g, :, :, P:DV])
+            nc.sync.dma_start(out=d_rest[g][:], in_=d_rows[g, :, :, 2 * P : DV])
 
         for window in windows:
             nc.vector.memset(window[:], 0.0)
@@ -82,22 +86,27 @@ def tile_attend_gat_v_kernel(tc, qT, kT, rw, dom, offs, out):
         k_dense = keep.tile([P, PACK, N], F32, name="k_dense")
         k_codes = keep.tile([P, N], U32, name="k_codes", align_bytes=64)
         k_scales = keep.tile([P, N], U8, name="k_scales", align_bytes=64)
-        q_bf = [
-            keep.tile([P, PACK, P, PACK], BF16, name="q_bf0", align_bytes=64),
-            after_quant.tile([P, PACK, P, PACK], BF16, name="q_bf1", tag="stage", align_bytes=64),
-        ]
+        q_bf0 = keep.tile([P, PACK * PASS], BF16, name="q_bf0", align_bytes=64)
+        q_then_d = keep.tile([P, (PACK + 3) * PASS], BF16, name="q_then_d", align_bytes=64)
+        q_bf = [t[:, : PACK * PASS].rearrange("p (t m j) -> p t m j", t=PACK, j=PACK) for t in (q_bf0, q_then_d)]
         q_codes = [keep.tile([P, PASS], U32, name="q_codes%d" % g, align_bytes=64) for g in range(G)]
         q_scales = [keep.tile([P, PASS], U8, name="q_scales%d" % g, align_bytes=64) for g in range(G)]
         w_bf = {}
         w_codes = [keep.tile([P, HALF + N], U32, name="w_codes%d" % g, align_bytes=64) for g in range(G)]
-        w_scales = [keep.tile([P, HALF + N], U8, name="w_scales%d" % g, align_bytes=64) for g in range(G)]
-        d_bf = {}
+        w_scales = {1: keep.tile([P, HALF + N], U8, name="w_scales1", align_bytes=64)}
+        d_bf = {(1, g): q_then_d[:, (PACK - 1 + g) * PASS : (PACK + g) * PASS] for g in range(G)}
+        d_bf0 = keep.tile([P, G * PASS], BF16, name="d_bf0", align_bytes=64)
+        d_late = keep.tile([P, 2 * G * PASS], BF16, name="d_late", align_bytes=64)
+        for e in range(2, E_TILES):
+            for g in range(G):
+                first = ((e - 2) * G + g) * PASS
+                d_bf.setdefault((e, g), d_late[:, first : first + PASS])
         d_codes = [keep.tile([P, G, P], U32, name="d_codes%d" % e, align_bytes=64) for e in range(E_TILES)]
         d_scales = [keep.tile([P, G, P], U8, name="d_scales%d" % e, align_bytes=64) for e in range(E_TILES)]
 
         for g in range(G):
             nc.vector.memset(w_codes[g][:, N:], 0)
-            nc.vector.memset(w_scales[g][:, N:].bitcast(U32), 0)
+        nc.vector.memset(w_scales[1][:, N:].bitcast(U32), 0)
 
         def gather(j, lo, hi):
             nc.vector.tensor_copy(
@@ -119,7 +128,7 @@ def tile_attend_gat_v_kernel(tc, qT, kT, rw, dom, offs, out):
             raw, first = [(raw, a) for raw, (a, b) in zip(q_raw, Q_PIECES) if a <= lo < b][0]
             ms = slice((lo - g * PASS) // PACK, (hi - g * PASS) // PACK)
             src = raw[:, :, lo - first : hi - first].rearrange("p j (m t) -> p m j t", t=PACK)
-            cast(engine, q_bf[g][:].rearrange("p t m j -> p m j t")[:, ms, :, ts], src[:, :, :, ts])
+            cast(engine, q_bf[g].rearrange("p t m j -> p m j t")[:, ms, :, ts], src[:, :, :, ts])
 
         def quant_q(g, lo, hi):
             for t in range(PACK):
@@ -129,30 +138,29 @@ def tile_attend_gat_v_kernel(tc, qT, kT, rw, dom, offs, out):
                     in_=q_bf[g][:, t, lo:hi, :].rearrange("p m j -> p (m j)"),
                 )
 
-        def cast_d(e, g, engine, lo=0, hi=P):
-            if e not in d_bf:
-                pool = {0: after_quant, 3: after_upper}.get(e, keep)
-                tag = "stage" if e in (0, 3) else "d_bf%d" % e
-                d_bf.setdefault(e, pool.tile([P, G, P, PACK], BF16, name="d_bf%d" % e, tag=tag, align_bytes=64))
-            src = d_first[g][:] if e == 0 else d_rest[g][:, :, (e - 1) * P : e * P]
-            src = src[:, :, lo:hi]
+        def cast_d(e, g, engine):
+            src = d_second[g][:] if e == 1 else d_rest[g][:, :, (e - 2) * P : (e - 1) * P]
             if engine == "G":
-                cast(engine, d_bf[e][:, g, lo:hi], src.rearrange("p j e -> p e j"))
+                cast(engine, d_bf[e, g].rearrange("p (e j) -> p e j", j=PACK), src.rearrange("p j e -> p e j"))
             else:
                 cast(
                     engine,
-                    d_bf[e][:, g, lo:hi].rearrange("p (c i) j -> p c j i", i=PACK),
+                    d_bf[e, g].rearrange("p (c i j) -> p c j i", i=PACK, j=PACK),
                     src.rearrange("p j (c i) -> p c j i", i=PACK),
                 )
 
-        def quant_d(e, groups=slice(0, G)):
+        def cast_first_d():
+            dst = d_bf0[:].rearrange("p (g e j) -> p g e j", g=G, j=PACK)
+            cast("G", dst, d_first[:].rearrange("p g j e -> p g e j"))
+
+        def quant_d(e, groups, src):
             nc.vector.quantize_mx(
                 out=d_codes[e][:, groups].rearrange("p g e -> p (g e)").bitcast(E5),
                 scales=d_scales[e][:, groups].rearrange("p g e -> p (g e)"),
-                in_=d_bf[e][:, groups].rearrange("p g e j -> p (g e j)"),
+                in_=src,
             )
 
-        def weights(g, c, pool, first_t=0):
+        def gated_scores(g, c, pool, first_t):
             cols = slice(c * CH, (c + 1) * CH)
             bank = spsum.tile([P, PACK, CH], F32, name="scores")
             for t in [(first_t + i) % PACK for i in range(PACK)]:
@@ -168,13 +176,21 @@ def tile_attend_gat_v_kernel(tc, qT, kT, rw, dom, offs, out):
             gated = pool.tile([P, PACK, CH + 1], F32, name="gated", tag="stage", align_bytes=64)
             for t in range(PACK):
                 nc.scalar.activation(out=gated[:, t, :CH], in_=bank[:, t, :], func=COPY, scale=gate[:, g, t : t + 1])
-            if g not in w_bf:
-                if g == 0:
-                    w_bf.setdefault(g, after_q.tile([P, N, PACK], BF16, name="w_bf0", tag="shared", align_bytes=64))
-                else:
-                    w_bf.setdefault(g, keep.tile([P, N, PACK], BF16, name="w_bf1", align_bytes=64))
+            return bank, gated
+
+        def positive_part(bank):
+            positive = after_pool.tile([P, CH, PACK], F32, name="positive", tag="stage0", align_bytes=64)
+            nc.scalar.activation(out=positive[:], in_=bank[:].rearrange("p t n -> p n t"), func=RELU)
+            return positive
+
+        def weights_on_gpsimd(g, c, positive, gated):
+            nc.gpsimd.tensor_tensor(
+                out=w_bf[g, c], in0=positive[:], in1=gated[:, :, :CH].rearrange("p t n -> p n t"), op=MULT
+            )
+
+        def weights(g, c, bank, gated):
             nc.vector.scalar_tensor_tensor(
-                out=w_bf[g][:, cols, :],
+                out=w_bf[g, c],
                 in0=bank[:].rearrange("p t n -> p n t"),
                 scalar=0.0,
                 in1=gated[:, :, :CH].rearrange("p t n -> p n t"),
@@ -182,11 +198,9 @@ def tile_attend_gat_v_kernel(tc, qT, kT, rw, dom, offs, out):
                 op1=MULT,
             )
 
-        def quant_w(g, lo, hi):
+        def quant_w(g, lo, src):
             nc.vector.quantize_mx(
-                out=w_codes[g][:, lo:hi].bitcast(E4),
-                scales=w_scales[g][:, lo:hi],
-                in_=w_bf[g][:, lo:hi, :].rearrange("p n t -> p (n t)"),
+                out=w_codes[g][:, lo : lo + HALF].bitcast(E4), scales=w_scales[g][:, lo : lo + HALF], in_=src
             )
 
         def product(e, first):
@@ -204,7 +218,7 @@ def tile_attend_gat_v_kernel(tc, qT, kT, rw, dom, offs, out):
             return acc
 
         def leave(acc, width, pool=dense_pool):
-            dense = pool.tile([P, N], F32, name="dense", tag="stage", align_bytes=64)
+            dense = pool.tile([P, N], F32, name="dense", tag="stage0", align_bytes=64)
             nc.scalar.activation(out=dense[:, :width], in_=acc[:, :width], func=COPY)
             return dense[:, :width]
 
@@ -240,35 +254,52 @@ def tile_attend_gat_v_kernel(tc, qT, kT, rw, dom, offs, out):
         cast_q(768, R, "V", slice(0, 2))
         cast_q(768, R - 0, "V", slice(2, PACK))
         quant_q(1, P // 2, P)
-        weights(0, 2, stage)
-        cast_d(0, 0, "G")
-        cast_d(0, 1, "G", 0, 64)
-        weights(0, 3, stage, PACK - 1)
-        weights(0, 0, stage, PACK - 1)
-        cast_d(0, 1, "S", 64, P)
-        weights(1, 2, stage)
-        quant_w(0, HALF, N)
-        weights(1, 3, stage, PACK - 1)
-        quant_d(0)
-        quant_w(1, HALF, N)
-        weights(0, 1, stage, PACK - 1)
-        weights(1, 0, stage, PACK - 1)
-        weights(1, 1, stage, PACK - 1)
-        quant_w(0, 0, HALF)
-        quant_w(1, 0, HALF)
-        upper = product(0, HALF)
-        lower = product(0, 0)
-        cast_d(1, 0, "S")
-        quant_d(1, slice(0, 1))
-        place(0, leave(upper, HALF, after_upper), HALF, N)
+        w_upper = [
+            after_q.tile([P, 2 * PASS], BF16, name="w_upper0", tag="shared", align_bytes=64),
+            keep.tile([P, 2 * PASS], BF16, name="w_upper1", align_bytes=64),
+        ]
+        w_lower = [q_then_d[:, (PACK + 1 - g) * PASS : (PACK + 3 - g) * PASS] for g in range(G)]
+        for g in range(G):
+            for c in range(PACK):
+                home = w_lower[g] if c < 2 else w_upper[g]
+                w_bf.setdefault((g, c), home[:, c % 2 * PASS : (c % 2 + 1) * PASS].rearrange("p (n t) -> p n t", t=PACK))
+        both = slice(0, G)
+        cast_d(1, 0, "G")
+        cast_first_d()
+        weights(0, 2, *gated_scores(0, 2, stage, 0))
+        weights(0, 3, *gated_scores(0, 3, stage, PACK - 1))
+        weights(0, 0, *gated_scores(0, 0, stage, PACK - 1))
+        weights(1, 2, *gated_scores(1, 2, stage, 0))
+        weights(1, 3, *gated_scores(1, 3, stage, PACK - 1))
+        w_scales.setdefault(0, after_cast.tile([P, HALF + N], U8, name="w_scales0", tag="shared", align_bytes=64))
+        nc.gpsimd.memset(w_scales[0][:, N:].bitcast(U32), 0)
+        quant_d(0, both, d_bf0[:])
+        quant_w(0, HALF, w_upper[0][:])
+        quant_w(1, HALF, w_upper[1][:])
+        weights(0, 1, *gated_scores(0, 1, stage, PACK - 1))
         cast_d(1, 1, "S")
-        quant_d(1, slice(1, 2))
-        place(0, leave(lower, HALF), 0, HALF)
+        last = gated_scores(1, 0, stage, PACK - 1)
+        side_bank, side_gated = gated_scores(1, 1, keep, PACK - 1)
+        positive = positive_part(side_bank)
+        quant_d(1, both, q_then_d[:, (PACK - 1) * PASS : (PACK + 1) * PASS])
+        quant_w(0, 0, w_lower[0])
+        weights(1, 0, *last)
+        weights_on_gpsimd(1, 1, positive, side_gated)
+        place(0, leave(product(0, HALF), HALF), HALF, N)
+        for g in range(G):
+            cast_d(2, g, "S")
+        quant_d(2, both, d_late[:, : G * PASS])
+        quant_w(1, 0, w_lower[1])
+        place(1, leave(product(1, HALF), HALF, after_pool), HALF, N)
+        lower = [product(e, 0) for e in range(2)]
+        for g in range(G):
+            cast_d(3, g, "S")
+        dense = leave(lower[0], HALF)
+        quant_d(3, both, d_late[:, G * PASS :])
+        place(0, dense, 0, HALF)
         store(0)
-        for e in (2, 3):
-            for g in range(G):
-                cast_d(e, g, "S")
-            quant_d(e)
-        for e in range(1, E_TILES):
+        place(1, leave(lower[1], HALF), 0, HALF)
+        store(1)
+        for e in range(2, E_TILES):
             place(e, leave(product(e, 0), N), 0, N)
             store(e)

@@ -60,8 +60,7 @@ def tile_attend_gat_v_kernel(tc, qT, kT, rw, dom, offs, out):
 
         gate = keep.tile([P, G, 2 * PACK], F32, name="gate")
         d_rows = dom[0].rearrange("(g p j) e -> g p j e", p=P, j=PACK)
-        d_first = after_cast.tile([P, G, PACK, P], F32, name="d_first", tag="shared", align_bytes=64)
-        d_second = [keep.tile([P, PACK, P], F32, name="d_second%d" % g) for g in range(G)]
+        d_first = [keep.tile([P, PACK, 2 * P], F32, name="d_first%d" % g) for g in range(G)]
         d_rest = [keep.tile([P, PACK, DV - 2 * P], F32, name="d_rest%d" % g) for g in range(G)]
         windows = [keep.tile([P, T], F32, name="window%d" % e) for e in range(WINDOWS)]
 
@@ -72,10 +71,8 @@ def tile_attend_gat_v_kernel(tc, qT, kT, rw, dom, offs, out):
         nc.scalar.dma_start(out=gate[:, :, :PACK], in_=rw[0].rearrange("(g p t) o -> p g (t o)", p=P, t=PACK))
         for raw, (lo, hi) in zip(q_raw, Q_PIECES):
             nc.sync.dma_start(out=raw[:], in_=q_rows[:, :, lo:hi])
-        nc.sync.dma_start(out=d_second[0][:], in_=d_rows[0, :, :, P : 2 * P])
         for g in range(G):
-            nc.sync.dma_start(out=d_first[:, g], in_=d_rows[g, :, :, 0:P])
-        nc.sync.dma_start(out=d_second[1][:], in_=d_rows[1, :, :, P : 2 * P])
+            nc.sync.dma_start(out=d_first[g][:], in_=d_rows[g, :, :, : 2 * P])
         for g in range(G):
             nc.sync.dma_start(out=d_rest[g][:], in_=d_rows[g, :, :, 2 * P : DV])
 
@@ -94,13 +91,12 @@ def tile_attend_gat_v_kernel(tc, qT, kT, rw, dom, offs, out):
         w_bf = {}
         w_codes = [keep.tile([P, HALF + N], U32, name="w_codes%d" % g, align_bytes=64) for g in range(G)]
         w_scales = {1: keep.tile([P, HALF + N], U8, name="w_scales1", align_bytes=64)}
-        d_bf = {(1, g): q_then_d[:, (PACK - 1 + g) * PASS : (PACK + g) * PASS] for g in range(G)}
-        d_bf0 = keep.tile([P, G * PASS], BF16, name="d_bf0", align_bytes=64)
-        d_late = keep.tile([P, 2 * G * PASS], BF16, name="d_late", align_bytes=64)
-        for e in range(2, E_TILES):
-            for g in range(G):
-                first = ((e - 2) * G + g) * PASS
-                d_bf.setdefault((e, g), d_late[:, first : first + PASS])
+        d_bf = {
+            (e, g): q_then_d[:, (1 + e * G + g) * PASS : (2 + e * G + g) * PASS] for e in range(2) for g in range(G)
+        }
+        d_third = keep.tile([P, G * PASS], BF16, name="d_third", align_bytes=64)
+        for g in range(G):
+            d_bf.setdefault((2, g), d_third[:, g * PASS : (g + 1) * PASS])
         d_codes = [keep.tile([P, G, P], U32, name="d_codes%d" % e, align_bytes=64) for e in range(E_TILES)]
         d_scales = [keep.tile([P, G, P], U8, name="d_scales%d" % e, align_bytes=64) for e in range(E_TILES)]
 
@@ -139,7 +135,7 @@ def tile_attend_gat_v_kernel(tc, qT, kT, rw, dom, offs, out):
                 )
 
         def cast_d(e, g, engine):
-            src = d_second[g][:] if e == 1 else d_rest[g][:, :, (e - 2) * P : (e - 1) * P]
+            src = (d_first if e < 2 else d_rest)[g][:, :, e % 2 * P : (e % 2 + 1) * P]
             if engine == "G":
                 cast(engine, d_bf[e, g].rearrange("p (e j) -> p e j", j=PACK), src.rearrange("p j e -> p e j"))
             else:
@@ -150,8 +146,8 @@ def tile_attend_gat_v_kernel(tc, qT, kT, rw, dom, offs, out):
                 )
 
         def cast_first_d():
-            dst = d_bf0[:].rearrange("p (g e j) -> p g e j", g=G, j=PACK)
-            cast("G", dst, d_first[:].rearrange("p g j e -> p g e j"))
+            dst = q_then_d[:, PASS : 5 * PASS].rearrange("p (h g e j) -> p h g e j", h=2, g=G, j=PACK)
+            cast("G", dst[:, :, 0], d_first[0][:].rearrange("p j (h e) -> p h e j", h=2))
 
         def quant_d(e, groups, src):
             nc.vector.quantize_mx(
@@ -178,14 +174,12 @@ def tile_attend_gat_v_kernel(tc, qT, kT, rw, dom, offs, out):
                 nc.scalar.activation(out=gated[:, t, :CH], in_=bank[:, t, :], func=COPY, scale=gate[:, g, t : t + 1])
             return bank, gated
 
-        def positive_part(bank):
-            positive = after_pool.tile([P, CH, PACK], F32, name="positive", tag="stage0", align_bytes=64)
-            nc.scalar.activation(out=positive[:], in_=bank[:].rearrange("p t n -> p n t"), func=RELU)
-            return positive
+        def positive_part(positive, bank, cols):
+            nc.scalar.activation(out=positive[:, cols], in_=bank[:, :, cols].rearrange("p t n -> p n t"), func=RELU)
 
-        def weights_on_gpsimd(g, c, positive, gated):
+        def weights_on_gpsimd(g, c, positive, gated, cols):
             nc.gpsimd.tensor_tensor(
-                out=w_bf[g, c], in0=positive[:], in1=gated[:, :, :CH].rearrange("p t n -> p n t"), op=MULT
+                out=w_bf[g, c][:, cols], in0=positive[:, cols], in1=gated[:, :, cols].rearrange("p t n -> p n t"), op=MULT
             )
 
         def weights(g, c, bank, gated):
@@ -247,12 +241,12 @@ def tile_attend_gat_v_kernel(tc, qT, kT, rw, dom, offs, out):
         cast_q(0, 352, "S", slice(2, PACK))
         cast_q(352, PASS, "V", slice(2, PACK))
         quant_q(0, 0, P)
-        cast_q(512, 512 + 128, "S")
-        cast_q(512 + 128, 768, "V", slice(0, 2))
-        cast_q(512 + 128, 768, "V", slice(2, PACK))
+        cast_q(512, 512 + 96, "S")
+        cast_q(512 + 96, 768, "V", slice(0, 2))
+        cast_q(512 + 96, 768, "V", slice(2, PACK))
         quant_q(1, 0, P // 2)
         cast_q(768, R, "V", slice(0, 2))
-        cast_q(768, R - 0, "V", slice(2, PACK))
+        cast_q(768, R, "V", slice(2, PACK))
         quant_q(1, P // 2, P)
         w_upper = [
             after_q.tile([P, 2 * PASS], BF16, name="w_upper0", tag="shared", align_bytes=64),
@@ -264,38 +258,45 @@ def tile_attend_gat_v_kernel(tc, qT, kT, rw, dom, offs, out):
                 home = w_lower[g] if c < 2 else w_upper[g]
                 w_bf.setdefault((g, c), home[:, c % 2 * PASS : (c % 2 + 1) * PASS].rearrange("p (n t) -> p n t", t=PACK))
         both = slice(0, G)
-        cast_d(1, 0, "G")
         cast_first_d()
+        cast_d(0, 1, "G")
         weights(0, 2, *gated_scores(0, 2, stage, 0))
         weights(0, 3, *gated_scores(0, 3, stage, PACK - 1))
         weights(0, 0, *gated_scores(0, 0, stage, PACK - 1))
-        weights(1, 2, *gated_scores(1, 2, stage, 0))
+        weights(1, 2, *gated_scores(1, 2, after_cast, 0))
         weights(1, 3, *gated_scores(1, 3, stage, PACK - 1))
-        w_scales.setdefault(0, after_cast.tile([P, HALF + N], U8, name="w_scales0", tag="shared", align_bytes=64))
+        w_scales.setdefault(0, after_cast.tile([P, HALF + N], U8, name="w_scales0", tag="stage", align_bytes=64))
         nc.gpsimd.memset(w_scales[0][:, N:].bitcast(U32), 0)
-        quant_d(0, both, d_bf0[:])
+        quant_d(0, both, q_then_d[:, PASS : 3 * PASS])
         quant_w(0, HALF, w_upper[0][:])
         quant_w(1, HALF, w_upper[1][:])
         weights(0, 1, *gated_scores(0, 1, stage, PACK - 1))
         cast_d(1, 1, "S")
         last = gated_scores(1, 0, stage, PACK - 1)
         side_bank, side_gated = gated_scores(1, 1, keep, PACK - 1)
-        positive = positive_part(side_bank)
+        positive = after_pool.tile([P, CH, PACK], F32, name="positive", tag="stage0", align_bytes=64)
+        halves = (slice(0, CH // 2), slice(CH // 2, CH))
+        positive_part(positive, side_bank, halves[0])
         quant_d(1, both, q_then_d[:, (PACK - 1) * PASS : (PACK + 1) * PASS])
         quant_w(0, 0, w_lower[0])
         weights(1, 0, *last)
-        weights_on_gpsimd(1, 1, positive, side_gated)
-        place(0, leave(product(0, HALF), HALF), HALF, N)
+        weights_on_gpsimd(1, 1, positive, side_gated, halves[0])
+        dense = leave(product(0, HALF), HALF)
+        positive_part(positive, side_bank, halves[1])
+        weights_on_gpsimd(1, 1, positive, side_gated, halves[1])
+        place(0, dense, HALF, N)
         for g in range(G):
             cast_d(2, g, "S")
-        quant_d(2, both, d_late[:, : G * PASS])
+        quant_d(2, both, d_third[:])
         quant_w(1, 0, w_lower[1])
         place(1, leave(product(1, HALF), HALF, after_pool), HALF, N)
         lower = [product(e, 0) for e in range(2)]
+        d_fourth = keep.tile([P, G * PASS], BF16, name="d_fourth", tag="stage", align_bytes=64)
         for g in range(G):
+            d_bf.setdefault((3, g), d_fourth[:, g * PASS : (g + 1) * PASS])
             cast_d(3, g, "S")
         dense = leave(lower[0], HALF)
-        quant_d(3, both, d_late[:, G * PASS :])
+        quant_d(3, both, d_fourth[:])
         place(0, dense, 0, HALF)
         store(0)
         place(1, leave(lower[1], HALF), 0, HALF)

@@ -14,6 +14,7 @@ E4 = mybir.dt.float8_e4m3fn_x4
 E5 = mybir.dt.float8_e5m2_x4
 COPY = mybir.ActivationFunctionType.Copy
 RELU = mybir.ActivationFunctionType.Relu
+SQUARE = mybir.ActivationFunctionType.Square
 MULT = mybir.AluOpType.mult
 ADD = mybir.AluOpType.add
 MAX = mybir.AluOpType.max
@@ -27,7 +28,8 @@ CH = 128
 HALF = N // 2
 Q_PIECES = ((0, 512), (512, 768), (768, 1024))
 Q_SHARE = 96
-WINDOWS = 3
+WINDOWS = 4
+KEPT = 112
 
 
 def tile_attend_gat_v_kernel(tc, qT, kT, rw, dom, offs, out):
@@ -43,7 +45,7 @@ def tile_attend_gat_v_kernel(tc, qT, kT, rw, dom, offs, out):
 
     with ExitStack() as ctx:
         keep = ctx.enter_context(tc.tile_pool(name="keep", bufs=1))
-        stage = ctx.enter_context(tc.tile_pool(name="stage", bufs=3))
+        stage = ctx.enter_context(tc.tile_pool(name="stage", bufs=5))
         after_pool = ctx.enter_context(tc.tile_pool(name="after_pool", bufs=1))
         after_cast = ctx.enter_context(tc.tile_pool(name="after_cast", bufs=1))
         after_q = ctx.enter_context(tc.tile_pool(name="after_q", bufs=1))
@@ -77,10 +79,12 @@ def tile_attend_gat_v_kernel(tc, qT, kT, rw, dom, offs, out):
             nc.sync.dma_start(out=d_rest[g][:], in_=d_rows[g, :, :, 2 * P : DV])
 
         for window in windows:
-            nc.vector.memset(window[:], 0.0)
+            nc.gpsimd.memset(window[:], 0.0)
+
+        side_gate = keep.tile([P, 1, PACK], F32, name="side_gate")
+        nc.scalar.activation(out=side_gate[:], in_=gate[:, 1:2, :PACK], func=COPY)
 
         k_bf = keep.tile([P, N, PACK], BF16, name="k_bf", align_bytes=64)
-        k_dense = keep.tile([P, PACK, N], F32, name="k_dense")
         k_codes = keep.tile([P, N], U32, name="k_codes", align_bytes=64)
         k_scales = keep.tile([P, N], U8, name="k_scales", align_bytes=64)
         q_bf0 = keep.tile([P, PACK * PASS], BF16, name="q_bf0", align_bytes=64)
@@ -98,19 +102,21 @@ def tile_attend_gat_v_kernel(tc, qT, kT, rw, dom, offs, out):
         for g in range(G):
             d_bf.setdefault((2, g), d_third[:, g * PASS : (g + 1) * PASS])
         d_codes = [keep.tile([P, G, P], U32, name="d_codes%d" % e, align_bytes=64) for e in range(E_TILES)]
-        d_scales = [keep.tile([P, G, P], U8, name="d_scales%d" % e, align_bytes=64) for e in range(E_TILES)]
+        d_scales = {e: keep.tile([P, G, P], U8, name="d_scales%d" % e, align_bytes=64) for e in (1, 3)}
+
+        def d_plane(e, groups):
+            if e == 0:
+                return w_scales[0][:, HALF + N + groups.start * P : HALF + N + groups.stop * P]
+            return d_scales[e][:, groups].rearrange("p g e -> p (g e)")
 
         for g in range(G):
-            nc.vector.memset(w_codes[g][:, N:], 0)
-        nc.vector.memset(w_scales[1][:, N:].bitcast(U32), 0)
+            nc.gpsimd.memset(w_codes[g][:, N:], 0)
+        nc.gpsimd.memset(w_scales[1][:, N:].bitcast(U32), 0)
 
         def gather(j, lo, hi):
             nc.vector.tensor_copy(
-                out=k_dense[:, j, lo:hi], in_=k_planes[j][:].indirect(offsets[:, lo // 16 : hi // 16])
+                out=k_bf[:, lo:hi, j], in_=k_planes[j][:].indirect(offsets[:, lo // 16 : hi // 16])
             )
-
-        def cast_k(j, lo, hi, engine):
-            cast(engine, k_bf[:, lo:hi, j : j + 2], k_dense[:, j : j + 2, lo:hi].rearrange("p j n -> p n j"))
 
         def quant_k(lo, hi):
             nc.vector.quantize_mx(
@@ -152,11 +158,11 @@ def tile_attend_gat_v_kernel(tc, qT, kT, rw, dom, offs, out):
         def quant_d(e, groups, src):
             nc.vector.quantize_mx(
                 out=d_codes[e][:, groups].rearrange("p g e -> p (g e)").bitcast(E5),
-                scales=d_scales[e][:, groups].rearrange("p g e -> p (g e)"),
+                scales=d_plane(e, groups),
                 in_=src,
             )
 
-        def gated_scores(g, c, pool, first_t):
+        def scores(g, c, first_t):
             cols = slice(c * CH, (c + 1) * CH)
             bank = spsum.tile([P, PACK, CH], F32, name="scores")
             for t in [(first_t + i) % PACK for i in range(PACK)]:
@@ -169,25 +175,32 @@ def tile_attend_gat_v_kernel(tc, qT, kT, rw, dom, offs, out):
                     start=True,
                     stop=True,
                 )
-            gated = pool.tile([P, PACK, CH + 1], F32, name="gated", tag="stage", align_bytes=64)
-            for t in range(PACK):
-                nc.scalar.activation(out=gated[:, t, :CH], in_=bank[:, t, :], func=COPY, scale=gate[:, g, t : t + 1])
+            return bank
+
+        def gated_scores(g, c, pool, first_t):
+            return gate_bank(g, scores(g, c, first_t), pool, CH)
+
+        def gate_bank(g, bank, pool, width, ts=range(PACK), gated=None):
+            if gated is None:
+                gated = pool.tile([P, PACK, CH + 1], F32, name="gated", tag="stage", align_bytes=64)
+            for t in ts:
+                nc.scalar.activation(out=gated[:, t, :width], in_=bank[:, t, :width], func=COPY, scale=gate[:, g, t : t + 1])
             return bank, gated
 
-        def positive_part(positive, bank, cols):
-            nc.scalar.activation(out=positive[:, cols], in_=bank[:, :, cols].rearrange("p t n -> p n t"), func=RELU)
-
-        def weights_on_gpsimd(g, c, positive, gated, cols):
+        def weights_on_gpsimd(squares, lo, hi):
             nc.gpsimd.tensor_tensor(
-                out=w_bf[g, c][:, cols], in0=positive[:, cols], in1=gated[:, :, cols].rearrange("p t n -> p n t"), op=MULT
+                out=w_lower[1].rearrange("p (n t) -> p n t", t=PACK)[:, KEPT + lo : KEPT + hi],
+                in0=squares[:, lo:hi],
+                in1=side_gate[:].to_broadcast([P, hi - lo, PACK]),
+                op=MULT,
             )
 
-        def weights(g, c, bank, gated):
+        def weights(g, c, bank, gated, width=CH):
             nc.vector.scalar_tensor_tensor(
-                out=w_bf[g, c],
-                in0=bank[:].rearrange("p t n -> p n t"),
+                out=w_bf[g, c][:, :width],
+                in0=bank[:, :, :width].rearrange("p t n -> p n t"),
                 scalar=0.0,
-                in1=gated[:, :, :CH].rearrange("p t n -> p n t"),
+                in1=gated[:, :, :width].rearrange("p t n -> p n t"),
                 op0=MAX,
                 op1=MULT,
             )
@@ -197,22 +210,23 @@ def tile_attend_gat_v_kernel(tc, qT, kT, rw, dom, offs, out):
                 out=w_codes[g][:, lo : lo + HALF].bitcast(E4), scales=w_scales[g][:, lo : lo + HALF], in_=src
             )
 
-        def product(e, first):
+        def product(e, first, groups=range(G)):
             acc = opsum.tile([P, N], F32, name="acc")
-            for g in range(G):
+            for g in groups:
                 nc.tensor.matmul_mx(
                     out=acc[:],
                     lhsT=d_codes[e][:, g, :].bitcast(E5),
-                    lhsT_scale=d_scales[e][:, g, :],
+                    lhsT_scale=d_plane(e, slice(g, g + 1)),
                     rhs=w_codes[g][:, first : first + N].bitcast(E4),
                     rhs_scale=w_scales[g][:, first : first + N],
-                    start=(g == 0),
-                    stop=(g == G - 1),
+                    start=(g == groups[0]),
+                    stop=(g == groups[-1]),
                 )
             return acc
 
-        def leave(acc, width, pool=dense_pool):
-            dense = pool.tile([P, N], F32, name="dense", tag="stage0", align_bytes=64)
+        def leave(acc, width, dense=None):
+            if dense is None:
+                dense = dense_pool.tile([P, N], F32, name="dense")
             nc.scalar.activation(out=dense[:, :width], in_=acc[:, :width], func=COPY)
             return dense[:, :width]
 
@@ -229,12 +243,8 @@ def tile_attend_gat_v_kernel(tc, qT, kT, rw, dom, offs, out):
 
         for j in range(PACK - 1):
             gather(j, 0, N)
-        cast_k(0, 0, N, "S")
         gather(PACK - 1, HALF, N)
         gather(PACK - 1, 0, HALF)
-        cast_k(2, HALF, HALF + CH, "S")
-        cast_k(2, HALF + CH, N, "V")
-        cast_k(2, 0, HALF, "V")
         quant_k(HALF, N)
         quant_k(0, HALF)
         cast_q(0, PASS, "V", slice(0, 2))
@@ -258,40 +268,49 @@ def tile_attend_gat_v_kernel(tc, qT, kT, rw, dom, offs, out):
                 home = w_lower[g] if c < 2 else w_upper[g]
                 w_bf.setdefault((g, c), home[:, c % 2 * PASS : (c % 2 + 1) * PASS].rearrange("p (n t) -> p n t", t=PACK))
         both = slice(0, G)
+        d_bf.update({(0, 1): w_lower[0][:, PASS:]})
+        side = HALF - KEPT
+        positive = keep.tile([P, side, PACK], F32, name="positive")
+        squares = after_pool.tile([P, side, PACK], F32, name="squares", align_bytes=64, offset=0)
         cast_first_d()
         cast_d(0, 1, "G")
         weights(0, 2, *gated_scores(0, 2, stage, 0))
         weights(0, 3, *gated_scores(0, 3, stage, PACK - 1))
         weights(0, 0, *gated_scores(0, 0, stage, PACK - 1))
+        late = gate_bank(0, scores(0, 1, PACK - 1), stage, CH, range(2))
         weights(1, 2, *gated_scores(1, 2, after_cast, 0))
         weights(1, 3, *gated_scores(1, 3, stage, PACK - 1))
-        w_scales.setdefault(0, after_cast.tile([P, HALF + N], U8, name="w_scales0", tag="stage", align_bytes=64))
-        nc.gpsimd.memset(w_scales[0][:, N:].bitcast(U32), 0)
-        quant_d(0, both, q_then_d[:, PASS : 3 * PASS])
+        w_scales.setdefault(0, after_cast.tile([P, HALF + N + G * P], U8, name="w_scales0", tag="stage", align_bytes=64))
+        nc.gpsimd.memset(w_scales[0][:, N : HALF + N].bitcast(U32), 0)
+        quant_d(0, slice(0, 1), d_bf[0, 0])
         quant_w(0, HALF, w_upper[0][:])
+        quant_d(0, slice(1, 2), d_bf[0, 1])
         quant_w(1, HALF, w_upper[1][:])
-        weights(0, 1, *gated_scores(0, 1, stage, PACK - 1))
+        weights(0, 1, *gate_bank(0, late[0], stage, CH, range(2, PACK), late[1]))
         cast_d(1, 1, "S")
-        last = gated_scores(1, 0, stage, PACK - 1)
-        side_bank, side_gated = gated_scores(1, 1, keep, PACK - 1)
-        positive = after_pool.tile([P, CH, PACK], F32, name="positive", tag="stage0", align_bytes=64)
-        halves = (slice(0, CH // 2), slice(CH // 2, CH))
-        positive_part(positive, side_bank, halves[0])
+        side_bank = scores(1, 1, PACK - 1)
+        nc.scalar.activation(out=positive[:, CH - KEPT :], in_=side_bank[:].rearrange("p t n -> p n t"), func=RELU)
+        shared_bank = scores(1, 0, PACK - 1)
+        nc.scalar.activation(
+            out=positive[:, : CH - KEPT], in_=shared_bank[:, :, KEPT:].rearrange("p t n -> p n t"), func=RELU
+        )
+        last = gate_bank(1, shared_bank, stage, KEPT)
+        nc.scalar.activation(out=squares[:], in_=positive[:], func=SQUARE)
         quant_d(1, both, q_then_d[:, (PACK - 1) * PASS : (PACK + 1) * PASS])
         quant_w(0, 0, w_lower[0])
-        weights(1, 0, *last)
-        weights_on_gpsimd(1, 1, positive, side_gated, halves[0])
+        weights(1, 0, *last, KEPT)
+        weights_on_gpsimd(squares, 0, side)
         dense = leave(product(0, HALF), HALF)
-        positive_part(positive, side_bank, halves[1])
-        weights_on_gpsimd(1, 1, positive, side_gated, halves[1])
         place(0, dense, HALF, N)
         for g in range(G):
             cast_d(2, g, "S")
-        quant_d(2, both, d_third[:])
         quant_w(1, 0, w_lower[1])
-        place(1, leave(product(1, HALF), HALF, after_pool), HALF, N)
-        lower = [product(e, 0) for e in range(2)]
-        d_fourth = keep.tile([P, G * PASS], BF16, name="d_fourth", tag="stage", align_bytes=64)
+        d_scales.setdefault(2, after_pool.tile([P, G, P], U8, name="d_scales2", align_bytes=64, offset=HALF * 4))
+        quant_d(2, both, d_third[:])
+        held = after_pool.tile([P, HALF], F32, name="held", align_bytes=64, offset=0)
+        place(1, leave(product(1, HALF), HALF, held), HALF, N)
+        lower = [product(0, 0), product(1, 0, (1, 0))]
+        d_fourth = after_pool.tile([P, G * PASS], BF16, name="d_fourth", align_bytes=64, offset=HALF * 4 + G * P)
         for g in range(G):
             d_bf.setdefault((3, g), d_fourth[:, g * PASS : (g + 1) * PASS])
             cast_d(3, g, "S")

@@ -23,60 +23,65 @@ P = 128
 PACK = 4
 PASS = P * PACK
 G = R // PASS
-E_TILES = DV // P
+VALUE_TILES = DV // P
 CH = 128
 HALF = N // 2
-Q_PIECES = ((0, 512), (512, 768), (768, 1024))
-Q_SHARE = 96
-WINDOWS = 4
+PER_COLUMN = 16
+BOTH = slice(0, G)
+LOW_PLACES, HIGH_PLACES = slice(0, 2), slice(2, PACK)
+
+Q_LOADS = ((0, 512), (512, 768), (768, 1024))
+FIRST_SHARE = 352
+SECOND_SHARE = 96
 KEPT = 112
+SIDE = HALF - KEPT
+GATED_ROW = CH + 1
 
 
 def tile_attend_gat_v_kernel(tc, qT, kT, rw, dom, offs, out):
     nc = tc.nc
 
     def cast(engine, dst, src):
-        if engine == "S":
+        if engine == "scalar":
             nc.scalar.activation(out=dst, in_=src, func=COPY)
-        elif engine == "V":
+        elif engine == "vector":
             nc.vector.tensor_copy(out=dst, in_=src)
         else:
             nc.gpsimd.tensor_scalar(out=dst, in0=src, scalar1=1.0, scalar2=0.0, op0=MULT, op1=ADD)
 
     with ExitStack() as ctx:
         keep = ctx.enter_context(tc.tile_pool(name="keep", bufs=1))
-        stage = ctx.enter_context(tc.tile_pool(name="stage", bufs=5))
-        after_pool = ctx.enter_context(tc.tile_pool(name="after_pool", bufs=1))
-        after_cast = ctx.enter_context(tc.tile_pool(name="after_cast", bufs=1))
-        after_q = ctx.enter_context(tc.tile_pool(name="after_q", bufs=1))
+        gated_pool = ctx.enter_context(tc.tile_pool(name="gated_pool", bufs=5))
+        after_side = ctx.enter_context(tc.tile_pool(name="after_side", bufs=1))
+        after_bank = ctx.enter_context(tc.tile_pool(name="after_bank", bufs=1))
+        after_queries = ctx.enter_context(tc.tile_pool(name="after_queries", bufs=1))
         dense_pool = ctx.enter_context(tc.tile_pool(name="dense_pool", bufs=2))
-        spsum = ctx.enter_context(tc.psum_pool(name="spsum", bufs=6))
-        opsum = ctx.enter_context(tc.psum_pool(name="opsum", bufs=2))
+        score_psum = ctx.enter_context(tc.psum_pool(name="score_psum", bufs=6))
+        sum_psum = ctx.enter_context(tc.psum_pool(name="sum_psum", bufs=2))
 
-        offsets = keep.tile([P, N // 16], U16, name="offsets")
+        offsets = keep.tile([P, N // PER_COLUMN], U16, name="offsets")
         k_planes = [keep.tile([P, T], F32, name="k_plane%d" % j) for j in range(PACK)]
         k_rows = kT.rearrange("(p j) c -> p j c", j=PACK)
         q_rows = qT[0].rearrange("(p j) r -> p j r", j=PACK)
-        q_raw = [keep.tile([P, PACK, hi - lo], F32, name="q_raw%d" % lo) for lo, hi in Q_PIECES[:-1]]
-        q_raw.append(after_q.tile([P, PACK, R - Q_PIECES[-1][0]], F32, name="q_last", tag="shared", align_bytes=64))
-
+        q_raw = [keep.tile([P, PACK, hi - lo], F32, name="q_raw%d" % lo) for lo, hi in Q_LOADS[:-1]]
+        q_raw.append(
+            after_queries.tile([P, PACK, R - Q_LOADS[-1][0]], F32, name="q_last", tag="shared", align_bytes=64)
+        )
         gate = keep.tile([P, G, 2 * PACK], F32, name="gate")
         d_rows = dom[0].rearrange("(g p j) e -> g p j e", p=P, j=PACK)
-        d_first = [keep.tile([P, PACK, 2 * P], F32, name="d_first%d" % g) for g in range(G)]
-        d_rest = [keep.tile([P, PACK, DV - 2 * P], F32, name="d_rest%d" % g) for g in range(G)]
-        windows = [keep.tile([P, T], F32, name="window%d" % e) for e in range(WINDOWS)]
+        d_raw = [[keep.tile([P, PACK, 2 * P], F32, name="d_raw%d%d" % (pair, g)) for g in range(G)] for pair in range(2)]
+        windows = [keep.tile([P, T], F32, name="window%d" % e) for e in range(VALUE_TILES)]
 
         nc.sync.dma_start(out=k_planes[0][:], in_=k_rows[:, 0, :])
         nc.sync.dma_start(offsets[:], offs)
         for j in range(1, PACK):
             nc.sync.dma_start(out=k_planes[j][:], in_=k_rows[:, j, :])
         nc.scalar.dma_start(out=gate[:, :, :PACK], in_=rw[0].rearrange("(g p t) o -> p g (t o)", p=P, t=PACK))
-        for raw, (lo, hi) in zip(q_raw, Q_PIECES):
+        for raw, (lo, hi) in zip(q_raw, Q_LOADS):
             nc.sync.dma_start(out=raw[:], in_=q_rows[:, :, lo:hi])
-        for g in range(G):
-            nc.sync.dma_start(out=d_first[g][:], in_=d_rows[g, :, :, : 2 * P])
-        for g in range(G):
-            nc.sync.dma_start(out=d_rest[g][:], in_=d_rows[g, :, :, 2 * P : DV])
+        for pair in range(2):
+            for g in range(G):
+                nc.sync.dma_start(out=d_raw[pair][g][:], in_=d_rows[g, :, :, pair * 2 * P : (pair + 1) * 2 * P])
 
         for window in windows:
             nc.gpsimd.memset(window[:], 0.0)
@@ -88,35 +93,31 @@ def tile_attend_gat_v_kernel(tc, qT, kT, rw, dom, offs, out):
         k_codes = keep.tile([P, N], U32, name="k_codes", align_bytes=64)
         k_scales = keep.tile([P, N], U8, name="k_scales", align_bytes=64)
         q_bf0 = keep.tile([P, PACK * PASS], BF16, name="q_bf0", align_bytes=64)
-        q_then_d = keep.tile([P, (PACK + 3) * PASS], BF16, name="q_then_d", align_bytes=64)
-        q_bf = [t[:, : PACK * PASS].rearrange("p (t m j) -> p t m j", t=PACK, j=PACK) for t in (q_bf0, q_then_d)]
+
+        arena = keep.tile([P, 7 * PASS], BF16, name="arena", align_bytes=64)
+
+        def cells(first, count=1):
+            return arena[:, first * PASS : (first + count) * PASS]
+
+        q_bf = [t.rearrange("p (t m j) -> p t m j", t=PACK, j=PACK) for t in (q_bf0[:], cells(0, PACK))]
         q_codes = [keep.tile([P, PASS], U32, name="q_codes%d" % g, align_bytes=64) for g in range(G)]
         q_scales = [keep.tile([P, PASS], U8, name="q_scales%d" % g, align_bytes=64) for g in range(G)]
-        w_bf = {}
-        w_codes = [keep.tile([P, HALF + N], U32, name="w_codes%d" % g, align_bytes=64) for g in range(G)]
-        w_scales = {1: keep.tile([P, HALF + N], U8, name="w_scales1", align_bytes=64)}
-        d_bf = {
-            (e, g): q_then_d[:, (1 + e * G + g) * PASS : (2 + e * G + g) * PASS] for e in range(2) for g in range(G)
-        }
-        d_third = keep.tile([P, G * PASS], BF16, name="d_third", align_bytes=64)
-        for g in range(G):
-            d_bf.setdefault((2, g), d_third[:, g * PASS : (g + 1) * PASS])
-        d_codes = [keep.tile([P, G, P], U32, name="d_codes%d" % e, align_bytes=64) for e in range(E_TILES)]
-        d_scales = {e: keep.tile([P, G, P], U8, name="d_scales%d" % e, align_bytes=64) for e in (1, 3)}
-
-        def d_plane(e, groups):
-            if e == 0:
-                return w_scales[0][:, HALF + N + groups.start * P : HALF + N + groups.stop * P]
-            return d_scales[e][:, groups].rearrange("p g e -> p (g e)")
+        w_codes = [keep.tile([P, N + HALF], U32, name="w_codes%d" % g, align_bytes=64) for g in range(G)]
+        w_scales = {1: keep.tile([P, N + HALF], U8, name="w_scales1", align_bytes=64)}
+        d_bf2 = keep.tile([P, G * PASS], BF16, name="d_bf2", align_bytes=64)
+        d_bf = {(0, 0): cells(1), (0, 1): cells(6), (1, 0): cells(3), (1, 1): cells(4)}
+        d_codes = [keep.tile([P, G * P], U32, name="d_codes%d" % e, align_bytes=64) for e in range(VALUE_TILES)]
+        d_scales = {e: keep.tile([P, G * P], U8, name="d_scales%d" % e, align_bytes=64) for e in (1, 3)}
 
         for g in range(G):
             nc.gpsimd.memset(w_codes[g][:, N:], 0)
         nc.gpsimd.memset(w_scales[1][:, N:].bitcast(U32), 0)
 
+        def entries(lo, hi):
+            return offsets[:, lo // PER_COLUMN : hi // PER_COLUMN]
+
         def gather(j, lo, hi):
-            nc.vector.tensor_copy(
-                out=k_bf[:, lo:hi, j], in_=k_planes[j][:].indirect(offsets[:, lo // 16 : hi // 16])
-            )
+            nc.vector.tensor_copy(out=k_bf[:, lo:hi, j], in_=k_planes[j][:].indirect(entries(lo, hi)))
 
         def quant_k(lo, hi):
             nc.vector.quantize_mx(
@@ -125,12 +126,12 @@ def tile_attend_gat_v_kernel(tc, qT, kT, rw, dom, offs, out):
                 in_=k_bf[:, lo:hi, :].rearrange("p n j -> p (n j)"),
             )
 
-        def cast_q(lo, hi, engine, ts=slice(0, PACK)):
+        def cast_q(lo, hi, engine, places=slice(0, PACK)):
             g = lo // PASS
-            raw, first = [(raw, a) for raw, (a, b) in zip(q_raw, Q_PIECES) if a <= lo < b][0]
+            raw, first = [(raw, a) for raw, (a, b) in zip(q_raw, Q_LOADS) if a <= lo < b][0]
             ms = slice((lo - g * PASS) // PACK, (hi - g * PASS) // PACK)
             src = raw[:, :, lo - first : hi - first].rearrange("p j (m t) -> p m j t", t=PACK)
-            cast(engine, q_bf[g].rearrange("p t m j -> p m j t")[:, ms, :, ts], src[:, :, :, ts])
+            cast(engine, q_bf[g].rearrange("p t m j -> p m j t")[:, ms, :, places], src[:, :, :, places])
 
         def quant_q(g, lo, hi):
             for t in range(PACK):
@@ -140,31 +141,21 @@ def tile_attend_gat_v_kernel(tc, qT, kT, rw, dom, offs, out):
                     in_=q_bf[g][:, t, lo:hi, :].rearrange("p m j -> p (m j)"),
                 )
 
-        def cast_d(e, g, engine):
-            src = (d_first if e < 2 else d_rest)[g][:, :, e % 2 * P : (e % 2 + 1) * P]
-            if engine == "G":
-                cast(engine, d_bf[e, g].rearrange("p (e j) -> p e j", j=PACK), src.rearrange("p j e -> p e j"))
-            else:
-                cast(
-                    engine,
-                    d_bf[e, g].rearrange("p (c i j) -> p c j i", i=PACK, j=PACK),
-                    src.rearrange("p j (c i) -> p c j i", i=PACK),
-                )
-
-        def cast_first_d():
-            dst = q_then_d[:, PASS : 5 * PASS].rearrange("p (h g e j) -> p h g e j", h=2, g=G, j=PACK)
-            cast("G", dst[:, :, 0], d_first[0][:].rearrange("p j (h e) -> p h e j", h=2))
-
-        def quant_d(e, groups, src):
-            nc.vector.quantize_mx(
-                out=d_codes[e][:, groups].rearrange("p g e -> p (g e)").bitcast(E5),
-                scales=d_plane(e, groups),
-                in_=src,
+        def cast_d(e, g, dst):
+            src = d_raw[e // 2][g][:, :, e % 2 * P : (e % 2 + 1) * P]
+            cast(
+                "scalar",
+                dst.rearrange("p (c i j) -> p c j i", i=PACK, j=PACK),
+                src.rearrange("p j (c i) -> p c j i", i=PACK),
             )
 
-        def scores(g, c, first_t):
+        def quant_d(e, groups, src):
+            cols = slice(groups.start * P, groups.stop * P)
+            nc.vector.quantize_mx(out=d_codes[e][:, cols].bitcast(E5), scales=d_scales[e][:, cols], in_=src)
+
+        def scores(g, c, first_t=PACK - 1):
             cols = slice(c * CH, (c + 1) * CH)
-            bank = spsum.tile([P, PACK, CH], F32, name="scores")
+            bank = score_psum.tile([P, PACK, CH], F32, name="scores")
             for t in [(first_t + i) % PACK for i in range(PACK)]:
                 nc.tensor.matmul_mx(
                     out=bank[:, t, :],
@@ -177,27 +168,18 @@ def tile_attend_gat_v_kernel(tc, qT, kT, rw, dom, offs, out):
                 )
             return bank
 
-        def gated_scores(g, c, pool, first_t):
-            return gate_bank(g, scores(g, c, first_t), pool, CH)
+        def gated_tile(pool=gated_pool):
+            return pool.tile([P, PACK, GATED_ROW], F32, name="gated", tag="gated", align_bytes=64)
 
-        def gate_bank(g, bank, pool, width, ts=range(PACK), gated=None):
-            if gated is None:
-                gated = pool.tile([P, PACK, CH + 1], F32, name="gated", tag="stage", align_bytes=64)
-            for t in ts:
-                nc.scalar.activation(out=gated[:, t, :width], in_=bank[:, t, :width], func=COPY, scale=gate[:, g, t : t + 1])
-            return bank, gated
+        def gate_scores(g, bank, gated, places=range(PACK), width=CH):
+            for t in places:
+                nc.scalar.activation(
+                    out=gated[:, t, :width], in_=bank[:, t, :width], func=COPY, scale=gate[:, g, t : t + 1]
+                )
 
-        def weights_on_gpsimd(squares, lo, hi):
-            nc.gpsimd.tensor_tensor(
-                out=w_lower[1].rearrange("p (n t) -> p n t", t=PACK)[:, KEPT + lo : KEPT + hi],
-                in0=squares[:, lo:hi],
-                in1=side_gate[:].to_broadcast([P, hi - lo, PACK]),
-                op=MULT,
-            )
-
-        def weights(g, c, bank, gated, width=CH):
+        def weights(dst, bank, gated, width=CH):
             nc.vector.scalar_tensor_tensor(
-                out=w_bf[g, c][:, :width],
+                out=dst.rearrange("p (n t) -> p n t", t=PACK)[:, :width],
                 in0=bank[:, :, :width].rearrange("p t n -> p n t"),
                 scalar=0.0,
                 in1=gated[:, :, :width].rearrange("p t n -> p n t"),
@@ -205,18 +187,24 @@ def tile_attend_gat_v_kernel(tc, qT, kT, rw, dom, offs, out):
                 op1=MULT,
             )
 
+        def whole_bank(dst, g, c, first_t=PACK - 1, pool=gated_pool):
+            bank = scores(g, c, first_t)
+            gated = gated_tile(pool)
+            gate_scores(g, bank, gated)
+            weights(dst, bank, gated)
+
         def quant_w(g, lo, src):
             nc.vector.quantize_mx(
                 out=w_codes[g][:, lo : lo + HALF].bitcast(E4), scales=w_scales[g][:, lo : lo + HALF], in_=src
             )
 
-        def product(e, first, groups=range(G)):
-            acc = opsum.tile([P, N], F32, name="acc")
+        def product(e, first, groups=(0, 1)):
+            acc = sum_psum.tile([P, N], F32, name="acc")
             for g in groups:
                 nc.tensor.matmul_mx(
                     out=acc[:],
-                    lhsT=d_codes[e][:, g, :].bitcast(E5),
-                    lhsT_scale=d_plane(e, slice(g, g + 1)),
+                    lhsT=d_codes[e][:, g * P : (g + 1) * P].bitcast(E5),
+                    lhsT_scale=d_scales[e][:, g * P : (g + 1) * P],
                     rhs=w_codes[g][:, first : first + N].bitcast(E4),
                     rhs_scale=w_scales[g][:, first : first + N],
                     start=(g == groups[0]),
@@ -224,22 +212,17 @@ def tile_attend_gat_v_kernel(tc, qT, kT, rw, dom, offs, out):
                 )
             return acc
 
-        def leave(acc, width, dense=None):
+        def to_sbuf(acc, width, dense=None):
             if dense is None:
                 dense = dense_pool.tile([P, N], F32, name="dense")
             nc.scalar.activation(out=dense[:, :width], in_=acc[:, :width], func=COPY)
             return dense[:, :width]
 
-        def place(e, src, lo, hi):
-            nc.vector.tensor_copy(out=windows[e % WINDOWS][:].indirect(offsets[:, lo // 16 : hi // 16]), in_=src)
+        def scatter(e, src, lo, hi):
+            nc.vector.tensor_copy(out=windows[e][:].indirect(entries(lo, hi)), in_=src)
 
-        def store(e):
-            rows = out[e * P : (e + 1) * P, :]
-            if e + 1 < E_TILES:
-                nc.sync.dma_start(out=rows, in_=windows[e % WINDOWS][:])
-            else:
-                nc.sync.dma_start(out=rows[:, : T // 2], in_=windows[e % WINDOWS][:, : T // 2])
-                nc.scalar.dma_start(out=rows[:, T // 2 :], in_=windows[e % WINDOWS][:, T // 2 :])
+        def store(e, queue=nc.sync):
+            queue.dma_start(out=out[e * P : (e + 1) * P, :], in_=windows[e][:])
 
         for j in range(PACK - 1):
             gather(j, 0, N)
@@ -247,79 +230,94 @@ def tile_attend_gat_v_kernel(tc, qT, kT, rw, dom, offs, out):
         gather(PACK - 1, 0, HALF)
         quant_k(HALF, N)
         quant_k(0, HALF)
-        cast_q(0, PASS, "V", slice(0, 2))
-        cast_q(0, 352, "S", slice(2, PACK))
-        cast_q(352, PASS, "V", slice(2, PACK))
+
+        (_, second), (_, third), _ = Q_LOADS
+        cast_q(0, second, "vector", LOW_PLACES)
+        cast_q(0, FIRST_SHARE, "scalar", HIGH_PLACES)
+        cast_q(FIRST_SHARE, second, "vector", HIGH_PLACES)
         quant_q(0, 0, P)
-        cast_q(512, 512 + 96, "S")
-        cast_q(512 + 96, 768, "V", slice(0, 2))
-        cast_q(512 + 96, 768, "V", slice(2, PACK))
+        cast_q(second, second + SECOND_SHARE, "scalar")
+        cast_q(second + SECOND_SHARE, third, "vector", LOW_PLACES)
+        cast_q(second + SECOND_SHARE, third, "vector", HIGH_PLACES)
         quant_q(1, 0, P // 2)
-        cast_q(768, R, "V", slice(0, 2))
-        cast_q(768, R, "V", slice(2, PACK))
+        cast_q(third, R, "vector", LOW_PLACES)
+        cast_q(third, R, "vector", HIGH_PLACES)
         quant_q(1, P // 2, P)
+
         w_upper = [
-            after_q.tile([P, 2 * PASS], BF16, name="w_upper0", tag="shared", align_bytes=64),
+            after_queries.tile([P, 2 * PASS], BF16, name="w_upper0", tag="shared", align_bytes=64),
             keep.tile([P, 2 * PASS], BF16, name="w_upper1", align_bytes=64),
         ]
-        w_lower = [q_then_d[:, (PACK + 1 - g) * PASS : (PACK + 3 - g) * PASS] for g in range(G)]
+        w_lower = [cells(5, 2), cells(4, 2)]
+        positive = keep.tile([P, SIDE, PACK], F32, name="positive")
+        squares = after_side.tile([P, SIDE, PACK], F32, name="squares", align_bytes=64, offset=0)
+
+        first_pair = cells(1, PACK).rearrange("p (h c e j) -> p h c e j", h=2, c=2, j=PACK)[:, :, 0]
+        cast("gpsimd", first_pair, d_raw[0][0][:].rearrange("p j (h e) -> p h e j", h=2))
+        cast(
+            "gpsimd",
+            d_bf[0, 1].rearrange("p (e j) -> p e j", j=PACK),
+            d_raw[0][1][:, :, :P].rearrange("p j e -> p e j"),
+        )
+        whole_bank(w_upper[0][:, :PASS], 0, 2, first_t=0)
+        whole_bank(w_upper[0][:, PASS:], 0, 3)
+        whole_bank(w_lower[0][:, :PASS], 0, 0)
+        later_bank = scores(0, 1)
+        later_gated = gated_tile()
+        gate_scores(0, later_bank, later_gated, range(PACK)[LOW_PLACES])
+        whole_bank(w_upper[1][:, :PASS], 1, 2, first_t=0, pool=after_bank)
+        whole_bank(w_upper[1][:, PASS:], 1, 3)
+
+        held_scales = after_bank.tile([P, N + HALF + G * P], U8, name="held_scales", tag="gated", align_bytes=64)
+        w_scales.update({0: held_scales[:, : N + HALF]})
+        d_scales.update({0: held_scales[:, N + HALF :]})
+        nc.gpsimd.memset(w_scales[0][:, N:].bitcast(U32), 0)
         for g in range(G):
-            for c in range(PACK):
-                home = w_lower[g] if c < 2 else w_upper[g]
-                w_bf.setdefault((g, c), home[:, c % 2 * PASS : (c % 2 + 1) * PASS].rearrange("p (n t) -> p n t", t=PACK))
-        both = slice(0, G)
-        d_bf.update({(0, 1): w_lower[0][:, PASS:]})
-        side = HALF - KEPT
-        positive = keep.tile([P, side, PACK], F32, name="positive")
-        squares = after_pool.tile([P, side, PACK], F32, name="squares", align_bytes=64, offset=0)
-        cast_first_d()
-        cast_d(0, 1, "G")
-        weights(0, 2, *gated_scores(0, 2, stage, 0))
-        weights(0, 3, *gated_scores(0, 3, stage, PACK - 1))
-        weights(0, 0, *gated_scores(0, 0, stage, PACK - 1))
-        late = gate_bank(0, scores(0, 1, PACK - 1), stage, CH, range(2))
-        weights(1, 2, *gated_scores(1, 2, after_cast, 0))
-        weights(1, 3, *gated_scores(1, 3, stage, PACK - 1))
-        w_scales.setdefault(0, after_cast.tile([P, HALF + N + G * P], U8, name="w_scales0", tag="stage", align_bytes=64))
-        nc.gpsimd.memset(w_scales[0][:, N : HALF + N].bitcast(U32), 0)
-        quant_d(0, slice(0, 1), d_bf[0, 0])
-        quant_w(0, HALF, w_upper[0][:])
-        quant_d(0, slice(1, 2), d_bf[0, 1])
-        quant_w(1, HALF, w_upper[1][:])
-        weights(0, 1, *gate_bank(0, late[0], stage, CH, range(2, PACK), late[1]))
-        cast_d(1, 1, "S")
-        side_bank = scores(1, 1, PACK - 1)
+            quant_d(0, slice(g, g + 1), d_bf[0, g])
+            quant_w(g, HALF, w_upper[g][:])
+
+        gate_scores(0, later_bank, later_gated, range(PACK)[HIGH_PLACES])
+        weights(w_lower[0][:, PASS:], later_bank, later_gated)
+        cast_d(1, 1, d_bf[1, 1])
+        side_bank = scores(1, 1)
         nc.scalar.activation(out=positive[:, CH - KEPT :], in_=side_bank[:].rearrange("p t n -> p n t"), func=RELU)
-        shared_bank = scores(1, 0, PACK - 1)
+        shared_bank = scores(1, 0)
         nc.scalar.activation(
             out=positive[:, : CH - KEPT], in_=shared_bank[:, :, KEPT:].rearrange("p t n -> p n t"), func=RELU
         )
-        last = gate_bank(1, shared_bank, stage, KEPT)
+        shared_gated = gated_tile()
+        gate_scores(1, shared_bank, shared_gated, width=KEPT)
         nc.scalar.activation(out=squares[:], in_=positive[:], func=SQUARE)
-        quant_d(1, both, q_then_d[:, (PACK - 1) * PASS : (PACK + 1) * PASS])
+        quant_d(1, BOTH, cells(3, 2))
         quant_w(0, 0, w_lower[0])
-        weights(1, 0, *last, KEPT)
-        weights_on_gpsimd(squares, 0, side)
-        dense = leave(product(0, HALF), HALF)
-        place(0, dense, HALF, N)
+        weights(w_lower[1][:, :PASS], shared_bank, shared_gated, KEPT)
+        nc.gpsimd.tensor_tensor(
+            out=w_lower[1].rearrange("p (n t) -> p n t", t=PACK)[:, KEPT:],
+            in0=squares[:],
+            in1=side_gate[:].to_broadcast([P, SIDE, PACK]),
+            op=MULT,
+        )
+
+        scatter(0, to_sbuf(product(0, HALF), HALF), HALF, N)
         for g in range(G):
-            cast_d(2, g, "S")
+            cast_d(2, g, d_bf2[:, g * PASS : (g + 1) * PASS])
         quant_w(1, 0, w_lower[1])
-        d_scales.setdefault(2, after_pool.tile([P, G, P], U8, name="d_scales2", align_bytes=64, offset=HALF * 4))
-        quant_d(2, both, d_third[:])
-        held = after_pool.tile([P, HALF], F32, name="held", align_bytes=64, offset=0)
-        place(1, leave(product(1, HALF), HALF, held), HALF, N)
-        lower = [product(0, 0), product(1, 0, (1, 0))]
-        d_fourth = after_pool.tile([P, G * PASS], BF16, name="d_fourth", align_bytes=64, offset=HALF * 4 + G * P)
+        upper_bytes = HALF * 4
+        d_scales.update({2: after_side.tile([P, G * P], U8, name="d_scales2", align_bytes=64, offset=upper_bytes)})
+        quant_d(2, BOTH, d_bf2[:])
+        second_upper = after_side.tile([P, HALF], F32, name="second_upper", align_bytes=64, offset=0)
+        scatter(1, to_sbuf(product(1, HALF), HALF, second_upper), HALF, N)
+        lower = [product(0, 0), product(1, 0, groups=(1, 0))]
+        d_bf3 = after_side.tile([P, G * PASS], BF16, name="d_bf3", align_bytes=64, offset=upper_bytes + G * P)
         for g in range(G):
-            d_bf.setdefault((3, g), d_fourth[:, g * PASS : (g + 1) * PASS])
-            cast_d(3, g, "S")
-        dense = leave(lower[0], HALF)
-        quant_d(3, both, d_fourth[:])
-        place(0, dense, 0, HALF)
+            cast_d(3, g, d_bf3[:, g * PASS : (g + 1) * PASS])
+        first_lower = to_sbuf(lower[0], HALF)
+        quant_d(3, BOTH, d_bf3[:])
+        scatter(0, first_lower, 0, HALF)
         store(0)
-        place(1, leave(lower[1], HALF), 0, HALF)
+        scatter(1, to_sbuf(lower[1], HALF), 0, HALF)
         store(1)
-        for e in range(2, E_TILES):
-            place(e, leave(product(e, 0), N), 0, N)
-            store(e)
+        scatter(2, to_sbuf(product(2, 0), N), 0, N)
+        store(2)
+        scatter(3, to_sbuf(product(3, 0), N), 0, N)
+        store(3, nc.scalar)

@@ -13,8 +13,6 @@ U8 = mybir.dt.uint8
 E4 = mybir.dt.float8_e4m3fn_x4
 E5 = mybir.dt.float8_e5m2_x4
 COPY = mybir.ActivationFunctionType.Copy
-RELU = mybir.ActivationFunctionType.Relu
-SQUARE = mybir.ActivationFunctionType.Square
 MULT = mybir.AluOpType.mult
 ADD = mybir.AluOpType.add
 MAX = mybir.AluOpType.max
@@ -27,14 +25,12 @@ VALUE_TILES = DV // P
 CH = 128
 HALF = N // 2
 PER_COLUMN = 16
-BOTH = slice(0, G)
+EARLY, LATE = 0, 1
 LOW_PLACES, HIGH_PLACES = slice(0, 2), slice(2, PACK)
 
 Q_LOADS = ((0, 512), (512, 768), (768, 1024))
 FIRST_SHARE = 352
 SECOND_SHARE = 96
-KEPT = 112
-SIDE = HALF - KEPT
 GATED_ROW = CH + 1
 
 
@@ -51,23 +47,21 @@ def tile_attend_gat_v_kernel(tc, qT, kT, rw, dom, offs, out):
 
     with ExitStack() as ctx:
         keep = ctx.enter_context(tc.tile_pool(name="keep", bufs=1))
-        gated_pool = ctx.enter_context(tc.tile_pool(name="gated_pool", bufs=5))
-        after_side = ctx.enter_context(tc.tile_pool(name="after_side", bufs=1))
-        after_bank = ctx.enter_context(tc.tile_pool(name="after_bank", bufs=1))
-        after_queries = ctx.enter_context(tc.tile_pool(name="after_queries", bufs=1))
-        dense_pool = ctx.enter_context(tc.tile_pool(name="dense_pool", bufs=2))
-        score_psum = ctx.enter_context(tc.psum_pool(name="score_psum", bufs=6))
-        sum_psum = ctx.enter_context(tc.psum_pool(name="sum_psum", bufs=2))
+        gated_pool = ctx.enter_context(tc.tile_pool(name="gated_pool", bufs=4))
+        chain = ctx.enter_context(tc.tile_pool(name="chain", bufs=1))
+        psum = ctx.enter_context(tc.psum_pool(name="psum", bufs=8))
+
+        def chained(shape, dtype, name):
+            return chain.tile(shape, dtype, name=name, tag="chain", align_bytes=64)
 
         offsets = keep.tile([P, N // PER_COLUMN], U16, name="offsets")
         k_planes = [keep.tile([P, T], F32, name="k_plane%d" % j) for j in range(PACK)]
         k_rows = kT.rearrange("(p j) c -> p j c", j=PACK)
         q_rows = qT[0].rearrange("(p j) r -> p j r", j=PACK)
         q_raw = [keep.tile([P, PACK, hi - lo], F32, name="q_raw%d" % lo) for lo, hi in Q_LOADS[:-1]]
-        q_raw.append(
-            after_queries.tile([P, PACK, R - Q_LOADS[-1][0]], F32, name="q_last", tag="shared", align_bytes=64)
-        )
-        gate = keep.tile([P, G, 2 * PACK], F32, name="gate")
+        q_raw.append(chained([P, PACK, R - Q_LOADS[-1][0]], F32, "q_last"))
+        gate_raw = keep.tile([P, G, 2 * PACK], F32, name="gate_raw")
+        gate = keep.tile([P, G, PACK], F32, name="gate")
         d_rows = dom[0].rearrange("(g p j) e -> g p j e", p=P, j=PACK)
         d_raw = [[keep.tile([P, PACK, 2 * P], F32, name="d_raw%d%d" % (pair, g)) for g in range(G)] for pair in range(2)]
         windows = [keep.tile([P, T], F32, name="window%d" % e) for e in range(VALUE_TILES)]
@@ -76,7 +70,7 @@ def tile_attend_gat_v_kernel(tc, qT, kT, rw, dom, offs, out):
         nc.sync.dma_start(offsets[:], offs)
         for j in range(1, PACK):
             nc.sync.dma_start(out=k_planes[j][:], in_=k_rows[:, j, :])
-        nc.scalar.dma_start(out=gate[:, :, :PACK], in_=rw[0].rearrange("(g p t) o -> p g (t o)", p=P, t=PACK))
+        nc.scalar.dma_start(out=gate_raw[:, :, :PACK], in_=rw[0].rearrange("(g p t) o -> p g (t o)", p=P, t=PACK))
         for raw, (lo, hi) in zip(q_raw, Q_LOADS):
             nc.sync.dma_start(out=raw[:], in_=q_rows[:, :, lo:hi])
         for pair in range(2):
@@ -86,15 +80,13 @@ def tile_attend_gat_v_kernel(tc, qT, kT, rw, dom, offs, out):
         for window in windows:
             nc.gpsimd.memset(window[:], 0.0)
 
-        side_gate = keep.tile([P, 1, PACK], F32, name="side_gate")
-        nc.scalar.activation(out=side_gate[:], in_=gate[:, 1:2, :PACK], func=COPY)
+        nc.scalar.activation(out=gate[:], in_=gate_raw[:, :, :PACK], func=COPY)
 
         k_bf = keep.tile([P, N, PACK], BF16, name="k_bf", align_bytes=64)
         k_codes = keep.tile([P, N], U32, name="k_codes", align_bytes=64)
         k_scales = keep.tile([P, N], U8, name="k_scales", align_bytes=64)
         q_bf0 = keep.tile([P, PACK * PASS], BF16, name="q_bf0", align_bytes=64)
-
-        arena = keep.tile([P, 7 * PASS], BF16, name="arena", align_bytes=64)
+        arena = keep.tile([P, 5 * PASS], BF16, name="arena", align_bytes=64)
 
         def cells(first, count=1):
             return arena[:, first * PASS : (first + count) * PASS]
@@ -102,16 +94,10 @@ def tile_attend_gat_v_kernel(tc, qT, kT, rw, dom, offs, out):
         q_bf = [t.rearrange("p (t m j) -> p t m j", t=PACK, j=PACK) for t in (q_bf0[:], cells(0, PACK))]
         q_codes = [keep.tile([P, PASS], U32, name="q_codes%d" % g, align_bytes=64) for g in range(G)]
         q_scales = [keep.tile([P, PASS], U8, name="q_scales%d" % g, align_bytes=64) for g in range(G)]
-        w_codes = [keep.tile([P, N + HALF], U32, name="w_codes%d" % g, align_bytes=64) for g in range(G)]
-        w_scales = {1: keep.tile([P, N + HALF], U8, name="w_scales1", align_bytes=64)}
-        d_bf2 = keep.tile([P, G * PASS], BF16, name="d_bf2", align_bytes=64)
-        d_bf = {(0, 0): cells(1), (0, 1): cells(6), (1, 0): cells(3), (1, 1): cells(4)}
+        w_codes = [keep.tile([P, G * HALF], U32, name="w_codes%d" % h, align_bytes=64) for h in range(2)]
+        w_scales = [keep.tile([P, G * HALF], U8, name="w_scales%d" % h, align_bytes=64) for h in range(2)]
         d_codes = [keep.tile([P, G * P], U32, name="d_codes%d" % e, align_bytes=64) for e in range(VALUE_TILES)]
-        d_scales = {e: keep.tile([P, G * P], U8, name="d_scales%d" % e, align_bytes=64) for e in (1, 3)}
-
-        for g in range(G):
-            nc.gpsimd.memset(w_codes[g][:, N:], 0)
-        nc.gpsimd.memset(w_scales[1][:, N:].bitcast(U32), 0)
+        d_scales = [keep.tile([P, G * P], U8, name="d_scales%d" % e, align_bytes=64) for e in range(VALUE_TILES)]
 
         def entries(lo, hi):
             return offsets[:, lo // PER_COLUMN : hi // PER_COLUMN]
@@ -119,12 +105,11 @@ def tile_attend_gat_v_kernel(tc, qT, kT, rw, dom, offs, out):
         def gather(j, lo, hi):
             nc.vector.tensor_copy(out=k_bf[:, lo:hi, j], in_=k_planes[j][:].indirect(entries(lo, hi)))
 
+        def quantise(codes, scales, src, fmt=E4):
+            nc.vector.quantize_mx(out=codes.bitcast(fmt), scales=scales, in_=src)
+
         def quant_k(lo, hi):
-            nc.vector.quantize_mx(
-                out=k_codes[:, lo:hi].bitcast(E4),
-                scales=k_scales[:, lo:hi],
-                in_=k_bf[:, lo:hi, :].rearrange("p n j -> p (n j)"),
-            )
+            quantise(k_codes[:, lo:hi], k_scales[:, lo:hi], k_bf[:, lo:hi, :].rearrange("p n j -> p (n j)"))
 
         def cast_q(lo, hi, engine, places=slice(0, PACK)):
             g = lo // PASS
@@ -135,27 +120,23 @@ def tile_attend_gat_v_kernel(tc, qT, kT, rw, dom, offs, out):
 
         def quant_q(g, lo, hi):
             for t in range(PACK):
-                nc.vector.quantize_mx(
-                    out=q_codes[g][:, t * P + lo : t * P + hi].bitcast(E4),
-                    scales=q_scales[g][:, t * P + lo : t * P + hi],
-                    in_=q_bf[g][:, t, lo:hi, :].rearrange("p m j -> p (m j)"),
+                cols = slice(t * P + lo, t * P + hi)
+                quantise(q_codes[g][:, cols], q_scales[g][:, cols], q_bf[g][:, t, lo:hi, :].rearrange("p m j -> p (m j)"))
+
+        def quant_d(e, src):
+            quantise(d_codes[e][:], d_scales[e][:], src, E5)
+
+        def cast_d(e, dst):
+            for g in range(G):
+                cast(
+                    "gpsimd",
+                    dst[:, g * PASS : (g + 1) * PASS].rearrange("p (e j) -> p e j", j=PACK),
+                    d_raw[e // 2][g][:, :, e % 2 * P : (e % 2 + 1) * P].rearrange("p j e -> p e j"),
                 )
 
-        def cast_d(e, g, dst):
-            src = d_raw[e // 2][g][:, :, e % 2 * P : (e % 2 + 1) * P]
-            cast(
-                "scalar",
-                dst.rearrange("p (c i j) -> p c j i", i=PACK, j=PACK),
-                src.rearrange("p j (c i) -> p c j i", i=PACK),
-            )
-
-        def quant_d(e, groups, src):
-            cols = slice(groups.start * P, groups.stop * P)
-            nc.vector.quantize_mx(out=d_codes[e][:, cols].bitcast(E5), scales=d_scales[e][:, cols], in_=src)
-
-        def scores(g, c, first_t=PACK - 1):
+        def weights(dst, g, c, first_t=PACK - 1):
             cols = slice(c * CH, (c + 1) * CH)
-            bank = score_psum.tile([P, PACK, CH], F32, name="scores")
+            bank = psum.tile([P, PACK, CH], F32, name="scores", tag="bank")
             for t in [(first_t + i) % PACK for i in range(PACK)]:
                 nc.tensor.matmul_mx(
                     out=bank[:, t, :],
@@ -166,70 +147,60 @@ def tile_attend_gat_v_kernel(tc, qT, kT, rw, dom, offs, out):
                     start=True,
                     stop=True,
                 )
-            return bank
-
-        def gated_tile(pool=gated_pool):
-            return pool.tile([P, PACK, GATED_ROW], F32, name="gated", tag="gated", align_bytes=64)
-
-        def gate_scores(g, bank, gated, places=range(PACK), width=CH):
-            for t in places:
-                nc.scalar.activation(
-                    out=gated[:, t, :width], in_=bank[:, t, :width], func=COPY, scale=gate[:, g, t : t + 1]
-                )
-
-        def weights(dst, bank, gated, width=CH):
+            gated = gated_pool.tile([P, PACK, GATED_ROW], F32, name="gated", align_bytes=64)
+            for t in range(PACK):
+                nc.scalar.activation(out=gated[:, t, :CH], in_=bank[:, t, :], func=COPY, scale=gate[:, g, t : t + 1])
+            first = (g * 2 + c % 2) * PASS
             nc.vector.scalar_tensor_tensor(
-                out=dst.rearrange("p (n t) -> p n t", t=PACK)[:, :width],
-                in0=bank[:, :, :width].rearrange("p t n -> p n t"),
+                out=dst[:, first : first + PASS].rearrange("p (n t) -> p n t", t=PACK),
+                in0=bank[:].rearrange("p t n -> p n t"),
                 scalar=0.0,
-                in1=gated[:, :, :width].rearrange("p t n -> p n t"),
+                in1=gated[:, :, :CH].rearrange("p t n -> p n t"),
                 op0=MAX,
                 op1=MULT,
             )
 
-        def whole_bank(dst, g, c, first_t=PACK - 1, pool=gated_pool):
-            bank = scores(g, c, first_t)
-            gated = gated_tile(pool)
-            gate_scores(g, bank, gated)
-            weights(dst, bank, gated)
+        def product(e, halves, groups=(0, 1)):
+            acc = psum.tile([P, len(halves), HALF], F32, name="acc", tag="bank")
+            for i, h in enumerate(halves):
+                for g in groups:
+                    nc.tensor.matmul_mx(
+                        out=acc[:, i, :],
+                        lhsT=d_codes[e][:, g * P : (g + 1) * P].bitcast(E5),
+                        lhsT_scale=d_scales[e][:, g * P : (g + 1) * P],
+                        rhs=w_codes[h][:, g * HALF : (g + 1) * HALF].bitcast(E4),
+                        rhs_scale=w_scales[h][:, g * HALF : (g + 1) * HALF],
+                        start=(g == groups[0]),
+                        stop=(g == groups[-1]),
+                    )
+            return acc[:].rearrange("p h n -> p (h n)")
 
-        def quant_w(g, lo, src):
-            nc.vector.quantize_mx(
-                out=w_codes[g][:, lo : lo + HALF].bitcast(E4), scales=w_scales[g][:, lo : lo + HALF], in_=src
-            )
+        def to_sbuf(engine, acc, dense):
+            if engine == "scalar":
+                nc.scalar.activation(out=dense, in_=acc, func=COPY)
+            else:
+                nc.vector.tensor_copy(out=dense, in_=acc)
+            return dense
 
-        def product(e, first, groups=(0, 1)):
-            acc = sum_psum.tile([P, N], F32, name="acc")
-            for g in groups:
-                nc.tensor.matmul_mx(
-                    out=acc[:],
-                    lhsT=d_codes[e][:, g * P : (g + 1) * P].bitcast(E5),
-                    lhsT_scale=d_scales[e][:, g * P : (g + 1) * P],
-                    rhs=w_codes[g][:, first : first + N].bitcast(E4),
-                    rhs_scale=w_scales[g][:, first : first + N],
-                    start=(g == groups[0]),
-                    stop=(g == groups[-1]),
-                )
-            return acc
-
-        def to_sbuf(acc, width, dense=None):
-            if dense is None:
-                dense = dense_pool.tile([P, N], F32, name="dense")
-            nc.scalar.activation(out=dense[:, :width], in_=acc[:, :width], func=COPY)
-            return dense[:, :width]
-
-        def scatter(e, src, lo, hi):
-            nc.vector.tensor_copy(out=windows[e][:].indirect(entries(lo, hi)), in_=src)
+        def scatter(engine, e, src, lo, hi):
+            target = windows[e][:].indirect(entries(lo, hi))
+            if engine == "scalar":
+                nc.scalar.activation(out=target, in_=src, func=COPY)
+            else:
+                nc.vector.tensor_copy(out=target, in_=src)
 
         def store(e, queue=nc.sync):
             queue.dma_start(out=out[e * P : (e + 1) * P, :], in_=windows[e][:])
 
+        def dense_tile(name, width):
+            return keep.tile([P, width], F32, name=name)[:]
+
         for j in range(PACK - 1):
             gather(j, 0, N)
-        gather(PACK - 1, HALF, N)
         gather(PACK - 1, 0, HALF)
-        quant_k(HALF, N)
+        gather(PACK - 1, HALF, N)
         quant_k(0, HALF)
+        quant_k(HALF, N)
 
         (_, second), (_, third), _ = Q_LOADS
         cast_q(0, second, "vector", LOW_PLACES)
@@ -244,80 +215,44 @@ def tile_attend_gat_v_kernel(tc, qT, kT, rw, dom, offs, out):
         cast_q(third, R, "vector", HIGH_PLACES)
         quant_q(1, P // 2, P)
 
-        w_upper = [
-            after_queries.tile([P, 2 * PASS], BF16, name="w_upper0", tag="shared", align_bytes=64),
-            keep.tile([P, 2 * PASS], BF16, name="w_upper1", align_bytes=64),
-        ]
-        w_lower = [cells(5, 2), cells(4, 2)]
-        positive = keep.tile([P, SIDE, PACK], F32, name="positive")
-        squares = after_side.tile([P, SIDE, PACK], F32, name="squares", align_bytes=64, offset=0)
-
-        first_pair = cells(1, PACK).rearrange("p (h c e j) -> p h c e j", h=2, c=2, j=PACK)[:, :, 0]
-        cast("gpsimd", first_pair, d_raw[0][0][:].rearrange("p j (h e) -> p h e j", h=2))
-        cast(
-            "gpsimd",
-            d_bf[0, 1].rearrange("p (e j) -> p e j", j=PACK),
-            d_raw[0][1][:, :, :P].rearrange("p j e -> p e j"),
-        )
-        whole_bank(w_upper[0][:, :PASS], 0, 2, first_t=0)
-        whole_bank(w_upper[0][:, PASS:], 0, 3)
-        whole_bank(w_lower[0][:, :PASS], 0, 0)
-        later_bank = scores(0, 1)
-        later_gated = gated_tile()
-        gate_scores(0, later_bank, later_gated, range(PACK)[LOW_PLACES])
-        whole_bank(w_upper[1][:, :PASS], 1, 2, first_t=0, pool=after_bank)
-        whole_bank(w_upper[1][:, PASS:], 1, 3)
-
-        held_scales = after_bank.tile([P, N + HALF + G * P], U8, name="held_scales", tag="gated", align_bytes=64)
-        w_scales.update({0: held_scales[:, : N + HALF]})
-        d_scales.update({0: held_scales[:, N + HALF :]})
-        nc.gpsimd.memset(w_scales[0][:, N:].bitcast(U32), 0)
+        w_early = chained([P, G * 2 * PASS], BF16, "w_early")
+        w_late = keep.tile([P, G * 2 * PASS], BF16, name="w_late", align_bytes=64)
+        d_pair = cells(1, PACK).rearrange("p (e g c j) -> p g e c j", e=2, g=G, j=PACK)
         for g in range(G):
-            quant_d(0, slice(g, g + 1), d_bf[0, g])
-            quant_w(g, HALF, w_upper[g][:])
+            cast("gpsimd", d_pair[:, g], d_raw[0][g][:].rearrange("p j (e c) -> p e c j", e=2))
+        weights(w_early, 0, 0, first_t=0)
+        weights(w_early, 0, 1)
+        weights(w_late, 0, 2)
+        weights(w_early, 1, 0, first_t=0)
+        weights(w_early, 1, 1)
+        quant_d(0, cells(1, 2))
+        quantise(w_codes[EARLY][:], w_scales[EARLY][:], w_early[:])
+        d_bf2 = chained([P, G * PASS], BF16, "d_bf2")
+        cast_d(2, d_bf2)
+        weights(w_late, 1, 2)
+        weights(w_late, 1, 3)
+        weights(w_late, 0, 3)
+        scatter("scalar", 0, to_sbuf("scalar", product(0, [EARLY]), dense_tile("dense0e", HALF)), 0, HALF)
+        for g in (1, 0):
+            cols = slice(g * HALF, (g + 1) * HALF)
+            quantise(w_codes[LATE][:, cols], w_scales[LATE][:, cols], w_late[:, g * 2 * PASS : (g + 1) * 2 * PASS])
+        first_late = product(0, [LATE], groups=(1, 0))
+        quant_d(1, cells(3, 2))
+        quant_d(2, d_bf2[:])
+        d_bf3 = chained([P, G * PASS], BF16, "d_bf3")
+        cast_d(3, d_bf3)
 
-        gate_scores(0, later_bank, later_gated, range(PACK)[HIGH_PLACES])
-        weights(w_lower[0][:, PASS:], later_bank, later_gated)
-        cast_d(1, 1, d_bf[1, 1])
-        side_bank = scores(1, 1)
-        nc.scalar.activation(out=positive[:, CH - KEPT :], in_=side_bank[:].rearrange("p t n -> p n t"), func=RELU)
-        shared_bank = scores(1, 0)
-        nc.scalar.activation(
-            out=positive[:, : CH - KEPT], in_=shared_bank[:, :, KEPT:].rearrange("p t n -> p n t"), func=RELU
-        )
-        shared_gated = gated_tile()
-        gate_scores(1, shared_bank, shared_gated, width=KEPT)
-        nc.scalar.activation(out=squares[:], in_=positive[:], func=SQUARE)
-        quant_d(1, BOTH, cells(3, 2))
-        quant_w(0, 0, w_lower[0])
-        weights(w_lower[1][:, :PASS], shared_bank, shared_gated, KEPT)
-        nc.gpsimd.tensor_tensor(
-            out=w_lower[1].rearrange("p (n t) -> p n t", t=PACK)[:, KEPT:],
-            in0=squares[:],
-            in1=side_gate[:].to_broadcast([P, SIDE, PACK]),
-            op=MULT,
-        )
-
-        scatter(0, to_sbuf(product(0, HALF), HALF), HALF, N)
-        for g in range(G):
-            cast_d(2, g, d_bf2[:, g * PASS : (g + 1) * PASS])
-        quant_w(1, 0, w_lower[1])
-        upper_bytes = HALF * 4
-        d_scales.update({2: after_side.tile([P, G * P], U8, name="d_scales2", align_bytes=64, offset=upper_bytes)})
-        quant_d(2, BOTH, d_bf2[:])
-        second_upper = after_side.tile([P, HALF], F32, name="second_upper", align_bytes=64, offset=0)
-        scatter(1, to_sbuf(product(1, HALF), HALF, second_upper), HALF, N)
-        lower = [product(0, 0), product(1, 0, groups=(1, 0))]
-        d_bf3 = after_side.tile([P, G * PASS], BF16, name="d_bf3", align_bytes=64, offset=upper_bytes + G * P)
-        for g in range(G):
-            cast_d(3, g, d_bf3[:, g * PASS : (g + 1) * PASS])
-        first_lower = to_sbuf(lower[0], HALF)
-        quant_d(3, BOTH, d_bf3[:])
-        scatter(0, first_lower, 0, HALF)
+        scatter("vector", 0, to_sbuf("scalar", first_late, dense_tile("dense0l", HALF)), HALF, N)
         store(0)
-        scatter(1, to_sbuf(lower[1], HALF), 0, HALF)
+        for h in (EARLY, LATE):
+            dense = to_sbuf("scalar", product(1, [h]), dense_tile("dense1%d" % h, HALF))
+            scatter("scalar", 1, dense, h * HALF, (h + 1) * HALF)
         store(1)
-        scatter(2, to_sbuf(product(2, 0), N), 0, N)
+        third_sums = product(2, [EARLY, LATE])
+        quant_d(3, d_bf3[:])
+        scatter("vector", 2, to_sbuf("vector", third_sums, chained([P, N], F32, "dense2")[:]), 0, N)
         store(2)
-        scatter(3, to_sbuf(product(3, 0), N), 0, N)
+        dense3 = to_sbuf("scalar", product(3, [EARLY, LATE]), dense_tile("dense3", N))
+        for h in (EARLY, LATE):
+            scatter("scalar", 3, dense3[:, h * HALF : (h + 1) * HALF], h * HALF, (h + 1) * HALF)
         store(3, nc.scalar)

@@ -49,6 +49,8 @@ def tile_attend_gat_v_kernel(tc, qT, kT, rw, dom, offs, out):
         keep = ctx.enter_context(tc.tile_pool(name="keep", bufs=1))
         gated_pool = ctx.enter_context(tc.tile_pool(name="gated_pool", bufs=4))
         chain = ctx.enter_context(tc.tile_pool(name="chain", bufs=1))
+        after_late = ctx.enter_context(tc.tile_pool(name="after_late", bufs=1))
+        after_bank = ctx.enter_context(tc.tile_pool(name="after_bank", bufs=1))
         psum = ctx.enter_context(tc.psum_pool(name="psum", bufs=8))
 
         def chained(shape, dtype, name):
@@ -95,9 +97,9 @@ def tile_attend_gat_v_kernel(tc, qT, kT, rw, dom, offs, out):
         q_codes = [keep.tile([P, PASS], U32, name="q_codes%d" % g, align_bytes=64) for g in range(G)]
         q_scales = [keep.tile([P, PASS], U8, name="q_scales%d" % g, align_bytes=64) for g in range(G)]
         w_codes = [keep.tile([P, G * HALF], U32, name="w_codes%d" % h, align_bytes=64) for h in range(2)]
-        w_scales = [keep.tile([P, G * HALF], U8, name="w_scales%d" % h, align_bytes=64) for h in range(2)]
+        w_scales = [keep.tile([P, G * HALF], U8, name="w_scales_early", align_bytes=64)]
         d_codes = [keep.tile([P, G * P], U32, name="d_codes%d" % e, align_bytes=64) for e in range(VALUE_TILES)]
-        d_scales = [keep.tile([P, G * P], U8, name="d_scales%d" % e, align_bytes=64) for e in range(VALUE_TILES)]
+        d_scales = {e: keep.tile([P, G * P], U8, name="d_scales%d" % e, align_bytes=64)[:] for e in (0, 3)}
 
         def entries(lo, hi):
             return offsets[:, lo // PER_COLUMN : hi // PER_COLUMN]
@@ -124,7 +126,7 @@ def tile_attend_gat_v_kernel(tc, qT, kT, rw, dom, offs, out):
                 quantise(q_codes[g][:, cols], q_scales[g][:, cols], q_bf[g][:, t, lo:hi, :].rearrange("p m j -> p (m j)"))
 
         def quant_d(e, src):
-            quantise(d_codes[e][:], d_scales[e][:], src, E5)
+            quantise(d_codes[e][:], d_scales[e], src, E5)
 
         def cast_d(e, dst):
             for g in range(G):
@@ -134,7 +136,7 @@ def tile_attend_gat_v_kernel(tc, qT, kT, rw, dom, offs, out):
                     d_raw[e // 2][g][:, :, e % 2 * P : (e % 2 + 1) * P].rearrange("p j e -> p e j"),
                 )
 
-        def weights(dst, g, c, first_t=PACK - 1):
+        def weights(dst, g, c, first_t=PACK - 1, pool=gated_pool):
             cols = slice(c * CH, (c + 1) * CH)
             bank = psum.tile([P, PACK, CH], F32, name="scores", tag="bank")
             for t in [(first_t + i) % PACK for i in range(PACK)]:
@@ -147,7 +149,7 @@ def tile_attend_gat_v_kernel(tc, qT, kT, rw, dom, offs, out):
                     start=True,
                     stop=True,
                 )
-            gated = gated_pool.tile([P, PACK, GATED_ROW], F32, name="gated", align_bytes=64)
+            gated = pool.tile([P, PACK, GATED_ROW], F32, name="gated", tag="gated", align_bytes=64)
             for t in range(PACK):
                 nc.scalar.activation(out=gated[:, t, :CH], in_=bank[:, t, :], func=COPY, scale=gate[:, g, t : t + 1])
             first = (g * 2 + c % 2) * PASS
@@ -160,20 +162,27 @@ def tile_attend_gat_v_kernel(tc, qT, kT, rw, dom, offs, out):
                 op1=MULT,
             )
 
-        def product(e, halves, groups=(0, 1)):
-            acc = psum.tile([P, len(halves), HALF], F32, name="acc", tag="bank")
-            for i, h in enumerate(halves):
-                for g in groups:
-                    nc.tensor.matmul_mx(
-                        out=acc[:, i, :],
-                        lhsT=d_codes[e][:, g * P : (g + 1) * P].bitcast(E5),
-                        lhsT_scale=d_scales[e][:, g * P : (g + 1) * P],
-                        rhs=w_codes[h][:, g * HALF : (g + 1) * HALF].bitcast(E4),
-                        rhs_scale=w_scales[h][:, g * HALF : (g + 1) * HALF],
-                        start=(g == groups[0]),
-                        stop=(g == groups[-1]),
-                    )
-            return acc[:].rearrange("p h n -> p (h n)")
+        def product(e, h, groups=(0, 1), lo=0, hi=HALF, acc=None):
+            if acc is None:
+                acc = psum.tile([P, hi - lo], F32, name="acc", tag="bank")[:]
+            for g in groups:
+                cols = slice(g * HALF + lo, g * HALF + hi)
+                nc.tensor.matmul_mx(
+                    out=acc,
+                    lhsT=d_codes[e][:, g * P : (g + 1) * P].bitcast(E5),
+                    lhsT_scale=d_scales[e][:, g * P : (g + 1) * P],
+                    rhs=w_codes[h][:, cols].bitcast(E4),
+                    rhs_scale=w_scales[h][:, cols],
+                    start=(g == groups[0]),
+                    stop=(g == groups[-1]),
+                )
+            return acc
+
+        def whole_product(e):
+            acc = psum.tile([P, N], F32, name="acc", tag="bank")
+            for h in (EARLY, LATE):
+                product(e, h, acc=acc[:, h * HALF : (h + 1) * HALF])
+            return acc[:]
 
         def to_sbuf(engine, acc, dense):
             if engine == "scalar":
@@ -216,7 +225,11 @@ def tile_attend_gat_v_kernel(tc, qT, kT, rw, dom, offs, out):
         quant_q(1, P // 2, P)
 
         w_early = chained([P, G * 2 * PASS], BF16, "w_early")
-        w_late = keep.tile([P, G * 2 * PASS], BF16, name="w_late", align_bytes=64)
+        w_late = after_late.tile([P, G * 2 * PASS], BF16, name="w_late", tag="late", align_bytes=64)
+
+        def quant_late(lo, hi):
+            quantise(w_codes[LATE][:, lo:hi], w_scales[LATE][:, lo:hi], w_late[:, lo * PACK : hi * PACK])
+
         d_pair = cells(1, PACK).rearrange("p (e g c j) -> p g e c j", e=2, g=G, j=PACK)
         for g in range(G):
             cast("gpsimd", d_pair[:, g], d_raw[0][g][:].rearrange("p j (e c) -> p e c j", e=2))
@@ -230,29 +243,35 @@ def tile_attend_gat_v_kernel(tc, qT, kT, rw, dom, offs, out):
         d_bf2 = chained([P, G * PASS], BF16, "d_bf2")
         cast_d(2, d_bf2)
         weights(w_late, 1, 2)
-        weights(w_late, 1, 3)
+        weights(w_late, 1, 3, pool=after_bank)
+        w_scales.append(after_bank.tile([P, G * HALF], U8, name="w_scales_late", tag="gated", align_bytes=64))
         weights(w_late, 0, 3)
-        scatter("scalar", 0, to_sbuf("scalar", product(0, [EARLY]), dense_tile("dense0e", HALF)), 0, HALF)
-        for g in (1, 0):
-            cols = slice(g * HALF, (g + 1) * HALF)
-            quantise(w_codes[LATE][:, cols], w_scales[LATE][:, cols], w_late[:, g * 2 * PASS : (g + 1) * 2 * PASS])
-        first_late = product(0, [LATE], groups=(1, 0))
+        scatter("scalar", 0, to_sbuf("scalar", product(0, EARLY), dense_tile("dense0e", HALF)), 0, HALF)
+        quant_late(HALF, 2 * HALF)
+        quant_late(0, CH)
+        quant_late(CH, HALF)
+        first_late = [product(0, LATE, (1, 0), lo, lo + CH) for lo in (0, CH)]
+        held_scales = after_late.tile([P, 2 * G * P], U8, name="held_scales", tag="late", align_bytes=64)
+        d_scales.update({1: held_scales[:, : G * P], 2: held_scales[:, G * P :]})
+        dense = dense_tile("dense0l", HALF)
+        for i, acc in enumerate(first_late):
+            to_sbuf("vector", acc, dense[:, i * CH : (i + 1) * CH])
         quant_d(1, cells(3, 2))
         quant_d(2, d_bf2[:])
         d_bf3 = chained([P, G * PASS], BF16, "d_bf3")
         cast_d(3, d_bf3)
 
-        scatter("vector", 0, to_sbuf("scalar", first_late, dense_tile("dense0l", HALF)), HALF, N)
+        scatter("vector", 0, dense, HALF, N)
         store(0)
         for h in (EARLY, LATE):
-            dense = to_sbuf("scalar", product(1, [h]), dense_tile("dense1%d" % h, HALF))
+            dense = to_sbuf("scalar", product(1, h), dense_tile("dense1%d" % h, HALF))
             scatter("scalar", 1, dense, h * HALF, (h + 1) * HALF)
         store(1)
-        third_sums = product(2, [EARLY, LATE])
+        third_sums = whole_product(2)
         quant_d(3, d_bf3[:])
         scatter("vector", 2, to_sbuf("vector", third_sums, chained([P, N], F32, "dense2")[:]), 0, N)
         store(2)
-        dense3 = to_sbuf("scalar", product(3, [EARLY, LATE]), dense_tile("dense3", N))
+        dense3 = to_sbuf("scalar", whole_product(3), dense_tile("dense3", N))
         for h in (EARLY, LATE):
             scatter("scalar", 3, dense3[:, h * HALF : (h + 1) * HALF], h * HALF, (h + 1) * HALF)
         store(3, nc.scalar)

@@ -51,6 +51,7 @@ def tile_attend_gat_v_kernel(tc, qT, kT, rw, dom, offs, out):
         chain = ctx.enter_context(tc.tile_pool(name="chain", bufs=1))
         after_late = ctx.enter_context(tc.tile_pool(name="after_late", bufs=1))
         after_bank = ctx.enter_context(tc.tile_pool(name="after_bank", bufs=1))
+        after_scatter = ctx.enter_context(tc.tile_pool(name="after_scatter", bufs=1))
         psum = ctx.enter_context(tc.psum_pool(name="psum", bufs=8))
 
         def chained(shape, dtype, name):
@@ -88,7 +89,7 @@ def tile_attend_gat_v_kernel(tc, qT, kT, rw, dom, offs, out):
         k_codes = keep.tile([P, N], U32, name="k_codes", align_bytes=64)
         k_scales = keep.tile([P, N], U8, name="k_scales", align_bytes=64)
         q_bf0 = keep.tile([P, PACK * PASS], BF16, name="q_bf0", align_bytes=64)
-        arena = keep.tile([P, 5 * PASS], BF16, name="arena", align_bytes=64)
+        arena = keep.tile([P, 4 * PASS], BF16, name="arena", align_bytes=64)
 
         def cells(first, count=1):
             return arena[:, first * PASS : (first + count) * PASS]
@@ -99,7 +100,7 @@ def tile_attend_gat_v_kernel(tc, qT, kT, rw, dom, offs, out):
         w_codes = [keep.tile([P, G * HALF], U32, name="w_codes%d" % h, align_bytes=64) for h in range(2)]
         w_scales = [keep.tile([P, G * HALF], U8, name="w_scales_early", align_bytes=64)]
         d_codes = [keep.tile([P, G * P], U32, name="d_codes%d" % e, align_bytes=64) for e in range(VALUE_TILES)]
-        d_scales = {e: keep.tile([P, G * P], U8, name="d_scales%d" % e, align_bytes=64)[:] for e in (0, 3)}
+        d_scales = {e: keep.tile([P, G * P], U8, name="d_scales%d" % e, align_bytes=64) for e in (0, 3)}
 
         def entries(lo, hi):
             return offsets[:, lo // PER_COLUMN : hi // PER_COLUMN]
@@ -125,18 +126,22 @@ def tile_attend_gat_v_kernel(tc, qT, kT, rw, dom, offs, out):
                 cols = slice(t * P + lo, t * P + hi)
                 quantise(q_codes[g][:, cols], q_scales[g][:, cols], q_bf[g][:, t, lo:hi, :].rearrange("p m j -> p (m j)"))
 
-        def quant_d(e, src):
-            quantise(d_codes[e][:], d_scales[e], src, E5)
+        def quant_d(e, src, first=0, groups=G):
+            cols = slice(first * P, (first + groups) * P)
+            quantise(d_codes[e][:, cols], d_scales[e][:, cols], src, E5)
 
-        def cast_d(e, dst):
-            for g in range(G):
+        def cast_d(engine, e, g, dst):
+            src = d_raw[e // 2][g][:, :, e % 2 * P : (e % 2 + 1) * P]
+            if engine == "scalar":
                 cast(
-                    "gpsimd",
-                    dst[:, g * PASS : (g + 1) * PASS].rearrange("p (e j) -> p e j", j=PACK),
-                    d_raw[e // 2][g][:, :, e % 2 * P : (e % 2 + 1) * P].rearrange("p j e -> p e j"),
+                    engine,
+                    dst.rearrange("p (c i j) -> p c j i", i=PACK, j=PACK),
+                    src.rearrange("p j (c i) -> p c j i", i=PACK),
                 )
+            else:
+                cast(engine, dst.rearrange("p (e j) -> p e j", j=PACK), src.rearrange("p j e -> p e j"))
 
-        def weights(dst, g, c, first_t=PACK - 1, pool=gated_pool):
+        def scores(g, c, first_t=PACK - 1):
             cols = slice(c * CH, (c + 1) * CH)
             bank = psum.tile([P, PACK, CH], F32, name="scores", tag="bank")
             for t in [(first_t + i) % PACK for i in range(PACK)]:
@@ -149,6 +154,10 @@ def tile_attend_gat_v_kernel(tc, qT, kT, rw, dom, offs, out):
                     start=True,
                     stop=True,
                 )
+            return bank
+
+        def weights(dst, g, c, first_t=PACK - 1, pool=gated_pool):
+            bank = scores(g, c, first_t)
             gated = pool.tile([P, PACK, GATED_ROW], F32, name="gated", tag="gated", align_bytes=64)
             for t in range(PACK):
                 nc.scalar.activation(out=gated[:, t, :CH], in_=bank[:, t, :], func=COPY, scale=gate[:, g, t : t + 1])
@@ -225,14 +234,14 @@ def tile_attend_gat_v_kernel(tc, qT, kT, rw, dom, offs, out):
         quant_q(1, P // 2, P)
 
         w_early = chained([P, G * 2 * PASS], BF16, "w_early")
-        w_late = after_late.tile([P, G * 2 * PASS], BF16, name="w_late", tag="late", align_bytes=64)
+        w_late = after_late.tile([P, G * 2 * PASS], BF16, name="w_late", align_bytes=64, offset=0)
 
         def quant_late(lo, hi):
             quantise(w_codes[LATE][:, lo:hi], w_scales[LATE][:, lo:hi], w_late[:, lo * PACK : hi * PACK])
 
-        d_pair = cells(1, PACK).rearrange("p (e g c j) -> p g e c j", e=2, g=G, j=PACK)
-        for g in range(G):
-            cast("gpsimd", d_pair[:, g], d_raw[0][g][:].rearrange("p j (e c) -> p e c j", e=2))
+        first_pair = cells(0, PACK).rearrange("p (e x c j) -> p x e c j", e=2, x=2, j=PACK)[:, 1]
+        cast("gpsimd", first_pair, d_raw[0][0][:].rearrange("p j (e c) -> p e c j", e=2))
+        cast_d("gpsimd", 0, 1, cells(2))
         weights(w_early, 0, 0, first_t=0)
         weights(w_early, 0, 1)
         weights(w_late, 0, 2)
@@ -240,36 +249,44 @@ def tile_attend_gat_v_kernel(tc, qT, kT, rw, dom, offs, out):
         weights(w_early, 1, 1)
         quant_d(0, cells(1, 2))
         quantise(w_codes[EARLY][:], w_scales[EARLY][:], w_early[:])
-        d_bf2 = chained([P, G * PASS], BF16, "d_bf2")
-        cast_d(2, d_bf2)
+        d_next = chained([P, 2 * PASS], BF16, "d_next")
+        cast_d("gpsimd", 1, 1, d_next[:, :PASS])
+        cast_d("gpsimd", 2, 1, d_next[:, PASS:])
         weights(w_late, 1, 2)
         weights(w_late, 1, 3, pool=after_bank)
         w_scales.append(after_bank.tile([P, G * HALF], U8, name="w_scales_late", tag="gated", align_bytes=64))
         weights(w_late, 0, 3)
+        d_bf20 = keep.tile([P, PASS], BF16, name="d_bf20", align_bytes=64)
+        cast_d("scalar", 2, 0, d_bf20[:])
         scatter("scalar", 0, to_sbuf("scalar", product(0, EARLY), dense_tile("dense0e", HALF)), 0, HALF)
         quant_late(HALF, 2 * HALF)
         quant_late(0, CH)
         quant_late(CH, HALF)
         first_late = [product(0, LATE, (1, 0), lo, lo + CH) for lo in (0, CH)]
-        held_scales = after_late.tile([P, 2 * G * P], U8, name="held_scales", tag="late", align_bytes=64)
-        d_scales.update({1: held_scales[:, : G * P], 2: held_scales[:, G * P :]})
-        dense = dense_tile("dense0l", HALF)
+        for e in (1, 2):
+            d_scales.update({e: after_late.tile([P, G * P], U8, name="d_scales%d" % e, align_bytes=64, offset=e * G * P)})
+        quant_d(1, cells(3), 0, 1)
+        quant_d(1, d_next[:, :PASS], 1, 1)
+        quant_d(2, d_bf20[:], 0, 1)
+        quant_d(2, d_next[:, PASS:], 1, 1)
+        dense = after_scatter.tile([P, HALF], F32, name="dense0l", tag="dense", align_bytes=64)[:]
         for i, acc in enumerate(first_late):
             to_sbuf("vector", acc, dense[:, i * CH : (i + 1) * CH])
-        quant_d(1, cells(3, 2))
-        quant_d(2, d_bf2[:])
-        d_bf3 = chained([P, G * PASS], BF16, "d_bf3")
-        cast_d(3, d_bf3)
+        d_bf3 = [chained([P, PASS], BF16, "d_bf30")]
+        cast_d("vector", 3, 0, d_bf3[0][:])
 
         scatter("vector", 0, dense, HALF, N)
         store(0)
+        d_bf3.append(after_scatter.tile([P, PASS], BF16, name="d_bf31", tag="dense", align_bytes=64))
+        cast_d("vector", 3, 1, d_bf3[1][:])
         for h in (EARLY, LATE):
             dense = to_sbuf("scalar", product(1, h), dense_tile("dense1%d" % h, HALF))
             scatter("scalar", 1, dense, h * HALF, (h + 1) * HALF)
         store(1)
-        third_sums = whole_product(2)
-        quant_d(3, d_bf3[:])
-        scatter("vector", 2, to_sbuf("vector", third_sums, chained([P, N], F32, "dense2")[:]), 0, N)
+        dense2 = to_sbuf("vector", whole_product(2), dense_tile("dense2", N))
+        for g in range(G):
+            quant_d(3, d_bf3[g][:], g, 1)
+        scatter("vector", 2, dense2, 0, N)
         store(2)
         dense3 = to_sbuf("scalar", whole_product(3), dense_tile("dense3", N))
         for h in (EARLY, LATE):

@@ -51,7 +51,7 @@ def tile_attend_gat_v_kernel(tc, qT, kT, rw, dom, offs, out):
         chain = ctx.enter_context(tc.tile_pool(name="chain", bufs=1))
         after_late = ctx.enter_context(tc.tile_pool(name="after_late", bufs=1))
         after_bank = ctx.enter_context(tc.tile_pool(name="after_bank", bufs=1))
-        after_scatter = ctx.enter_context(tc.tile_pool(name="after_scatter", bufs=1))
+        after_early = ctx.enter_context(tc.tile_pool(name="after_early", bufs=1))
         psum = ctx.enter_context(tc.psum_pool(name="psum", bufs=8))
 
         def chained(shape, dtype, name):
@@ -98,9 +98,10 @@ def tile_attend_gat_v_kernel(tc, qT, kT, rw, dom, offs, out):
         q_codes = [keep.tile([P, PASS], U32, name="q_codes%d" % g, align_bytes=64) for g in range(G)]
         q_scales = [keep.tile([P, PASS], U8, name="q_scales%d" % g, align_bytes=64) for g in range(G)]
         w_codes = [keep.tile([P, G * HALF], U32, name="w_codes%d" % h, align_bytes=64) for h in range(2)]
-        w_scales = [keep.tile([P, G * HALF], U8, name="w_scales_early", align_bytes=64)]
+        w_scales = []
         d_codes = [keep.tile([P, G * P], U32, name="d_codes%d" % e, align_bytes=64) for e in range(VALUE_TILES)]
-        d_scales = {e: keep.tile([P, G * P], U8, name="d_scales%d" % e, align_bytes=64) for e in (0, 3)}
+        d_scales0 = keep.tile([P, G * P], U8, name="d_scales0", align_bytes=64)
+        d_scales = {(0, g): d_scales0[:, g * P :] for g in range(G)}
 
         def entries(lo, hi):
             return offsets[:, lo // PER_COLUMN : hi // PER_COLUMN]
@@ -128,7 +129,7 @@ def tile_attend_gat_v_kernel(tc, qT, kT, rw, dom, offs, out):
 
         def quant_d(e, src, first=0, groups=G):
             cols = slice(first * P, (first + groups) * P)
-            quantise(d_codes[e][:, cols], d_scales[e][:, cols], src, E5)
+            quantise(d_codes[e][:, cols], d_scales[e, first][:, : groups * P], src, E5)
 
         def cast_d(engine, e, g, dst):
             src = d_raw[e // 2][g][:, :, e % 2 * P : (e % 2 + 1) * P]
@@ -171,7 +172,7 @@ def tile_attend_gat_v_kernel(tc, qT, kT, rw, dom, offs, out):
                 op1=MULT,
             )
 
-        def product(e, h, groups=(0, 1), lo=0, hi=HALF, acc=None):
+        def product(e, h, groups=(0, 1), lo=0, hi=HALF, acc=None, first=None, last=None):
             if acc is None:
                 acc = psum.tile([P, hi - lo], F32, name="acc", tag="bank")[:]
             for g in groups:
@@ -179,11 +180,11 @@ def tile_attend_gat_v_kernel(tc, qT, kT, rw, dom, offs, out):
                 nc.tensor.matmul_mx(
                     out=acc,
                     lhsT=d_codes[e][:, g * P : (g + 1) * P].bitcast(E5),
-                    lhsT_scale=d_scales[e][:, g * P : (g + 1) * P],
+                    lhsT_scale=d_scales[e, g][:, :P],
                     rhs=w_codes[h][:, cols].bitcast(E4),
                     rhs_scale=w_scales[h][:, cols],
-                    start=(g == groups[0]),
-                    stop=(g == groups[-1]),
+                    start=(g == (groups[0] if first is None else first)),
+                    stop=(g == (groups[-1] if last is None else last)),
                 )
             return acc
 
@@ -246,9 +247,15 @@ def tile_attend_gat_v_kernel(tc, qT, kT, rw, dom, offs, out):
         weights(w_early, 0, 1)
         weights(w_late, 0, 2)
         weights(w_early, 1, 0, first_t=0)
-        weights(w_early, 1, 1)
+        weights(w_early, 1, 1, pool=after_early)
+        early_scales = after_early.tile([P, G * HALF + P], U8, name="early_scales", tag="gated", align_bytes=64)
+        w_scales.append(early_scales[:, : G * HALF])
+        d_scales.update({(1, 0): early_scales[:, G * HALF :]})
         quant_d(0, cells(1, 2))
-        quantise(w_codes[EARLY][:], w_scales[EARLY][:], w_early[:])
+        quant_d(1, cells(3), 0, 1)
+        for g in range(G):
+            cols = slice(g * HALF, (g + 1) * HALF)
+            quantise(w_codes[EARLY][:, cols], w_scales[EARLY][:, cols], w_early[:, g * 2 * PASS : (g + 1) * 2 * PASS])
         d_next = chained([P, 2 * PASS], BF16, "d_next")
         cast_d("gpsimd", 1, 1, d_next[:, :PASS])
         cast_d("gpsimd", 2, 1, d_next[:, PASS:])
@@ -258,29 +265,32 @@ def tile_attend_gat_v_kernel(tc, qT, kT, rw, dom, offs, out):
         weights(w_late, 0, 3)
         d_bf20 = keep.tile([P, PASS], BF16, name="d_bf20", align_bytes=64)
         cast_d("scalar", 2, 0, d_bf20[:])
-        scatter("scalar", 0, to_sbuf("scalar", product(0, EARLY), dense_tile("dense0e", HALF)), 0, HALF)
+        dense = to_sbuf("scalar", product(0, EARLY), dense_tile("dense0e", HALF))
+        second_early = product(1, EARLY, (0,), last=1)
+        d_bf3 = [keep.tile([P, PASS], BF16, name="d_bf30", align_bytes=64)]
+        cast_d("scalar", 3, 0, d_bf3[0][:])
+        scatter("scalar", 0, dense, 0, HALF)
         quant_late(HALF, 2 * HALF)
         quant_late(0, CH)
         quant_late(CH, HALF)
         first_late = [product(0, LATE, (1, 0), lo, lo + CH) for lo in (0, CH)]
-        for e in (1, 2):
-            d_scales.update({e: after_late.tile([P, G * P], U8, name="d_scales%d" % e, align_bytes=64, offset=e * G * P)})
-        quant_d(1, cells(3), 0, 1)
+        late_scales = after_late.tile([P, 5 * P], U8, name="late_scales", align_bytes=64, offset=0)
+        for i, block in enumerate(((1, 1), (2, 0), (2, 1), (3, 0), (3, 1))):
+            d_scales.update({block: late_scales[:, i * P : (i + 1) * P]})
         quant_d(1, d_next[:, :PASS], 1, 1)
         quant_d(2, d_bf20[:], 0, 1)
         quant_d(2, d_next[:, PASS:], 1, 1)
-        dense = after_scatter.tile([P, HALF], F32, name="dense0l", tag="dense", align_bytes=64)[:]
+        dense = dense_tile("dense0l", HALF)
         for i, acc in enumerate(first_late):
             to_sbuf("vector", acc, dense[:, i * CH : (i + 1) * CH])
-        d_bf3 = [chained([P, PASS], BF16, "d_bf30")]
-        cast_d("vector", 3, 0, d_bf3[0][:])
+        d_bf3.append(chained([P, PASS], BF16, "d_bf31"))
+        cast_d("vector", 3, 1, d_bf3[1][:])
 
         scatter("vector", 0, dense, HALF, N)
         store(0)
-        d_bf3.append(after_scatter.tile([P, PASS], BF16, name="d_bf31", tag="dense", align_bytes=64))
-        cast_d("vector", 3, 1, d_bf3[1][:])
+        second = [product(1, EARLY, (1,), acc=second_early, first=0), product(1, LATE)]
         for h in (EARLY, LATE):
-            dense = to_sbuf("scalar", product(1, h), dense_tile("dense1%d" % h, HALF))
+            dense = to_sbuf(("scalar", "vector")[h], second[h], dense_tile("dense1%d" % h, HALF))
             scatter("scalar", 1, dense, h * HALF, (h + 1) * HALF)
         store(1)
         dense2 = to_sbuf("vector", whole_product(2), dense_tile("dense2", N))
@@ -288,7 +298,7 @@ def tile_attend_gat_v_kernel(tc, qT, kT, rw, dom, offs, out):
             quant_d(3, d_bf3[g][:], g, 1)
         scatter("vector", 2, dense2, 0, N)
         store(2)
-        dense3 = to_sbuf("scalar", whole_product(3), dense_tile("dense3", N))
+        dense3 = [to_sbuf("scalar", product(3, h), dense_tile("dense3%d" % h, HALF)) for h in (EARLY, LATE)]
         for h in (EARLY, LATE):
-            scatter("scalar", 3, dense3[:, h * HALF : (h + 1) * HALF], h * HALF, (h + 1) * HALF)
+            scatter("scalar", 3, dense3[h], h * HALF, (h + 1) * HALF)
         store(3, nc.scalar)

@@ -32,6 +32,7 @@ Q_LOADS = ((0, 512), (512, 768), (768, 1024))
 FIRST_SHARE = 352
 SECOND_SHARE = 96
 GATED_ROW = CH + 1
+KEY_SHARE = 320
 
 
 def tile_attend_gat_v_kernel(tc, qT, kT, rw, dom, offs, out):
@@ -66,7 +67,7 @@ def tile_attend_gat_v_kernel(tc, qT, kT, rw, dom, offs, out):
         gate_raw = keep.tile([P, G, 2 * PACK], F32, name="gate_raw")
         gate = keep.tile([P, G, PACK], F32, name="gate")
         d_rows = dom[0].rearrange("(g p j) e -> g p j e", p=P, j=PACK)
-        d_raw = [[keep.tile([P, PACK, 2 * P], F32, name="d_raw%d%d" % (pair, g)) for g in range(G)] for pair in range(2)]
+        d_raw = [keep.tile([P, PACK, DV], F32, name="d_raw%d" % g) for g in range(G)]
         windows = [keep.tile([P, T], F32, name="window%d" % e) for e in range(VALUE_TILES)]
 
         nc.sync.dma_start(out=k_planes[0][:], in_=k_rows[:, 0, :])
@@ -78,7 +79,8 @@ def tile_attend_gat_v_kernel(tc, qT, kT, rw, dom, offs, out):
             nc.sync.dma_start(out=raw[:], in_=q_rows[:, :, lo:hi])
         for pair in range(2):
             for g in range(G):
-                nc.sync.dma_start(out=d_raw[pair][g][:], in_=d_rows[g, :, :, pair * 2 * P : (pair + 1) * 2 * P])
+                cols = slice(pair * 2 * P, (pair + 1) * 2 * P)
+                nc.sync.dma_start(out=d_raw[g][:, :, cols], in_=d_rows[g, :, :, cols])
 
         for window in windows:
             nc.gpsimd.memset(window[:], 0.0)
@@ -131,8 +133,8 @@ def tile_attend_gat_v_kernel(tc, qT, kT, rw, dom, offs, out):
             cols = slice(first * P, (first + groups) * P)
             quantise(d_codes[e][:, cols], d_scales[e, first][:, : groups * P], src, E5)
 
-        def cast_d(engine, e, g, dst):
-            src = d_raw[e // 2][g][:, :, e % 2 * P : (e % 2 + 1) * P]
+        def cast_d(engine, e, g, dst, tiles=1):
+            src = d_raw[g][:, :, e * P : (e + tiles) * P]
             if engine == "scalar":
                 cast(
                     engine,
@@ -214,10 +216,14 @@ def tile_attend_gat_v_kernel(tc, qT, kT, rw, dom, offs, out):
         def dense_tile(name, width):
             return keep.tile([P, width], F32, name=name)[:]
 
-        for j in range(PACK - 1):
-            gather(j, 0, N)
-        gather(PACK - 1, 0, HALF)
-        gather(PACK - 1, HALF, N)
+        k_side = keep.tile([P, 2, N - KEY_SHARE], BF16, name="k_side")
+        for j in range(PACK):
+            gather(j, 0, N if j < 2 else KEY_SHARE)
+            if j >= 2:
+                nc.scalar.activation(
+                    out=k_side[:, j - 2, :], in_=k_planes[j][:].indirect(entries(KEY_SHARE, N)), func=COPY
+                )
+        nc.scalar.activation(out=k_bf[:, KEY_SHARE:, 2:], in_=k_side[:].rearrange("p j n -> p n j"), func=COPY)
         quant_k(0, HALF)
         quant_k(HALF, N)
 
@@ -241,7 +247,7 @@ def tile_attend_gat_v_kernel(tc, qT, kT, rw, dom, offs, out):
             quantise(w_codes[LATE][:, lo:hi], w_scales[LATE][:, lo:hi], w_late[:, lo * PACK : hi * PACK])
 
         first_pair = cells(0, PACK).rearrange("p (e x c j) -> p x e c j", e=2, x=2, j=PACK)[:, 1]
-        cast("gpsimd", first_pair, d_raw[0][0][:].rearrange("p j (e c) -> p e c j", e=2))
+        cast("gpsimd", first_pair, d_raw[0][:, :, : 2 * P].rearrange("p j (e c) -> p e c j", e=2))
         cast_d("gpsimd", 0, 1, cells(2))
         weights(w_early, 0, 0, first_t=0)
         weights(w_early, 0, 1)
@@ -257,8 +263,7 @@ def tile_attend_gat_v_kernel(tc, qT, kT, rw, dom, offs, out):
             cols = slice(g * HALF, (g + 1) * HALF)
             quantise(w_codes[EARLY][:, cols], w_scales[EARLY][:, cols], w_early[:, g * 2 * PASS : (g + 1) * 2 * PASS])
         d_next = chained([P, 2 * PASS], BF16, "d_next")
-        cast_d("gpsimd", 1, 1, d_next[:, :PASS])
-        cast_d("gpsimd", 2, 1, d_next[:, PASS:])
+        cast_d("gpsimd", 1, 1, d_next[:], tiles=2)
         weights(w_late, 1, 2)
         weights(w_late, 1, 3, pool=after_bank)
         w_scales.append(after_bank.tile([P, G * HALF], U8, name="w_scales_late", tag="gated", align_bytes=64))

@@ -266,7 +266,9 @@ def tile_attend_gat_v_kernel(tc, qT, kT, rw, dom, offs, out):
         cast_d("gpsimd", 1, 1, d_next[:], tiles=2)
         weights(w_late, 1, 2)
         weights(w_late, 1, 3, pool=after_bank)
-        w_scales.append(after_bank.tile([P, G * HALF], U8, name="w_scales_late", tag="gated", align_bytes=64))
+        bank_scales = after_bank.tile([P, G * HALF + P], U8, name="bank_scales", tag="gated", align_bytes=64)
+        w_scales.append(bank_scales[:, : G * HALF])
+        d_scales.update({(1, 1): bank_scales[:, G * HALF :]})
         weights(w_late, 0, 3)
         d_bf20 = keep.tile([P, PASS], BF16, name="d_bf20", align_bytes=64)
         cast_d("scalar", 2, 0, d_bf20[:])
@@ -279,8 +281,8 @@ def tile_attend_gat_v_kernel(tc, qT, kT, rw, dom, offs, out):
         quant_late(0, CH)
         quant_late(CH, HALF)
         first_late = [product(0, LATE, (1, 0), lo, lo + CH) for lo in (0, CH)]
-        late_scales = after_late.tile([P, 5 * P], U8, name="late_scales", align_bytes=64, offset=0)
-        for i, block in enumerate(((1, 1), (2, 0), (2, 1), (3, 0), (3, 1))):
+        late_scales = after_late.tile([P, 4 * P], U8, name="late_scales", align_bytes=64, offset=0)
+        for i, block in enumerate(((2, 0), (2, 1), (3, 0), (3, 1))):
             d_scales.update({block: late_scales[:, i * P : (i + 1) * P]})
         quant_d(1, d_next[:, :PASS], 1, 1)
         quant_d(2, d_bf20[:], 0, 1)

@@ -29,6 +29,7 @@ EARLY, LATE = 0, 1
 LOW_PLACES, HIGH_PLACES = slice(0, 2), slice(2, PACK)
 
 Q_LOADS = ((0, 512), (512, 768), (768, 1024))
+D_LOADS = ((0, 0, 1), (1, 0, 2), (0, 1, 4), (1, 2, 4))
 FIRST_SHARE = 352
 SECOND_SHARE = 96
 GATED_ROW = CH + 1
@@ -53,6 +54,7 @@ def tile_attend_gat_v_kernel(tc, qT, kT, rw, dom, offs, out):
         after_late = ctx.enter_context(tc.tile_pool(name="after_late", bufs=1))
         after_bank = ctx.enter_context(tc.tile_pool(name="after_bank", bufs=1))
         after_early = ctx.enter_context(tc.tile_pool(name="after_early", bufs=1))
+        first_dom = ctx.enter_context(tc.tile_pool(name="first_dom", bufs=1))
         psum = ctx.enter_context(tc.psum_pool(name="psum", bufs=8))
 
         def chained(shape, dtype, name):
@@ -67,7 +69,10 @@ def tile_attend_gat_v_kernel(tc, qT, kT, rw, dom, offs, out):
         gate_raw = keep.tile([P, G, 2 * PACK], F32, name="gate_raw")
         gate = keep.tile([P, G, PACK], F32, name="gate")
         d_rows = dom[0].rearrange("(g p j) e -> g p j e", p=P, j=PACK)
-        d_raw = [keep.tile([P, PACK, DV], F32, name="d_raw%d" % g) for g in range(G)]
+        d_raw = [
+            (first_dom if i == 0 else keep).tile([P, PACK, (hi - lo) * P], F32, name="d_raw%d" % i, align_bytes=64)
+            for i, (_, lo, hi) in enumerate(D_LOADS)
+        ]
         windows = [keep.tile([P, T], F32, name="window%d" % e) for e in range(VALUE_TILES)]
 
         nc.sync.dma_start(out=k_planes[0][:], in_=k_rows[:, 0, :])
@@ -77,10 +82,8 @@ def tile_attend_gat_v_kernel(tc, qT, kT, rw, dom, offs, out):
         nc.scalar.dma_start(out=gate_raw[:, :, :PACK], in_=rw[0].rearrange("(g p t) o -> p g (t o)", p=P, t=PACK))
         for raw, (lo, hi) in zip(q_raw, Q_LOADS):
             nc.sync.dma_start(out=raw[:], in_=q_rows[:, :, lo:hi])
-        for pair in range(2):
-            for g in range(G):
-                cols = slice(pair * 2 * P, (pair + 1) * 2 * P)
-                nc.sync.dma_start(out=d_raw[g][:, :, cols], in_=d_rows[g, :, :, cols])
+        for raw, (g, lo, hi) in zip(d_raw, D_LOADS):
+            nc.sync.dma_start(out=raw[:], in_=d_rows[g, :, :, lo * P : hi * P])
 
         for window in windows:
             nc.gpsimd.memset(window[:], 0.0)
@@ -102,8 +105,7 @@ def tile_attend_gat_v_kernel(tc, qT, kT, rw, dom, offs, out):
         w_codes = [keep.tile([P, G * HALF], U32, name="w_codes%d" % h, align_bytes=64) for h in range(2)]
         w_scales = []
         d_codes = [keep.tile([P, G * P], U32, name="d_codes%d" % e, align_bytes=64) for e in range(VALUE_TILES)]
-        d_scales0 = keep.tile([P, G * P], U8, name="d_scales0", align_bytes=64)
-        d_scales = {(0, g): d_scales0[:, g * P :] for g in range(G)}
+        d_scales = {}
 
         def entries(lo, hi):
             return offsets[:, lo // PER_COLUMN : hi // PER_COLUMN]
@@ -134,7 +136,8 @@ def tile_attend_gat_v_kernel(tc, qT, kT, rw, dom, offs, out):
             quantise(d_codes[e][:, cols], d_scales[e, first][:, : groups * P], src, E5)
 
         def cast_d(engine, e, g, dst, tiles=1):
-            src = d_raw[g][:, :, e * P : (e + tiles) * P]
+            raw, lo = [(raw, a) for raw, (group, a, b) in zip(d_raw, D_LOADS) if group == g and a <= e < b][0]
+            src = raw[:, :, (e - lo) * P : (e - lo + tiles) * P]
             if engine == "scalar":
                 cast(
                     engine,
@@ -246,36 +249,38 @@ def tile_attend_gat_v_kernel(tc, qT, kT, rw, dom, offs, out):
         def quant_late(lo, hi):
             quantise(w_codes[LATE][:, lo:hi], w_scales[LATE][:, lo:hi], w_late[:, lo * PACK : hi * PACK])
 
-        first_pair = cells(0, PACK).rearrange("p (e x c j) -> p x e c j", e=2, x=2, j=PACK)[:, 1]
-        cast("gpsimd", first_pair, d_raw[0][:, :, : 2 * P].rearrange("p j (e c) -> p e c j", e=2))
-        cast_d("gpsimd", 0, 1, cells(2))
+        cast_d("gpsimd", 0, 0, cells(3))
+        d_pair = first_dom.tile([P, 2 * PASS], BF16, name="d_pair", tag="d_raw0", align_bytes=64)
+        cast_d("gpsimd", 0, 1, d_pair[:], tiles=2)
         weights(w_early, 0, 0, first_t=0)
         weights(w_early, 0, 1)
         weights(w_late, 0, 2)
         weights(w_early, 1, 0, first_t=0)
         weights(w_early, 1, 1, pool=after_early)
-        early_scales = after_early.tile([P, G * HALF + P], U8, name="early_scales", tag="gated", align_bytes=64)
+        early_scales = after_early.tile([P, G * HALF + 3 * P], U8, name="early_scales", tag="gated", align_bytes=64)
         w_scales.append(early_scales[:, : G * HALF])
-        d_scales.update({(1, 0): early_scales[:, G * HALF :]})
-        quant_d(0, cells(1, 2))
-        quant_d(1, cells(3), 0, 1)
+        d_scales.update({(1, 1): early_scales[:, G * HALF :]})
+        d_scales.update({(0, g): early_scales[:, G * HALF + (1 + g) * P :] for g in range(G)})
+        quant_d(0, cells(3), 0, 1)
+        quant_d(0, d_pair[:, :PASS], 1, 1)
+        quant_d(1, d_pair[:, PASS:], 1, 1)
         for g in range(G):
             cols = slice(g * HALF, (g + 1) * HALF)
             quantise(w_codes[EARLY][:, cols], w_scales[EARLY][:, cols], w_early[:, g * 2 * PASS : (g + 1) * 2 * PASS])
         d_next = chained([P, 2 * PASS], BF16, "d_next")
-        cast_d("gpsimd", 1, 1, d_next[:], tiles=2)
+        cast_d("gpsimd", 1, 0, d_next[:], tiles=2)
         weights(w_late, 1, 2)
         weights(w_late, 1, 3, pool=after_bank)
         bank_scales = after_bank.tile([P, G * HALF + P], U8, name="bank_scales", tag="gated", align_bytes=64)
         w_scales.append(bank_scales[:, : G * HALF])
-        d_scales.update({(1, 1): bank_scales[:, G * HALF :]})
+        d_scales.update({(1, 0): bank_scales[:, G * HALF :]})
         weights(w_late, 0, 3)
-        d_bf20 = keep.tile([P, PASS], BF16, name="d_bf20", align_bytes=64)
-        cast_d("scalar", 2, 0, d_bf20[:])
-        dense = to_sbuf("scalar", product(0, EARLY), dense_tile("dense0e", HALF))
-        second_early = product(1, EARLY, (0,), last=1)
         d_bf3 = [keep.tile([P, PASS], BF16, name="d_bf30", align_bytes=64)]
         cast_d("scalar", 3, 0, d_bf3[0][:])
+        dense = to_sbuf("scalar", product(0, EARLY), dense_tile("dense0e", HALF))
+        second_early = product(1, EARLY, (1,), last=0)
+        d_bf21 = keep.tile([P, PASS], BF16, name="d_bf21", align_bytes=64)
+        cast_d("scalar", 2, 1, d_bf21[:])
         scatter("scalar", 0, dense, 0, HALF)
         quant_late(HALF, 2 * HALF)
         quant_late(0, CH)
@@ -284,9 +289,9 @@ def tile_attend_gat_v_kernel(tc, qT, kT, rw, dom, offs, out):
         late_scales = after_late.tile([P, 4 * P], U8, name="late_scales", align_bytes=64, offset=0)
         for i, block in enumerate(((2, 0), (2, 1), (3, 0), (3, 1))):
             d_scales.update({block: late_scales[:, i * P : (i + 1) * P]})
-        quant_d(1, d_next[:, :PASS], 1, 1)
-        quant_d(2, d_bf20[:], 0, 1)
-        quant_d(2, d_next[:, PASS:], 1, 1)
+        quant_d(1, d_next[:, :PASS], 0, 1)
+        quant_d(2, d_next[:, PASS:], 0, 1)
+        quant_d(2, d_bf21[:], 1, 1)
         dense = dense_tile("dense0l", HALF)
         for i, acc in enumerate(first_late):
             to_sbuf("vector", acc, dense[:, i * CH : (i + 1) * CH])
@@ -295,7 +300,7 @@ def tile_attend_gat_v_kernel(tc, qT, kT, rw, dom, offs, out):
 
         scatter("vector", 0, dense, HALF, N)
         store(0)
-        second = [product(1, EARLY, (1,), acc=second_early, first=0), product(1, LATE)]
+        second = [product(1, EARLY, (0,), acc=second_early, first=1), product(1, LATE)]
         for h in (EARLY, LATE):
             dense = to_sbuf(("scalar", "vector")[h], second[h], dense_tile("dense1%d" % h, HALF))
             scatter("scalar", 1, dense, h * HALF, (h + 1) * HALF)

@@ -54,7 +54,6 @@ def tile_attend_gat_v_kernel(tc, qT, kT, rw, dom, offs, out):
         after_late = ctx.enter_context(tc.tile_pool(name="after_late", bufs=1))
         after_bank = ctx.enter_context(tc.tile_pool(name="after_bank", bufs=1))
         after_early = ctx.enter_context(tc.tile_pool(name="after_early", bufs=1))
-        first_dom = ctx.enter_context(tc.tile_pool(name="first_dom", bufs=1))
         psum = ctx.enter_context(tc.psum_pool(name="psum", bufs=8))
 
         def chained(shape, dtype, name):
@@ -70,7 +69,7 @@ def tile_attend_gat_v_kernel(tc, qT, kT, rw, dom, offs, out):
         gate = keep.tile([P, G, PACK], F32, name="gate")
         d_rows = dom[0].rearrange("(g p j) e -> g p j e", p=P, j=PACK)
         d_raw = [
-            (first_dom if i == 0 else keep).tile([P, PACK, (hi - lo) * P], F32, name="d_raw%d" % i, align_bytes=64)
+            keep.tile([P, PACK, (hi - lo) * P], F32, name="d_raw%d" % i)
             for i, (_, lo, hi) in enumerate(D_LOADS)
         ]
         windows = [keep.tile([P, T], F32, name="window%d" % e) for e in range(VALUE_TILES)]
@@ -94,7 +93,7 @@ def tile_attend_gat_v_kernel(tc, qT, kT, rw, dom, offs, out):
         k_codes = keep.tile([P, N], U32, name="k_codes", align_bytes=64)
         k_scales = keep.tile([P, N], U8, name="k_scales", align_bytes=64)
         q_bf0 = keep.tile([P, PACK * PASS], BF16, name="q_bf0", align_bytes=64)
-        arena = keep.tile([P, 4 * PASS], BF16, name="arena", align_bytes=64)
+        arena = keep.tile([P, 5 * PASS], BF16, name="arena", align_bytes=64)
 
         def cells(first, count=1):
             return arena[:, first * PASS : (first + count) * PASS]
@@ -105,7 +104,8 @@ def tile_attend_gat_v_kernel(tc, qT, kT, rw, dom, offs, out):
         w_codes = [keep.tile([P, G * HALF], U32, name="w_codes%d" % h, align_bytes=64) for h in range(2)]
         w_scales = []
         d_codes = [keep.tile([P, G * P], U32, name="d_codes%d" % e, align_bytes=64) for e in range(VALUE_TILES)]
-        d_scales = {}
+        d_scales0 = keep.tile([P, G * P], U8, name="d_scales0", align_bytes=64)
+        d_scales = {(0, g): d_scales0[:, g * P :] for g in range(G)}
 
         def entries(lo, hi):
             return offsets[:, lo // PER_COLUMN : hi // PER_COLUMN]
@@ -167,7 +167,7 @@ def tile_attend_gat_v_kernel(tc, qT, kT, rw, dom, offs, out):
             gated = pool.tile([P, PACK, GATED_ROW], F32, name="gated", tag="gated", align_bytes=64)
             for t in range(PACK):
                 nc.scalar.activation(out=gated[:, t, :CH], in_=bank[:, t, :], func=COPY, scale=gate[:, g, t : t + 1])
-            first = (g * 2 + c % 2) * PASS
+            first = (c % 2) * PASS
             nc.vector.scalar_tensor_tensor(
                 out=dst[:, first : first + PASS].rearrange("p (n t) -> p n t", t=PACK),
                 in0=bank[:].rearrange("p t n -> p n t"),
@@ -244,33 +244,32 @@ def tile_attend_gat_v_kernel(tc, qT, kT, rw, dom, offs, out):
         quant_q(1, P // 2, P)
 
         w_early = chained([P, G * 2 * PASS], BF16, "w_early")
-        w_late = after_late.tile([P, G * 2 * PASS], BF16, name="w_late", align_bytes=64, offset=0)
+        w_late = after_late.tile([P, 2 * PASS], BF16, name="w_late", align_bytes=64, offset=0)
 
         def quant_late(lo, hi):
-            quantise(w_codes[LATE][:, lo:hi], w_scales[LATE][:, lo:hi], w_late[:, lo * PACK : hi * PACK])
+            src = w_late[:, lo * PACK : hi * PACK] if lo < HALF else cells(3, 2)
+            quantise(w_codes[LATE][:, lo:hi], w_scales[LATE][:, lo:hi], src)
 
-        cast_d("gpsimd", 0, 0, cells(3))
-        d_pair = first_dom.tile([P, 2 * PASS], BF16, name="d_pair", tag="d_raw0", align_bytes=64)
-        cast_d("gpsimd", 0, 1, d_pair[:], tiles=2)
+        cast_d("gpsimd", 0, 0, cells(2))
+        d_pair = cells(3, 2)
+        cast_d("gpsimd", 0, 1, d_pair, tiles=2)
         weights(w_early, 0, 0, first_t=0)
         weights(w_early, 0, 1)
         weights(w_late, 0, 2)
-        weights(w_early, 1, 0, first_t=0)
-        weights(w_early, 1, 1, pool=after_early)
-        early_scales = after_early.tile([P, G * HALF + 3 * P], U8, name="early_scales", tag="gated", align_bytes=64)
+        weights(w_early[:, 2 * PASS :], 1, 0, first_t=0)
+        weights(w_early[:, 2 * PASS :], 1, 1, pool=after_early)
+        early_scales = after_early.tile([P, G * HALF + P], U8, name="early_scales", tag="gated", align_bytes=64)
         w_scales.append(early_scales[:, : G * HALF])
         d_scales.update({(1, 1): early_scales[:, G * HALF :]})
-        d_scales.update({(0, g): early_scales[:, G * HALF + (1 + g) * P :] for g in range(G)})
-        quant_d(0, cells(3), 0, 1)
-        quant_d(0, d_pair[:, :PASS], 1, 1)
+        quant_d(0, cells(2, 2))
         quant_d(1, d_pair[:, PASS:], 1, 1)
         for g in range(G):
             cols = slice(g * HALF, (g + 1) * HALF)
             quantise(w_codes[EARLY][:, cols], w_scales[EARLY][:, cols], w_early[:, g * 2 * PASS : (g + 1) * 2 * PASS])
         d_next = chained([P, 2 * PASS], BF16, "d_next")
         cast_d("gpsimd", 1, 0, d_next[:], tiles=2)
-        weights(w_late, 1, 2)
-        weights(w_late, 1, 3, pool=after_bank)
+        weights(d_pair, 1, 2)
+        weights(d_pair, 1, 3, pool=after_bank)
         bank_scales = after_bank.tile([P, G * HALF + P], U8, name="bank_scales", tag="gated", align_bytes=64)
         w_scales.append(bank_scales[:, : G * HALF])
         d_scales.update({(1, 0): bank_scales[:, G * HALF :]})

@@ -28,7 +28,7 @@ PER_COLUMN = 16
 EARLY, LATE = 0, 1
 LOW_PLACES, HIGH_PLACES = slice(0, 2), slice(2, PACK)
 
-Q_LOADS = ((0, 512), (512, 768), (768, 1024))
+Q_LOADS = ((0, 512), (512, 832), (832, 1024))
 D_LOADS = ((0, 0, 1), (1, 0, 2), (0, 1, 4), (1, 2, 4))
 FIRST_SHARE = 352
 SECOND_SHARE = 96

@@ -32,7 +32,8 @@ Q_LOADS = ((0, 512), (512, 832), (832, 1024))
 D_LOADS = ((0, 0, 1), (1, 0, 2), (0, 1, 4), (1, 2, 4))
 FIRST_SHARE = 352
 SECOND_SHARE = 96
-GATED_ROW = CH + 1
+GATED_ROW = CH + 17
+ROW_PAD = 16
 KEY_SHARE = 320
 
 
@@ -63,13 +64,13 @@ def tile_attend_gat_v_kernel(tc, qT, kT, rw, dom, offs, out):
         k_planes = [keep.tile([P, T], F32, name="k_plane%d" % j) for j in range(PACK)]
         k_rows = kT.rearrange("(p j) c -> p j c", j=PACK)
         q_rows = qT[0].rearrange("(p j) r -> p j r", j=PACK)
-        q_raw = [keep.tile([P, PACK, hi - lo], F32, name="q_raw%d" % lo) for lo, hi in Q_LOADS[:-1]]
-        q_raw.append(chained([P, PACK, R - Q_LOADS[-1][0]], F32, "q_last"))
+        q_raw = [keep.tile([P, PACK, hi - lo + ROW_PAD], F32, name="q_raw%d" % lo) for lo, hi in Q_LOADS[:-1]]
+        q_raw.append(chained([P, PACK, R - Q_LOADS[-1][0] + ROW_PAD], F32, "q_last"))
         gate_raw = keep.tile([P, G, 2 * PACK], F32, name="gate_raw")
         gate = keep.tile([P, G, PACK], F32, name="gate")
         d_rows = dom[0].rearrange("(g p j) e -> g p j e", p=P, j=PACK)
         d_raw = [
-            keep.tile([P, PACK, (hi - lo) * P], F32, name="d_raw%d" % i)
+            keep.tile([P, PACK, (hi - lo) * P + ROW_PAD], F32, name="d_raw%d" % i)
             for i, (_, lo, hi) in enumerate(D_LOADS)
         ]
         windows = [keep.tile([P, T], F32, name="window%d" % e) for e in range(VALUE_TILES)]
@@ -80,9 +81,9 @@ def tile_attend_gat_v_kernel(tc, qT, kT, rw, dom, offs, out):
             nc.sync.dma_start(out=k_planes[j][:], in_=k_rows[:, j, :])
         nc.scalar.dma_start(out=gate_raw[:, :, :PACK], in_=rw[0].rearrange("(g p t) o -> p g (t o)", p=P, t=PACK))
         for raw, (lo, hi) in zip(q_raw, Q_LOADS):
-            nc.sync.dma_start(out=raw[:], in_=q_rows[:, :, lo:hi])
+            nc.sync.dma_start(out=raw[:, :, : hi - lo], in_=q_rows[:, :, lo:hi])
         for raw, (g, lo, hi) in zip(d_raw, D_LOADS):
-            nc.sync.dma_start(out=raw[:], in_=d_rows[g, :, :, lo * P : hi * P])
+            nc.sync.dma_start(out=raw[:, :, : (hi - lo) * P], in_=d_rows[g, :, :, lo * P : hi * P])
 
         for window in windows:
             nc.gpsimd.memset(window[:], 0.0)

from contextlib import ExitStack

import concourse.mybir as mybir

N, T, D, DV, R = 512, 2048, 512, 512, 1024
FLOPS = 2 * R * N * D + 2 * R * N * DV

F32 = mybir.dt.float32
BF16 = mybir.dt.bfloat16
U32 = mybir.dt.uint32
U16 = mybir.dt.uint16
U8 = mybir.dt.uint8
E4 = mybir.dt.float8_e4m3fn_x4
E5 = mybir.dt.float8_e5m2_x4
COPY = mybir.ActivationFunctionType.Copy
MULT = mybir.AluOpType.mult
ADD = mybir.AluOpType.add
MAX = mybir.AluOpType.max

P = 128
PACK = 4
PASS = P * PACK
G = R // PASS
VALUE_TILES = DV // P
CH = 128
HALF = N // 2
PER_COLUMN = 16
EARLY, LATE = 0, 1
LOW_PLACES, HIGH_PLACES = slice(0, 2), slice(2, PACK)

Q_LOADS = ((0, 512), (512, 832), (832, 1024))
D_LOADS = ((0, 0, 1), (1, 0, 2), (0, 1, 4), (1, 2, 4))
FIRST_SHARE = 352
SECOND_SHARE = 96
GATED_ROW = CH + 17
ROW_PAD = 16
KEY_SHARE = 320


def tile_attend_gat_v_kernel(tc, qT, kT, rw, dom, offs, out):
    nc = tc.nc

    def cast(engine, dst, src):
        if engine == "scalar":
            nc.scalar.activation(out=dst, in_=src, func=COPY)
        elif engine == "vector":
            nc.vector.tensor_copy(out=dst, in_=src)
        else:
            nc.gpsimd.tensor_scalar(out=dst, in0=src, scalar1=1.0, scalar2=0.0, op0=MULT, op1=ADD)

    with ExitStack() as ctx:
        keep = ctx.enter_context(tc.tile_pool(name="keep", bufs=1))
        gated_pool = ctx.enter_context(tc.tile_pool(name="gated_pool", bufs=4))
        chain = ctx.enter_context(tc.tile_pool(name="chain", bufs=1))
        after_late = ctx.enter_context(tc.tile_pool(name="after_late", bufs=1))
        after_bank = ctx.enter_context(tc.tile_pool(name="after_bank", bufs=1))
        after_early = ctx.enter_context(tc.tile_pool(name="after_early", bufs=1))
        psum = ctx.enter_context(tc.psum_pool(name="psum", bufs=8))

        def chained(shape, dtype, name):
            return chain.tile(shape, dtype, name=name, tag="chain", align_bytes=64)

        offsets = keep.tile([P, N // PER_COLUMN], U16, name="offsets")
        k_planes = [keep.tile([P, T], F32, name="k_plane%d" % j) for j in range(PACK)]
        k_rows = kT.rearrange("(p j) c -> p j c", j=PACK)
        q_rows = qT[0].rearrange("(p j) r -> p j r", j=PACK)
        q_raw = [keep.tile([P, PACK, hi - lo + ROW_PAD], F32, name="q_raw%d" % lo) for lo, hi in Q_LOADS[:-1]]
        q_raw.append(chained([P, PACK, R - Q_LOADS[-1][0] + ROW_PAD], F32, "q_last"))
        gate_raw = keep.tile([P, G, 2 * PACK], F32, name="gate_raw")
        gate = keep.tile([P, G, PACK], F32, name="gate")
        d_rows = dom[0].rearrange("(g p j) e -> g p j e", p=P, j=PACK)
        d_raw = [
            keep.tile([P, PACK, (hi - lo) * P + ROW_PAD], F32, name="d_raw%d" % i)
            for i, (_, lo, hi) in enumerate(D_LOADS)
        ]
        windows = [keep.tile([P, T], F32, name="window%d" % e) for e in range(VALUE_TILES)]

        nc.sync.dma_start(out=k_planes[0][:], in_=k_rows[:, 0, :])
        nc.sync.dma_start(offsets[:], offs)
        for j in range(1, PACK):
            nc.sync.dma_start(out=k_planes[j][:], in_=k_rows[:, j, :])
        nc.scalar.dma_start(out=gate_raw[:, :, :PACK], in_=rw[0].rearrange("(g p t) o -> p g (t o)", p=P, t=PACK))
        for raw, (lo, hi) in zip(q_raw, Q_LOADS):
            nc.sync.dma_start(out=raw[:, :, : hi - lo], in_=q_rows[:, :, lo:hi])
        for raw, (g, lo, hi) in zip(d_raw, D_LOADS):
            nc.sync.dma_start(out=raw[:, :, : (hi - lo) * P], in_=d_rows[g, :, :, lo * P : hi * P])

        for window in windows:
            nc.gpsimd.memset(window[:], 0.0)

        nc.scalar.activation(out=gate[:], in_=gate_raw[:, :, :PACK], func=COPY)

        k_bf = keep.tile([P, N, PACK], BF16, name="k_bf", align_bytes=64)
        k_codes = keep.tile([P, N], U32, name="k_codes", align_bytes=64)
        k_scales = keep.tile([P, N], U8, name="k_scales", align_bytes=64)
        q_bf0 = keep.tile([P, PACK * PASS], BF16, name="q_bf0", align_bytes=64)
        arena = keep.tile([P, 5 * PASS], BF16, name="arena", align_bytes=64)

        def cells(first, count=1):
            return arena[:, first * PASS : (first + count) * PASS]

        q_bf = [t.rearrange("p (t m j) -> p t m j", t=PACK, j=PACK) for t in (q_bf0[:], cells(0, PACK))]
        q_codes = [keep.tile([P, PASS], U32, name="q_codes%d" % g, align_bytes=64) for g in range(G)]
        q_scales = [keep.tile([P, PASS], U8, name="q_scales%d" % g, align_bytes=64) for g in range(G)]
        w_codes = [keep.tile([P, G * HALF], U32, name="w_codes%d" % h, align_bytes=64) for h in range(2)]
        w_scales = []
        d_codes = [keep.tile([P, G * P], U32, name="d_codes%d" % e, align_bytes=64) for e in range(VALUE_TILES)]
        d_scales0 = keep.tile([P, G * P], U8, name="d_scales0", align_bytes=64)
        d_scales = {(0, g): d_scales0[:, g * P :] for g in range(G)}

        def entries(lo, hi):
            return offsets[:, lo // PER_COLUMN : hi // PER_COLUMN]

        def gather(j, lo, hi):
            nc.vector.tensor_copy(out=k_bf[:, lo:hi, j], in_=k_planes[j][:].indirect(entries(lo, hi)))

        def quantise(codes, scales, src, fmt=E4):
            nc.vector.quantize_mx(out=codes.bitcast(fmt), scales=scales, in_=src)

        def quant_k(lo, hi):
            quantise(k_codes[:, lo:hi], k_scales[:, lo:hi], k_bf[:, lo:hi, :].rearrange("p n j -> p (n j)"))

        def cast_q(lo, hi, engine, places=slice(0, PACK)):
            g = lo // PASS
            raw, first = [(raw, a) for raw, (a, b) in zip(q_raw, Q_LOADS) if a <= lo < b][0]
            ms = slice((lo - g * PASS) // PACK, (hi - g * PASS) // PACK)
            src = raw[:, :, lo - first : hi - first].rearrange("p j (m t) -> p m j t", t=PACK)
            cast(engine, q_bf[g].rearrange("p t m j -> p m j t")[:, ms, :, places], src[:, :, :, places])

        def quant_q(g, lo, hi):
            for t in range(PACK):
                cols = slice(t * P + lo, t * P + hi)
                quantise(q_codes[g][:, cols], q_scales[g][:, cols], q_bf[g][:, t, lo:hi, :].rearrange("p m j -> p (m j)"))

        def quant_d(e, src, first=0, groups=G):
            cols = slice(first * P, (first + groups) * P)
            quantise(d_codes[e][:, cols], d_scales[e, first][:, : groups * P], src, E5)

        def cast_d(engine, e, g, dst, tiles=1):
            raw, lo = [(raw, a) for raw, (group, a, b) in zip(d_raw, D_LOADS) if group == g and a <= e < b][0]
            src = raw[:, :, (e - lo) * P : (e - lo + tiles) * P]
            if engine == "scalar":
                cast(
                    engine,
                    dst.rearrange("p (c i j) -> p c j i", i=PACK, j=PACK),
                    src.rearrange("p j (c i) -> p c j i", i=PACK),
                )
            else:
                cast(engine, dst.rearrange("p (e j) -> p e j", j=PACK), src.rearrange("p j e -> p e j"))

        def scores(g, c, first_t=PACK - 1):
            cols = slice(c * CH, (c + 1) * CH)
            bank = psum.tile([P, PACK, CH], F32, name="scores", tag="bank")
            for t in [(first_t + i) % PACK for i in range(PACK)]:
                nc.tensor.matmul_mx(
                    out=bank[:, t, :],
                    lhsT=q_codes[g][:, t * P : (t + 1) * P].bitcast(E4),
                    lhsT_scale=q_scales[g][:, t * P : (t + 1) * P],
                    rhs=k_codes[:, cols].bitcast(E4),
                    rhs_scale=k_scales[:, cols],
                    start=True,
                    stop=True,
                )
            return bank

        def weights(dst, g, c, first_t=PACK - 1, pool=gated_pool):
            bank = scores(g, c, first_t)
            gated = pool.tile([P, PACK, GATED_ROW], F32, name="gated", tag="gated", align_bytes=64)
            for t in range(PACK):
                nc.scalar.activation(out=gated[:, t, :CH], in_=bank[:, t, :], func=COPY, scale=gate[:, g, t : t + 1])
            first = (c % 2) * PASS
            nc.vector.scalar_tensor_tensor(
                out=dst[:, first : first + PASS].rearrange("p (n t) -> p n t", t=PACK),
                in0=bank[:].rearrange("p t n -> p n t"),
                scalar=0.0,
                in1=gated[:, :, :CH].rearrange("p t n -> p n t"),
                op0=MAX,
                op1=MULT,
            )

        def product(e, h, groups=(0, 1), lo=0, hi=HALF, acc=None, first=None, last=None):
            if acc is None:
                acc = psum.tile([P, hi - lo], F32, name="acc", tag="bank")[:]
            for g in groups:
                cols = slice(g * HALF + lo, g * HALF + hi)
                nc.tensor.matmul_mx(
                    out=acc,
                    lhsT=d_codes[e][:, g * P : (g + 1) * P].bitcast(E5),
                    lhsT_scale=d_scales[e, g][:, :P],
                    rhs=w_codes[h][:, cols].bitcast(E4),
                    rhs_scale=w_scales[h][:, cols],
                    start=(g == (groups[0] if first is None else first)),
                    stop=(g == (groups[-1] if last is None else last)),
                )
            return acc

        def whole_product(e):
            acc = psum.tile([P, N], F32, name="acc", tag="bank")
            for h in (EARLY, LATE):
                product(e, h, acc=acc[:, h * HALF : (h + 1) * HALF])
            return acc[:]

        def to_sbuf(engine, acc, dense):
            if engine == "scalar":
                nc.scalar.activation(out=dense, in_=acc, func=COPY)
            else:
                nc.vector.tensor_copy(out=dense, in_=acc)
            return dense

        def scatter(engine, e, src, lo, hi):
            target = windows[e][:].indirect(entries(lo, hi))
            if engine == "scalar":
                nc.scalar.activation(out=target, in_=src, func=COPY)
            else:
                nc.vector.tensor_copy(out=target, in_=src)

        def store(e, queue=nc.sync):
            queue.dma_start(out=out[e * P : (e + 1) * P, :], in_=windows[e][:])

        def dense_tile(name, width):
            return keep.tile([P, width], F32, name=name)[:]

        k_side = keep.tile([P, 2, N - KEY_SHARE], BF16, name="k_side")
        for j in range(PACK):
            gather(j, 0, N if j < 2 else KEY_SHARE)
            if j >= 2:
                nc.scalar.activation(
                    out=k_side[:, j - 2, :], in_=k_planes[j][:].indirect(entries(KEY_SHARE, N)), func=COPY
                )
        nc.scalar.activation(out=k_bf[:, KEY_SHARE:, 2:], in_=k_side[:].rearrange("p j n -> p n j"), func=COPY)
        quant_k(0, HALF)
        quant_k(HALF, N)

        (_, second), (_, third), _ = Q_LOADS
        cast_q(0, second, "vector", LOW_PLACES)
        cast_q(0, FIRST_SHARE, "scalar", HIGH_PLACES)
        cast_q(FIRST_SHARE, second, "vector", HIGH_PLACES)
        quant_q(0, 0, P)
        cast_q(second, second + SECOND_SHARE, "scalar")
        cast_q(second + SECOND_SHARE, third, "vector", LOW_PLACES)
        cast_q(second + SECOND_SHARE, third, "vector", HIGH_PLACES)
        quant_q(1, 0, P // 2)
        cast_q(third, R, "vector", LOW_PLACES)
        cast_q(third, R, "vector", HIGH_PLACES)
        quant_q(1, P // 2, P)

        w_early = chained([P, G * 2 * PASS], BF16, "w_early")
        w_late = after_late.tile([P, 2 * PASS], BF16, name="w_late", align_bytes=64, offset=0)

        def quant_late(lo, hi):
            src = w_late[:, lo * PACK : hi * PACK] if lo < HALF else cells(3, 2)
            quantise(w_codes[LATE][:, lo:hi], w_scales[LATE][:, lo:hi], src)

        cast_d("gpsimd", 0, 0, cells(2))
        d_pair = cells(3, 2)
        cast_d("gpsimd", 0, 1, d_pair, tiles=2)
        weights(w_early, 0, 0, first_t=0)
        weights(w_early, 0, 1)
        weights(w_late, 0, 2)
        weights(w_early[:, 2 * PASS :], 1, 0, first_t=0)
        weights(w_early[:, 2 * PASS :], 1, 1, pool=after_early)
        early_scales = after_early.tile([P, G * HALF + P], U8, name="early_scales", tag="gated", align_bytes=64)
        w_scales.append(early_scales[:, : G * HALF])
        d_scales.update({(1, 1): early_scales[:, G * HALF :]})
        quant_d(0, cells(2, 2))
        quant_d(1, d_pair[:, PASS:], 1, 1)
        for g in range(G):
            cols = slice(g * HALF, (g + 1) * HALF)
            quantise(w_codes[EARLY][:, cols], w_scales[EARLY][:, cols], w_early[:, g * 2 * PASS : (g + 1) * 2 * PASS])
        d_next = chained([P, 2 * PASS], BF16, "d_next")
        cast_d("gpsimd", 1, 0, d_next[:], tiles=2)
        weights(d_pair, 1, 2)
        weights(d_pair, 1, 3, pool=after_bank)
        bank_scales = after_bank.tile([P, G * HALF + P], U8, name="bank_scales", tag="gated", align_bytes=64)
        w_scales.append(bank_scales[:, : G * HALF])
        d_scales.update({(1, 0): bank_scales[:, G * HALF :]})
        weights(w_late, 0, 3)
        d_bf3 = [keep.tile([P, PASS], BF16, name="d_bf30", align_bytes=64)]
        cast_d("scalar", 3, 0, d_bf3[0][:])
        dense = to_sbuf("scalar", product(0, EARLY), dense_tile("dense0e", HALF))
        second_early = product(1, EARLY, (1,), last=0)
        d_bf21 = keep.tile([P, PASS], BF16, name="d_bf21", align_bytes=64)
        cast_d("scalar", 2, 1, d_bf21[:])
        scatter("scalar", 0, dense, 0, HALF)
        quant_late(HALF, 2 * HALF)
        quant_late(0, CH)
        quant_late(CH, HALF)
        first_late = [product(0, LATE, (1, 0), lo, lo + CH) for lo in (0, CH)]
        late_scales = after_late.tile([P, 4 * P], U8, name="late_scales", align_bytes=64, offset=0)
        for i, block in enumerate(((2, 0), (2, 1), (3, 0), (3, 1))):
            d_scales.update({block: late_scales[:, i * P : (i + 1) * P]})
        quant_d(1, d_next[:, :PASS], 0, 1)
        quant_d(2, d_next[:, PASS:], 0, 1)
        quant_d(2, d_bf21[:], 1, 1)
        dense = dense_tile("dense0l", HALF)
        for i, acc in enumerate(first_late):
            to_sbuf("vector", acc, dense[:, i * CH : (i + 1) * CH])
        d_bf3.append(chained([P, PASS], BF16, "d_bf31"))
        cast_d("vector", 3, 1, d_bf3[1][:])

        scatter("vector", 0, dense, HALF, N)
        store(0)
        second = [product(1, EARLY, (0,), acc=second_early, first=1), product(1, LATE)]
        for h in (EARLY, LATE):
            dense = to_sbuf(("scalar", "vector")[h], second[h], dense_tile("dense1%d" % h, HALF))
            scatter("scalar", 1, dense, h * HALF, (h + 1) * HALF)
        store(1)
        dense2 = to_sbuf("vector", whole_product(2), dense_tile("dense2", N))
        for g in range(G):
            quant_d(3, d_bf3[g][:], g, 1)
        scatter("vector", 2, dense2, 0, N)
        store(2)
        dense3 = [to_sbuf("scalar", product(3, h), dense_tile("dense3%d" % h, HALF)) for h in (EARLY, LATE)]
        for h in (EARLY, LATE):
            scatter("scalar", 3, dense3[h], h * HALF, (h + 1) * HALF)
        store(3, nc.scalar)
